import numpy as np
import ml_dtypes


def mxq(x, axis, fmt="e4m3"):
    dtype, down = {"e4m3": (ml_dtypes.float8_e4m3fn, 7), "e5m2": (ml_dtypes.float8_e5m2, 14)}[fmt]
    v = np.moveaxis(np.asarray(x, np.float32).astype(ml_dtypes.bfloat16).astype(np.float64), axis, -1)
    blocks = v.reshape(v.shape[:-1] + (-1, 32))
    amax = np.abs(blocks).max(-1, keepdims=True)
    byte = np.maximum(np.where(amax > 0, np.frexp(amax)[1] - 1 + 127, 0) - down, 1)
    scale = np.exp2(byte - 127.0)
    codes = (blocks / scale).astype(np.float32).astype(dtype).astype(np.float64)
    return np.moveaxis((codes * scale).reshape(v.shape), -1, axis)


WIDE = False


def mx_kscale(k):
    if not WIDE:
        return np.ones(k)
    levels = np.array([10, -10, 5, -5, 0])
    if k % 512:
        return np.exp2(np.random.permutation(np.resize(levels, k // 32))).repeat(32)
    a = np.empty((k // 512, 16))
    for p in range(k // 512):
        a[p, :8] = np.random.permutation(np.resize(levels, 8))
        for g in range(8):
            far = levels[np.abs(levels - a[p, g]) >= 10]
            a[p, g + 8] = far[np.random.randint(len(far))]
    return np.exp2(a.ravel()).repeat(32)


BF16 = ml_dtypes.bfloat16


def bf(x):
    return np.asarray(x, np.float32).astype(BF16)


def f64(x):
    return np.asarray(x).astype(np.float64)


E2M1 = np.array([0.0, 0.5, 1.0, 1.5, 2.0, 3.0, 4.0, 6.0, -0.0, -0.5, -1.0, -1.5, -2.0, -3.0, -4.0, -6.0])


def pack_weight(w, fmt):
    k, n = w.shape
    w = f64(bf(w)).reshape(k // 32, 32, n)
    amax = np.abs(w).max(1)
    if fmt == "e4m3":
        byte = np.frexp(amax)[1] - 1 + 127 - 7
    else:
        mant, ex = np.frexp(amax / 6.0)
        byte = np.where(mant > 0.5, ex, ex - 1) + 127
    byte = np.clip(np.where(amax > 0, byte, 1), 1, 254)
    scaled = (w * np.exp2(127.0 - byte)[:, None, :]).reshape(k, n).astype(np.float32)
    by_word = np.ascontiguousarray(scaled.reshape(k // 512, 128, 4, n).transpose(0, 1, 3, 2))
    if fmt == "e4m3":
        words = by_word.astype(ml_dtypes.float8_e4m3fn).view(np.uint8)
    else:
        c = by_word.astype(ml_dtypes.float4_e2m1fn).view(np.uint8) & 0xF
        words = c[..., 0::2] | (c[..., 1::2] << 4)
    return np.ascontiguousarray(words), np.ascontiguousarray(byte.astype(np.uint8).reshape(k // 512, 16, n))


def unpack_weight(words, scales, fmt):
    g, p, n, _ = words.shape
    if fmt == "e4m3":
        vals = np.ascontiguousarray(words).view(ml_dtypes.float8_e4m3fn).astype(np.float64)
    else:
        nib = np.empty((g, p, n, 4), np.uint8)
        nib[..., 0::2] = words & 0xF
        nib[..., 1::2] = words >> 4
        vals = E2M1[nib]
    vals = vals * np.repeat(np.exp2(scales.astype(np.float64) - 127.0), 8, axis=1)[..., None]
    return vals.transpose(0, 1, 3, 2).reshape(g * 512, n)
def pack4(w):
    words, scales = pack_weight(w, "e2m1")
    return words.reshape(words.shape[0], 128, -1), scales


def unpack4(words, scales):
    return unpack_weight(words.reshape(words.shape[0], 128, -1, 2), scales, "e2m1")


R, T, D, E = 2048, 4096, 1024, 512


def setup_inputs():
    s, t = mx_kscale(T), mx_kscale(D)
    keys_words, keys_scales = pack4(np.random.standard_normal((T, D)) / np.sqrt(T) * s[:, None] * t)
    values_words, values_scales = pack4(np.random.standard_normal((T, E)) / s[:, None])
    return {"keys_words": keys_words,
            "keys_scales": keys_scales,
            "values_words": values_words,
            "values_scales": values_scales,
            "old": bf(np.random.standard_normal((D, E)) * t[:, None]),
            "retain": bf(np.random.uniform(0.3, 0.95, D)),
            "query": bf(np.random.standard_normal((R, D)) / np.sqrt(D) / t),
            "gate": bf(np.random.uniform(0.2, 1.0, (R, E)))}


def reference(keys_words, keys_scales, values_words, values_scales, old, retain, query, gate):
    keys = unpack4(keys_words, keys_scales)
    values = unpack4(values_words, values_scales)
    write = keys.T @ values
    memory = f64(retain)[:, None] * f64(old) + write
    read = mxq(f64(query), 1, "e4m3") @ mxq(memory, 0, "e4m3")
    return read * f64(gate)

@@ -1,0 +1,418 @@
+from contextlib import ExitStack
+
+import concourse.mybir as mybir
+from concourse.masks import make_identity
+
+R, T, D, E = 2048, 4096, 1024, 512
+FLOPS = 2 * T * D * E + 2 * R * D * E
+
+F32 = mybir.dt.float32
+BF16 = mybir.dt.bfloat16
+I32 = mybir.dt.int32
+U32 = mybir.dt.uint32
+U8 = mybir.dt.uint8
+FP8X4 = mybir.dt.float8_e4m3fn_x4
+FP4X4 = mybir.dt.float4_e2m1fn_x4
+MULT = mybir.AluOpType.mult
+ADD = mybir.AluOpType.add
+COPY = mybir.ActivationFunctionType.Copy
+
+P = 128
+PACK = 4
+K_PASS = P * PACK
+T_PASSES = T // K_PASS
+D_PASSES = D // K_PASS
+E_TILES = E // P
+R_TILES = R // P
+CHUNK = 4
+SCALE_RUNS = [(0, 2), (2, 8)]
+
+
+def tile_memory_write_read_s4_kernel(
+    tc, keys_words, keys_scales, values_words, values_scales, old, retain, query, gate, out
+):
+    nc = tc.nc
+    with ExitStack() as ctx:
+        keep = ctx.enter_context(tc.tile_pool(name="keep", bufs=1))
+        ring = ctx.enter_context(tc.tile_pool(name="ring", bufs=4))
+        psum = ctx.enter_context(tc.psum_pool(name="psum", bufs=1))
+        ctx.enter_context(tc.manual_schedule())
+
+        def bank(b, shape):
+            return psum.tile(shape, F32, name=f"bank{b}", tag=f"bank{b}")
+
+        def kept(name, shape, dtype):
+            return keep.tile(shape, dtype, name=name, tag=name, align_bytes=64)
+
+        ident = kept("ident", [P, P], F32)
+        make_identity(nc, ident[:])
+
+        def scale_plane(name, passes, width):
+            plane = kept(name, [P, passes, width], U8)
+            nc.vector.memset(plane[:].bitcast(I32), 0)
+            return plane
+
+        v_planes, k_planes, v_scale, k_scale = {}, {}, {}, {}
+        for g0, g1 in SCALE_RUNS:
+            v_planes[g0] = scale_plane(f"v_scale{g0}", g1 - g0, E)
+            k_planes[g0] = scale_plane(f"k_scale{g0}", g1 - g0, D)
+            for g in range(g0, g1):
+                v_scale[g] = v_planes[g0][:, g - g0, :]
+                k_scale[g] = k_planes[g0][:, g - g0, :]
+
+        def load_scale_run(n):
+            g0, g1 = SCALE_RUNS[n]
+            load_scales(v_planes[g0], values_scales[g0:g1])
+            load_scales(k_planes[g0], keys_scales[g0:g1])
+
+        def load_scales(plane, rows):
+            by_row = rows.rearrange("g (q r) n -> r q g n", r=4)
+            for r in range(4):
+                nc.sync.dma_start(out=plane[r:P:32, :, :].bitcast(I32), in_=by_row[r].bitcast(I32))
+
+        v_words, k_words = {}, {}
+
+        def load_words(name, into, words, g0, g1):
+            w = kept(f"{name}{g0}", [P, g1 - g0, words.shape[2]], U8)
+            nc.sync.dma_start(out=w[:].bitcast(I32), in_=words[g0:g1].rearrange("g p n -> p g n").bitcast(I32))
+            for g in range(g0, g1):
+                into[name, g] = w[:, g - g0, :]
+
+        def load_first_words(g0, g1):
+            load_words("v", v_words, values_words, g0, g1)
+            load_words("k", k_words, keys_words, g0, g1)
+
+        retain_sb = kept("retain_sb", [P, D_PASSES, PACK], BF16)
+        old_sb = [kept(f"old_sb{h}", [P, PACK, E], BF16) for h in range(D_PASSES)]
+        query_sb = [kept(f"query_sb{c}", [P, CHUNK, D], BF16) for c in range(R_TILES // CHUNK)]
+        gate_sb = [kept(f"gate_sb{c}", [P, CHUNK, E], BF16) for c in range(R_TILES // CHUNK)]
+        old_rows = old.rearrange("(h p t) e -> h p t e", p=P, t=PACK)
+        query_rows = query.rearrange("(c p j) d -> c p j d", p=P, j=CHUNK)
+        gate_rows = gate.rearrange("(c p j) e -> c p j e", p=P, j=CHUNK)
+        out_rows = out.rearrange("(c p j) e -> c p j e", p=P, j=CHUNK)
+
+        def load_old(h):
+            nc.sync.dma_start(out=old_sb[h][:], in_=old_rows[h])
+
+        def load_query(c):
+            nc.sync.dma_start(out=query_sb[c][:], in_=query_rows[c])
+
+        def load_gate(c):
+            nc.sync.dma_start(out=gate_sb[c][:], in_=gate_rows[c])
+
+        def load_retain():
+            nc.sync.dma_start(out=retain_sb[:], in_=retain.rearrange("(h p t) -> p h t", p=P, t=PACK))
+
+        retained = [kept(f"retained{h}", [P, E, PACK], F32) for h in range(D_PASSES)]
+        memory = [kept(f"memory{h}", [P, E, PACK], BF16) for h in range(D_PASSES)]
+        m_codes = [kept(f"m_codes{h}", [P, E], U32) for h in range(D_PASSES)]
+        m_scale = [kept(f"m_scale{h}", [P, E], U8) for h in range(D_PASSES)]
+        q_codes = [kept(f"q_codes{i}", [P, D_PASSES * P], U32) for i in range(R_TILES)]
+        q_scale = [kept(f"q_scale{i}", [P, D_PASSES * P], U8) for i in range(R_TILES)]
+        write_t, turned, split, q_turned, grouped, result, acc = {}, {}, {}, {}, {}, {}, {}
+
+        def retain_old(h, j):
+            cols = slice(P * j, P * (j + 1))
+            nc.vector.tensor_tensor(
+                out=retained[h][:, cols, :],
+                in0=old_sb[h][:, :, cols].rearrange("p t e -> p e t"),
+                in1=retain_sb[:, h, :].unsqueeze(1).to_broadcast([P, P, PACK]),
+                op=MULT,
+            )
+
+        def write_pass(h, j, g, b):
+            if g == 0:
+                acc[h, j] = bank(b, [P, K_PASS])
+            nc.tensor.matmul_mx(
+                out=acc[h, j][:],
+                lhsT=v_words["v", g][:, 2 * P * j : 2 * P * (j + 1)].bitcast(FP4X4),
+                lhsT_scale=v_scale[g][:, P * j : P * (j + 1)],
+                rhs=k_words["k", g][:, 2 * K_PASS * h : 2 * K_PASS * (h + 1)].bitcast(FP4X4),
+                rhs_scale=k_scale[g][:, K_PASS * h : K_PASS * (h + 1)],
+                start=(g == 0),
+                stop=(g == T_PASSES - 1),
+            )
+
+        def write_group(h, j, b):
+            for g in range(T_PASSES):
+                write_pass(h, j, g, b)
+
+        def write_out(h, j, on_vector=False):
+            w = ring.tile([P, PACK, P], F32, name=f"write_t{h}{j}", tag="write_t", bufs=8)
+            copy = nc.vector.tensor_copy if on_vector else nc.scalar.copy
+            copy(out=w[:], in_=acc[h, j][:].rearrange("e (p t) -> e t p", t=PACK))
+            write_t[h, j] = w
+
+        def turn_write(h, j, b):
+            turned[h, j] = bank(b, [P, PACK, P])
+            for t in range(PACK):
+                nc.tensor.transpose(turned[h, j][:, t, :], write_t[h, j][:, t, :], ident[:])
+
+        def add_old(h, j):
+            cols = slice(P * j, P * (j + 1))
+            nc.vector.tensor_tensor(
+                out=memory[h][:, cols, :],
+                in0=turned[h, j][:].rearrange("p t e -> p e t"),
+                in1=retained[h][:, cols, :],
+                op=ADD,
+            )
+
+        def quantize_memory(h, j0, j1):
+            cols = slice(P * j0, P * j1)
+            nc.vector.quantize_mx(
+                out=m_codes[h][:, cols].bitcast(FP8X4),
+                scales=m_scale[h][:, cols],
+                in_=memory[h][:, cols, :].rearrange("p e t -> p (e t)"),
+            )
+
+        def split_query(i, on_vector):
+            s = keep.tile([P, D_PASSES, 2, P], F32, name=f"split{i}", tag="split", bufs=16, align_bytes=64)
+            words = query_sb[i // CHUNK][:, i % CHUNK, :].bitcast(F32).rearrange("r (g p u) -> r g u p", g=D_PASSES, u=2)
+            if on_vector:
+                nc.vector.tensor_copy(out=s[:], in_=words)
+            else:
+                nc.scalar.copy(out=s[:], in_=words)
+            split[i] = s
+
+        def turn_query(i, b):
+            q_turned[i] = bank(b, [P, D_PASSES, 2, P])
+            for g in range(D_PASSES):
+                for u in range(2):
+                    nc.tensor.transpose(q_turned[i][:, g, u, :], split[i][:, g, u, :], ident[:])
+
+        def query_out(i, on_vector):
+            q = ring.tile([P, D_PASSES * K_PASS], BF16, name=f"grouped{i}", tag="grouped", bufs=6, align_bytes=64)
+            copy = nc.vector.tensor_copy if on_vector else nc.scalar.copy
+            copy(
+                out=q[:].bitcast(F32).rearrange("p (g r u) -> p g r u", g=D_PASSES, u=2),
+                in_=q_turned[i][:].rearrange("p g u r -> p g r u"),
+            )
+            grouped[i] = q
+
+        def quantize_query(i):
+            nc.vector.quantize_mx(out=q_codes[i][:].bitcast(FP8X4), scales=q_scale[i][:], in_=grouped[i][:])
+
+        def read(i, b):
+            acc[i] = bank(b, [P, E])
+            for g in range(D_PASSES):
+                rows = slice(P * g, P * (g + 1))
+                nc.tensor.matmul_mx(
+                    out=acc[i][:],
+                    lhsT=q_codes[i][:, rows].bitcast(FP8X4),
+                    lhsT_scale=q_scale[i][:, rows],
+                    rhs=m_codes[g][:].bitcast(FP8X4),
+                    rhs_scale=m_scale[g][:],
+                    start=(g == 0),
+                    stop=(g == D_PASSES - 1),
+                )
+
+        def gate_out(i):
+            c, j = divmod(i, CHUNK)
+            if i % 2 == 0:
+                result[i // 2] = ring.tile([P, 2, E], F32, name=f"result{i}", tag="result")
+            nc.vector.tensor_tensor(out=result[i // 2][:, i % 2, :], in0=acc[i][:], in1=gate_sb[c][:, j, :], op=MULT)
+            if i >= R_TILES - 2:
+                nc.sync.dma_start(out=out_rows[c][:, j, :], in_=result[i // 2][:, i % 2, :])
+            elif i % 2 == 1:
+                nc.sync.dma_start(out=out_rows[c][:, j - 1 : j + 1, :], in_=result[i // 2][:])
+
+        load_first_words(0, 1)
+        load_scale_run(0)
+        load_first_words(1, 3)
+        load_scale_run(1)
+        load_first_words(3, 5)
+        load_old(0)
+        load_first_words(5, 6)
+        load_retain()
+        load_first_words(6, 8)
+        load_old(1)
+        load_query(0)
+        load_query(2)
+        load_gate(0)
+        load_query(3)
+        load_query(1)
+        load_gate(2)
+        load_gate(3)
+        load_gate(1)
+        write_pass(0, 0, 0, 0)
+        write_pass(0, 1, 0, 1)
+        write_pass(0, 2, 0, 2)
+        write_pass(0, 3, 0, 3)
+        write_pass(1, 0, 0, 4)
+        write_pass(1, 1, 0, 5)
+        write_pass(0, 0, 1, 0)
+        write_pass(0, 1, 1, 1)
+        write_pass(0, 2, 1, 2)
+        write_pass(0, 3, 1, 3)
+        write_pass(1, 0, 1, 4)
+        write_pass(1, 1, 1, 5)
+        write_pass(0, 0, 2, 0)
+        write_pass(0, 1, 2, 1)
+        write_pass(0, 2, 2, 2)
+        write_pass(0, 3, 2, 3)
+        write_pass(1, 0, 2, 4)
+        write_pass(1, 1, 2, 5)
+        write_pass(0, 0, 3, 0)
+        write_pass(0, 1, 3, 1)
+        write_pass(0, 2, 3, 2)
+        write_pass(0, 3, 3, 3)
+        write_pass(1, 0, 3, 4)
+        write_pass(1, 1, 3, 5)
+        write_pass(0, 0, 4, 0)
+        write_pass(0, 1, 4, 1)
+        retain_old(0, 0)
+        write_pass(0, 2, 4, 2)
+        write_pass(0, 3, 4, 3)
+        write_pass(1, 0, 4, 4)
+        retain_old(0, 1)
+        write_pass(1, 1, 4, 5)
+        write_pass(0, 0, 5, 0)
+        retain_old(0, 2)
+        write_pass(0, 1, 5, 1)
+        write_pass(0, 2, 5, 2)
+        write_pass(0, 3, 5, 3)
+        retain_old(0, 3)
+        write_pass(1, 0, 5, 4)
+        write_pass(1, 1, 5, 5)
+        write_pass(0, 0, 6, 0)
+        retain_old(1, 0)
+        write_pass(0, 1, 6, 1)
+        write_pass(0, 2, 6, 2)
+        write_pass(0, 3, 6, 3)
+        retain_old(1, 1)
+        write_pass(1, 0, 6, 4)
+        write_pass(1, 1, 6, 5)
+        retain_old(1, 2)
+        write_pass(0, 0, 7, 0)
+        write_pass(0, 1, 7, 1)
+        write_pass(0, 2, 7, 2)
+        retain_old(1, 3)
+        split_query(2, False)
+        write_pass(0, 3, 7, 3)
+        write_pass(1, 0, 7, 4)
+        split_query(1, False)
+        split_query(3, True)
+        write_pass(1, 1, 7, 5)
+        write_out(0, 0, True)
+        write_group(1, 2, 6)
+        write_out(0, 1, False)
+        write_out(0, 2, True)
+        write_out(1, 1, False)
+        write_out(0, 3, True)
+        split_query(0, False)
+        split_query(8, True)
+        split_query(9, False)
+        write_out(1, 0, True)
+        split_query(10, False)
+        turn_query(1, 7)
+        split_query(11, True)
+        turn_write(0, 2, 0)
+        write_out(1, 2, False)
+        turn_write(0, 1, 1)
+        turn_query(2, 2)
+        query_out(1, False)
+        add_old(0, 2)
+        turn_write(1, 0, 3)
+        add_old(0, 1)
+        turn_write(0, 0, 4)
+        query_out(2, False)
+        turn_write(0, 3, 5)
+        quantize_query(1)
+        split_query(12, False)
+        turn_write(1, 2, 6)
+        add_old(1, 0)
+        turn_write(1, 1, 7)
+        split_query(15, False)
+        quantize_query(2)
+        write_group(1, 3, 0)
+        add_old(0, 0)
+        split_query(13, False)
+        add_old(0, 3)
+        split_query(14, False)
+        split_query(7, True)
+        split_query(6, False)
+        add_old(1, 2)
+        split_query(4, False)
+        add_old(1, 1)
+        turn_query(0, 1)
+        write_out(1, 3, False)
+        turn_query(7, 2)
+        quantize_memory(0, 0, 4)
+        turn_query(3, 3)
+        query_out(0, False)
+        quantize_memory(1, 0, 2)
+        quantize_memory(1, 2, 3)
+        turn_query(4, 4)
+        turn_write(1, 3, 5)
+        split_query(5, True)
+        query_out(7, False)
+        turn_query(6, 6)
+        quantize_query(0)
+        query_out(3, False)
+        turn_query(10, 7)
+        add_old(1, 3)
+        turn_query(5, 0)
+        query_out(4, False)
+        quantize_query(7)
+        turn_query(9, 1)
+        quantize_query(3)
+        turn_query(11, 2)
+        query_out(6, False)
+        quantize_memory(1, 3, 4)
+        quantize_query(4)
+        read(0, 3)
+        query_out(10, False)
+        query_out(9, True)
+        turn_query(12, 4)
+        query_out(5, False)
+        quantize_query(6)
+        turn_query(15, 5)
+        quantize_query(10)
+        query_out(11, False)
+        quantize_query(9)
+        read(1, 6)
+        quantize_query(5)
+        query_out(12, False)
+        gate_out(0)
+        turn_query(8, 7)
+        query_out(15, False)
+        quantize_query(11)
+        read(2, 0)
+        quantize_query(12)
+        query_out(8, False)
+        gate_out(1)
+        read(3, 1)
+        quantize_query(15)
+        read(4, 2)
+        quantize_query(8)
+        read(5, 3)
+        gate_out(2)
+        read(6, 4)
+        gate_out(3)
+        read(7, 5)
+        gate_out(4)
+        read(8, 6)
+        gate_out(5)
+        gate_out(6)
+        turn_query(13, 7)
+        turn_query(14, 0)
+        gate_out(7)
+        query_out(13, False)
+        read(9, 1)
+        gate_out(8)
+        query_out(14, False)
+        read(10, 2)
+        quantize_query(13)
+        gate_out(9)
+        read(11, 3)
+        quantize_query(14)
+        read(12, 4)
+        gate_out(10)
+        read(13, 5)
+        gate_out(11)
+        read(14, 6)
+        gate_out(12)
+        read(15, 7)
+        gate_out(13)
+        gate_out(14)
+        gate_out(15)

@@ -25,7 +25,10 @@ D_PASSES = D // K_PASS
 E_TILES = E // P
 R_TILES = R // P
 CHUNK = 4
-SCALE_RUNS = [(0, 2), (2, 8)]
+HALF = E // 2
+WARM_PASSES = 18
+SINGLE = [0,1,3,4,5,6,7]
+SCALE_RUNS = [(0, 3), (3, 8)]
 
 
 def tile_memory_write_read_s4_kernel(
@@ -53,12 +56,31 @@ def tile_memory_write_read_s4_kernel(
             return plane
 
         v_planes, k_planes, v_scale, k_scale = {}, {}, {}, {}
+        warm = kept("warm", [P, K_PASS], BF16)
+        warm_codes = kept("warm_codes", [P, P], U32)
+        warm_scale = kept("warm_scale", [P, P], U8)
         for g0, g1 in SCALE_RUNS:
             v_planes[g0] = scale_plane(f"v_scale{g0}", g1 - g0, E)
+            if g0 == 0:
+                nc.vector.memset(warm[:], 1.0)
+            else:
+                nc.vector.quantize_mx(out=warm_codes[:].bitcast(FP8X4), scales=warm_scale[:], in_=warm[:])
             k_planes[g0] = scale_plane(f"k_scale{g0}", g1 - g0, D)
             for g in range(g0, g1):
                 v_scale[g] = v_planes[g0][:, g - g0, :]
                 k_scale[g] = k_planes[g0][:, g - g0, :]
+
+        warm_out = bank(7, [P, P])
+        for n in range(WARM_PASSES):
+            nc.tensor.matmul_mx(
+                out=warm_out[:],
+                lhsT=warm_codes[:].bitcast(FP8X4),
+                lhsT_scale=warm_scale[:],
+                rhs=warm_codes[:].bitcast(FP8X4),
+                rhs_scale=warm_scale[:],
+                start=True,
+                stop=True,
+            )
 
         def load_scale_run(n):
             g0, g1 = SCALE_RUNS[n]
@@ -84,7 +106,7 @@ def tile_memory_write_read_s4_kernel(
 
         retain_sb = kept("retain_sb", [P, D_PASSES, PACK], BF16)
         old_sb = [kept(f"old_sb{h}", [P, PACK, E], BF16) for h in range(D_PASSES)]
-        query_sb = [kept(f"query_sb{c}", [P, CHUNK, D], BF16) for c in range(R_TILES // CHUNK)]
+        query_sb = [kept(f"query_sb{c}", [P, 2, D], BF16) for c in range(R_TILES // 2)]
         gate_sb = [kept(f"gate_sb{c}", [P, CHUNK, E], BF16) for c in range(R_TILES // CHUNK)]
         old_rows = old.rearrange("(h p t) e -> h p t e", p=P, t=PACK)
         query_rows = query.rearrange("(c p j) d -> c p j d", p=P, j=CHUNK)
@@ -95,7 +117,7 @@ def tile_memory_write_read_s4_kernel(
             nc.sync.dma_start(out=old_sb[h][:], in_=old_rows[h])
 
         def load_query(c):
-            nc.sync.dma_start(out=query_sb[c][:], in_=query_rows[c])
+            nc.sync.dma_start(out=query_sb[c][:], in_=query_rows[c // 2][:, 2 * (c % 2) : 2 * (c % 2) + 2, :])
 
         def load_gate(c):
             nc.sync.dma_start(out=gate_sb[c][:], in_=gate_rows[c])
@@ -107,16 +129,15 @@ def tile_memory_write_read_s4_kernel(
         memory = [kept(f"memory{h}", [P, E, PACK], BF16) for h in range(D_PASSES)]
         m_codes = [kept(f"m_codes{h}", [P, E], U32) for h in range(D_PASSES)]
         m_scale = [kept(f"m_scale{h}", [P, E], U8) for h in range(D_PASSES)]
-        q_codes = [kept(f"q_codes{i}", [P, D_PASSES * P], U32) for i in range(R_TILES)]
-        q_scale = [kept(f"q_scale{i}", [P, D_PASSES * P], U8) for i in range(R_TILES)]
-        write_t, turned, split, q_turned, grouped, result, acc = {}, {}, {}, {}, {}, {}, {}
+        q_codes = [kept(f"q_codes{i}", [P, 2 * D_PASSES * P], U32) for i in range(R_TILES // 2)]
+        q_scale = [kept(f"q_scale{i}", [P, 2 * D_PASSES * P], U8) for i in range(R_TILES // 2)]
+        write_t, turned, split, q_turned, grouped, result, acc, sums = {}, {}, {}, {}, {}, {}, {}, {}
 
-        def retain_old(h, j):
-            cols = slice(P * j, P * (j + 1))
+        def retain_old(h):
             nc.vector.tensor_tensor(
-                out=retained[h][:, cols, :],
-                in0=old_sb[h][:, :, cols].rearrange("p t e -> p e t"),
-                in1=retain_sb[:, h, :].unsqueeze(1).to_broadcast([P, P, PACK]),
+                out=retained[h][:],
+                in0=old_sb[h][:].rearrange("p t e -> p e t"),
+                in1=retain_sb[:, h, :].unsqueeze(1).to_broadcast([P, E, PACK]),
                 op=MULT,
             )
 
@@ -138,7 +159,7 @@ def tile_memory_write_read_s4_kernel(
                 write_pass(h, j, g, b)
 
         def write_out(h, j, on_vector=False):
-            w = ring.tile([P, PACK, P], F32, name=f"write_t{h}{j}", tag="write_t", bufs=8)
+            w = ring.tile([P, PACK, P], F32, name=f"write_t{h}{j}", tag="write_t", bufs=6)
             copy = nc.vector.tensor_copy if on_vector else nc.scalar.copy
             copy(out=w[:], in_=acc[h, j][:].rearrange("e (p t) -> e t p", t=PACK))
             write_t[h, j] = w
@@ -157,262 +178,307 @@ def tile_memory_write_read_s4_kernel(
                 op=ADD,
             )
 
-        def quantize_memory(h, j0, j1):
-            cols = slice(P * j0, P * j1)
+        def quantize_memory(h, side):
+            cols = slice(HALF * side, HALF * (side + 1))
             nc.vector.quantize_mx(
                 out=m_codes[h][:, cols].bitcast(FP8X4),
                 scales=m_scale[h][:, cols],
                 in_=memory[h][:, cols, :].rearrange("p e t -> p (e t)"),
             )
 
-        def split_query(i, on_vector):
-            s = keep.tile([P, D_PASSES, 2, P], F32, name=f"split{i}", tag="split", bufs=16, align_bytes=64)
-            words = query_sb[i // CHUNK][:, i % CHUNK, :].bitcast(F32).rearrange("r (g p u) -> r g u p", g=D_PASSES, u=2)
-            if on_vector:
-                nc.vector.tensor_copy(out=s[:], in_=words)
-            else:
-                nc.scalar.copy(out=s[:], in_=words)
-            split[i] = s
+        def split_query(c, on_vector):
+            s = keep.tile([P, 2 * D_PASSES, 2, P], F32, name=f"split{c}", tag="split", bufs=6, align_bytes=64)
+            words = query_sb[c][:].rearrange("r j d -> r (j d)").bitcast(F32)
+            copy = nc.vector.tensor_copy if on_vector else nc.scalar.copy
+            copy(out=s[:], in_=words.rearrange("r (n p u) -> r n u p", p=P, u=2))
+            split[c] = s
 
         def turn_query(i, b):
             q_turned[i] = bank(b, [P, D_PASSES, 2, P])
             for g in range(D_PASSES):
                 for u in range(2):
-                    nc.tensor.transpose(q_turned[i][:, g, u, :], split[i][:, g, u, :], ident[:])
+                    if i // 2 in split:
+                        src = split[i // 2][:, D_PASSES * (i % 2) + g, u, :]
+                    else:
+                        src = query_sb[i // 2][:, i % 2, :].bitcast(F32)[:, 2 * P * g + u : 2 * P * (g + 1) : 2]
+                    nc.tensor.transpose(q_turned[i][:, g, u, :], src, ident[:])
 
         def query_out(i, on_vector):
-            q = ring.tile([P, D_PASSES * K_PASS], BF16, name=f"grouped{i}", tag="grouped", bufs=6, align_bytes=64)
+            if i // 2 not in grouped:
+                grouped[i // 2] = ring.tile([P, 2, D], BF16, name=f"grouped{i}", tag="grouped", bufs=4, align_bytes=64)
             copy = nc.vector.tensor_copy if on_vector else nc.scalar.copy
             copy(
-                out=q[:].bitcast(F32).rearrange("p (g r u) -> p g r u", g=D_PASSES, u=2),
+                out=grouped[i // 2][:, i % 2, :].bitcast(F32).rearrange("p (g r u) -> p g r u", g=D_PASSES, u=2),
                 in_=q_turned[i][:].rearrange("p g u r -> p g r u"),
             )
-            grouped[i] = q
 
-        def quantize_query(i):
-            nc.vector.quantize_mx(out=q_codes[i][:].bitcast(FP8X4), scales=q_scale[i][:], in_=grouped[i][:])
+        def quantize_query(c):
+            nc.vector.quantize_mx(
+                out=q_codes[c][:].bitcast(FP8X4), scales=q_scale[c][:], in_=grouped[c][:].rearrange("p j d -> p (j d)")
+            )
 
         def read(i, b):
             acc[i] = bank(b, [P, E])
             for g in range(D_PASSES):
-                rows = slice(P * g, P * (g + 1))
+                n = D_PASSES * (i % 2) + g
+                rows = slice(P * n, P * (n + 1))
                 nc.tensor.matmul_mx(
                     out=acc[i][:],
-                    lhsT=q_codes[i][:, rows].bitcast(FP8X4),
-                    lhsT_scale=q_scale[i][:, rows],
+                    lhsT=q_codes[i // 2][:, rows].bitcast(FP8X4),
+                    lhsT_scale=q_scale[i // 2][:, rows],
                     rhs=m_codes[g][:].bitcast(FP8X4),
                     rhs_scale=m_scale[g][:],
                     start=(g == 0),
                     stop=(g == D_PASSES - 1),
                 )
 
-        def gate_out(i):
+        def read_out(i):
+            sums[i] = ring.tile([P, E], F32, name="sums", tag="sums", bufs=2)
+            nc.scalar.copy(out=sums[i][:], in_=acc[i][:])
+
+        def gate_out(i, on_gpsimd):
             c, j = divmod(i, CHUNK)
-            if i % 2 == 0:
-                result[i // 2] = ring.tile([P, 2, E], F32, name=f"result{i}", tag="result")
-            nc.vector.tensor_tensor(out=result[i // 2][:, i % 2, :], in0=acc[i][:], in1=gate_sb[c][:, j, :], op=MULT)
-            if i >= R_TILES - 2:
+            if i // 2 not in result:
+                result[i // 2] = ring.tile([P, 2, E], F32, name=f"result{i}", tag="result", bufs=3)
+            if on_gpsimd:
+                nc.gpsimd.tensor_tensor(out=result[i // 2][:, i % 2, :], in0=sums[i][:], in1=gate_sb[c][:, j, :], op=MULT)
+            else:
+                nc.vector.tensor_tensor(out=result[i // 2][:, i % 2, :], in0=acc[i][:], in1=gate_sb[c][:, j, :], op=MULT)
+
+        def store(i):
+            c, j = divmod(i, CHUNK)
+            if i // 2 in SINGLE:
                 nc.sync.dma_start(out=out_rows[c][:, j, :], in_=result[i // 2][:, i % 2, :])
             elif i % 2 == 1:
                 nc.sync.dma_start(out=out_rows[c][:, j - 1 : j + 1, :], in_=result[i // 2][:])
 
+
+        def read_half(c, side, b):
+            cols = slice(HALF * side, HALF * (side + 1))
+            acc[c, side, "read"] = bank(b, [P, 2, HALF])
+            for j in range(2):
+                for g in range(D_PASSES):
+                    n = D_PASSES * j + g
+                    rows = slice(P * n, P * (n + 1))
+                    nc.tensor.matmul_mx(
+                        out=acc[c, side, "read"][:, j, :],
+                        lhsT=q_codes[c][:, rows].bitcast(FP8X4),
+                        lhsT_scale=q_scale[c][:, rows],
+                        rhs=m_codes[g][:, cols].bitcast(FP8X4),
+                        rhs_scale=m_scale[g][:, cols],
+                        start=(g == 0),
+                        stop=(g == D_PASSES - 1),
+                    )
+
+        def gate_half(c, side):
+            cols = slice(HALF * side, HALF * (side + 1))
+            rows = slice(2 * (c % 2), 2 * (c % 2) + 2)
+            r = ring.tile([P, 2, HALF], F32, name=f"result{c}{side}", tag="half", bufs=6)
+            nc.vector.tensor_tensor(out=r[:], in0=acc[c, side, "read"][:], in1=gate_sb[c // 2][:, rows, cols], op=MULT)
+            result[c, side, "half"] = r
+
+        def store_half(c, side):
+            cols = slice(HALF * side, HALF * (side + 1))
+            rows = slice(2 * (c % 2), 2 * (c % 2) + 2)
+            nc.sync.dma_start(out=out_rows[c // 2][:, rows, cols], in_=result[c, side, "half"][:])
+
         load_first_words(0, 1)
         load_scale_run(0)
-        load_first_words(1, 3)
+        load_first_words(1, 2)
+        load_first_words(2, 3)
         load_scale_run(1)
         load_first_words(3, 5)
         load_old(0)
-        load_first_words(5, 6)
         load_retain()
-        load_first_words(6, 8)
+        load_first_words(5, 6)
+        load_first_words(6, 7)
         load_old(1)
+        load_first_words(7, 8)
         load_query(0)
-        load_query(2)
-        load_gate(0)
-        load_query(3)
         load_query(1)
-        load_gate(2)
-        load_gate(3)
+        load_query(2)
+        load_query(3)
+        load_query(4)
+        load_gate(0)
         load_gate(1)
+        load_query(5)
+        load_gate(2)
+        load_query(6)
+        load_query(7)
+        load_gate(3)
         write_pass(0, 0, 0, 0)
-        write_pass(0, 1, 0, 1)
-        write_pass(0, 2, 0, 2)
-        write_pass(0, 3, 0, 3)
-        write_pass(1, 0, 0, 4)
-        write_pass(1, 1, 0, 5)
+        write_pass(1, 0, 0, 1)
+        write_pass(0, 1, 0, 2)
+        write_pass(1, 1, 0, 3)
+        write_pass(0, 2, 0, 4)
+        write_pass(1, 2, 0, 5)
         write_pass(0, 0, 1, 0)
-        write_pass(0, 1, 1, 1)
-        write_pass(0, 2, 1, 2)
-        write_pass(0, 3, 1, 3)
-        write_pass(1, 0, 1, 4)
-        write_pass(1, 1, 1, 5)
+        write_pass(1, 0, 1, 1)
+        write_pass(0, 1, 1, 2)
+        write_pass(1, 1, 1, 3)
+        write_pass(0, 2, 1, 4)
+        write_pass(1, 2, 1, 5)
         write_pass(0, 0, 2, 0)
-        write_pass(0, 1, 2, 1)
-        write_pass(0, 2, 2, 2)
-        write_pass(0, 3, 2, 3)
-        write_pass(1, 0, 2, 4)
-        write_pass(1, 1, 2, 5)
+        write_pass(1, 0, 2, 1)
+        write_pass(0, 1, 2, 2)
+        write_pass(1, 1, 2, 3)
+        write_pass(0, 2, 2, 4)
+        write_pass(1, 2, 2, 5)
+        retain_old(0)
         write_pass(0, 0, 3, 0)
-        write_pass(0, 1, 3, 1)
-        write_pass(0, 2, 3, 2)
-        write_pass(0, 3, 3, 3)
-        write_pass(1, 0, 3, 4)
-        write_pass(1, 1, 3, 5)
+        write_pass(1, 0, 3, 1)
+        write_pass(0, 1, 3, 2)
+        write_pass(1, 1, 3, 3)
+        write_pass(0, 2, 3, 4)
+        write_pass(1, 2, 3, 5)
         write_pass(0, 0, 4, 0)
-        write_pass(0, 1, 4, 1)
-        retain_old(0, 0)
-        write_pass(0, 2, 4, 2)
-        write_pass(0, 3, 4, 3)
-        write_pass(1, 0, 4, 4)
-        retain_old(0, 1)
-        write_pass(1, 1, 4, 5)
+        write_pass(1, 0, 4, 1)
+        write_pass(0, 1, 4, 2)
+        write_pass(1, 1, 4, 3)
+        write_pass(0, 2, 4, 4)
+        write_pass(1, 2, 4, 5)
+        retain_old(1)
         write_pass(0, 0, 5, 0)
-        retain_old(0, 2)
-        write_pass(0, 1, 5, 1)
-        write_pass(0, 2, 5, 2)
-        write_pass(0, 3, 5, 3)
-        retain_old(0, 3)
-        write_pass(1, 0, 5, 4)
-        write_pass(1, 1, 5, 5)
+        write_pass(1, 0, 5, 1)
+        write_pass(0, 1, 5, 2)
+        write_pass(1, 1, 5, 3)
+        write_pass(0, 2, 5, 4)
+        write_pass(1, 2, 5, 5)
         write_pass(0, 0, 6, 0)
-        retain_old(1, 0)
-        write_pass(0, 1, 6, 1)
-        write_pass(0, 2, 6, 2)
-        write_pass(0, 3, 6, 3)
-        retain_old(1, 1)
-        write_pass(1, 0, 6, 4)
-        write_pass(1, 1, 6, 5)
-        retain_old(1, 2)
         write_pass(0, 0, 7, 0)
-        write_pass(0, 1, 7, 1)
-        write_pass(0, 2, 7, 2)
-        retain_old(1, 3)
-        split_query(2, False)
-        write_pass(0, 3, 7, 3)
-        write_pass(1, 0, 7, 4)
+        write_out(0, 0, False)
+        write_pass(1, 0, 6, 0)
+        write_pass(1, 0, 7, 0)
+        write_out(1, 0, False)
+        write_pass(0, 1, 6, 0)
+        write_pass(0, 1, 7, 0)
+        split_query(0, True)
+        write_pass(1, 1, 6, 0)
+        write_pass(1, 1, 7, 0)
         split_query(1, False)
-        split_query(3, True)
-        write_pass(1, 1, 7, 5)
-        write_out(0, 0, True)
-        write_group(1, 2, 6)
-        write_out(0, 1, False)
-        write_out(0, 2, True)
-        write_out(1, 1, False)
-        write_out(0, 3, True)
-        split_query(0, False)
-        split_query(8, True)
-        split_query(9, False)
-        write_out(1, 0, True)
-        split_query(10, False)
-        turn_query(1, 7)
-        split_query(11, True)
-        turn_write(0, 2, 0)
-        write_out(1, 2, False)
-        turn_write(0, 1, 1)
-        turn_query(2, 2)
-        query_out(1, False)
-        add_old(0, 2)
-        turn_write(1, 0, 3)
-        add_old(0, 1)
-        turn_write(0, 0, 4)
-        query_out(2, False)
-        turn_write(0, 3, 5)
-        quantize_query(1)
-        split_query(12, False)
-        turn_write(1, 2, 6)
-        add_old(1, 0)
-        turn_write(1, 1, 7)
-        split_query(15, False)
-        quantize_query(2)
-        write_group(1, 3, 0)
-        add_old(0, 0)
-        split_query(13, False)
-        add_old(0, 3)
-        split_query(14, False)
-        split_query(7, True)
-        split_query(6, False)
-        add_old(1, 2)
-        split_query(4, False)
-        add_old(1, 1)
-        turn_query(0, 1)
-        write_out(1, 3, False)
-        turn_query(7, 2)
-        quantize_memory(0, 0, 4)
-        turn_query(3, 3)
+        write_out(1, 1, True)
+        write_pass(0, 2, 6, 0)
+        write_pass(0, 2, 7, 0)
+        write_out(0, 1, True)
+        write_pass(1, 2, 6, 0)
+        write_pass(1, 2, 7, 0)
+        write_out(0, 2, False)
+        turn_query(0, 6)
+        split_query(2, True)
+        turn_write(0, 0, 7)
         query_out(0, False)
-        quantize_memory(1, 0, 2)
-        quantize_memory(1, 2, 3)
-        turn_query(4, 4)
-        turn_write(1, 3, 5)
-        split_query(5, True)
-        query_out(7, False)
-        turn_query(6, 6)
-        quantize_query(0)
+        turn_write(1, 0, 0)
+        add_old(0, 0)
+        turn_query(1, 1)
+        write_out(1, 2, False)
+        turn_write(0, 1, 3)
+        add_old(1, 0)
+        query_out(1, False)
+        turn_query(2, 2)
+        turn_query(3, 4)
+        add_old(0, 1)
+        query_out(2, False)
+        turn_query(4, 6)
+        split_query(3, True)
+        turn_query(5, 7)
         query_out(3, False)
-        turn_query(10, 7)
-        add_old(1, 3)
-        turn_query(5, 0)
+        turn_write(1, 1, 5)
+        quantize_memory(0, 0)
+        turn_write(0, 2, 0)
         query_out(4, False)
-        quantize_query(7)
-        turn_query(9, 1)
-        quantize_query(3)
-        turn_query(11, 2)
-        query_out(6, False)
-        quantize_memory(1, 3, 4)
-        quantize_query(4)
-        read(0, 3)
-        query_out(10, False)
-        query_out(9, True)
-        turn_query(12, 4)
+        add_old(1, 1)
+        turn_write(1, 2, 1)
+        turn_query(6, 3)
         query_out(5, False)
-        quantize_query(6)
-        turn_query(15, 5)
-        quantize_query(10)
-        query_out(11, False)
-        quantize_query(9)
-        read(1, 6)
-        quantize_query(5)
-        query_out(12, False)
-        gate_out(0)
-        turn_query(8, 7)
-        query_out(15, False)
-        quantize_query(11)
-        read(2, 0)
-        quantize_query(12)
+        add_old(0, 2)
+        turn_query(7, 2)
+        add_old(1, 2)
+        quantize_query(0)
+        quantize_query(1)
+        query_out(6, False)
+        write_group(0, 3, 4)
+        quantize_query(2)
+        write_out(0, 3, False)
+        query_out(7, True)
+        split_query(5, False)
+        quantize_memory(1, 0)
+        quantize_query(3)
+        split_query(6, False)
+        write_group(1, 3, 6)
+        split_query(4, True)
+        turn_write(0, 3, 5)
+        add_old(0, 3)
+        write_out(1, 3, False)
+        read_half(3, 0, 7)
+        gate_half(3, 0)
+        store_half(3, 0)
+        split_query(7, False)
+        read_half(2, 0, 0)
+        gate_half(2, 0)
+        store_half(2, 0)
+        read_half(0, 0, 1)
+        turn_write(1, 3, 3)
+        quantize_memory(0, 1)
+        turn_query(8, 4)
+        add_old(1, 3)
+        turn_query(9, 2)
         query_out(8, False)
-        gate_out(1)
-        read(3, 1)
-        quantize_query(15)
-        read(4, 2)
-        quantize_query(8)
-        read(5, 3)
-        gate_out(2)
-        read(6, 4)
-        gate_out(3)
-        read(7, 5)
-        gate_out(4)
-        read(8, 6)
-        gate_out(5)
-        gate_out(6)
-        turn_query(13, 7)
-        turn_query(14, 0)
-        gate_out(7)
+        gate_half(0, 0)
+        store_half(0, 0)
+        read_half(1, 0, 5)
+        query_out(9, False)
+        quantize_memory(1, 1)
+        turn_query(10, 6)
+        gate_half(1, 0)
+        store_half(1, 0)
+        turn_query(11, 7)
+        query_out(10, False)
+        quantize_query(4)
+        read_half(2, 1, 0)
+        query_out(11, False)
+        gate_half(2, 1)
+        store_half(2, 1)
+        read_half(1, 1, 3)
+        quantize_query(5)
+        read_half(0, 1, 4)
+        read_half(4, 0, 1)
+        gate_half(0, 1)
+        store_half(0, 1)
+        read_half(4, 1, 2)
+        gate_half(1, 1)
+        store_half(1, 1)
+        turn_query(12, 5)
+        gate_half(4, 1)
+        store_half(4, 1)
+        turn_query(13, 6)
+        query_out(12, False)
+        gate_half(4, 0)
+        store_half(4, 0)
+        read(10, 7)
         query_out(13, False)
-        read(9, 1)
-        gate_out(8)
+        gate_out(10, False)
+        store(10)
+        read_half(3, 1, 0)
+        turn_query(14, 4)
+        gate_half(3, 1)
+        store_half(3, 1)
+        turn_query(15, 3)
         query_out(14, False)
-        read(10, 2)
-        quantize_query(13)
-        gate_out(9)
-        read(11, 3)
-        quantize_query(14)
-        read(12, 4)
-        gate_out(10)
-        read(13, 5)
-        gate_out(11)
+        quantize_query(6)
+        read(11, 2)
+        query_out(15, False)
+        gate_out(11, False)
+        store(11)
+        quantize_query(7)
+        read(12, 5)
+        gate_out(12, False)
+        store(12)
+        read(13, 1)
+        gate_out(13, False)
+        store(13)
         read(14, 6)
-        gate_out(12)
+        gate_out(14, False)
+        store(14)
         read(15, 7)
-        gate_out(13)
-        gate_out(14)
-        gate_out(15)
+        gate_out(15, False)
+        store(15)

@@ -26,8 +26,8 @@ E_TILES = E // P
 R_TILES = R // P
 CHUNK = 4
 HALF = E // 2
-WARM_PASSES = 18
-SINGLE = [0,1,3,4,5,6,7]
+WARM_PASSES = 36
+SINGLE = [0,2,3,4,5,6,7]
 SCALE_RUNS = [(0, 3), (3, 8)]
 
 
@@ -282,30 +282,28 @@ def tile_memory_write_read_s4_kernel(
             rows = slice(2 * (c % 2), 2 * (c % 2) + 2)
             nc.sync.dma_start(out=out_rows[c // 2][:, rows, cols], in_=result[c, side, "half"][:])
 
-        load_first_words(0, 1)
+        load_first_words(0, 2)
         load_scale_run(0)
-        load_first_words(1, 2)
-        load_first_words(2, 3)
         load_scale_run(1)
-        load_first_words(3, 5)
-        load_old(0)
+        load_first_words(2, 3)
         load_retain()
-        load_first_words(5, 6)
-        load_first_words(6, 7)
+        load_first_words(3, 4)
+        load_first_words(4, 6)
+        load_old(0)
+        load_first_words(6, 8)
         load_old(1)
-        load_first_words(7, 8)
+        load_gate(0)
         load_query(0)
         load_query(1)
         load_query(2)
         load_query(3)
         load_query(4)
-        load_gate(0)
         load_gate(1)
         load_query(5)
         load_gate(2)
         load_query(6)
-        load_query(7)
         load_gate(3)
+        load_query(7)
         write_pass(0, 0, 0, 0)
         write_pass(1, 0, 0, 1)
         write_pass(0, 1, 0, 2)
@@ -324,26 +322,26 @@ def tile_memory_write_read_s4_kernel(
         write_pass(1, 1, 2, 3)
         write_pass(0, 2, 2, 4)
         write_pass(1, 2, 2, 5)
-        retain_old(0)
         write_pass(0, 0, 3, 0)
         write_pass(1, 0, 3, 1)
         write_pass(0, 1, 3, 2)
         write_pass(1, 1, 3, 3)
         write_pass(0, 2, 3, 4)
         write_pass(1, 2, 3, 5)
+        retain_old(0)
         write_pass(0, 0, 4, 0)
         write_pass(1, 0, 4, 1)
         write_pass(0, 1, 4, 2)
         write_pass(1, 1, 4, 3)
         write_pass(0, 2, 4, 4)
         write_pass(1, 2, 4, 5)
-        retain_old(1)
         write_pass(0, 0, 5, 0)
         write_pass(1, 0, 5, 1)
         write_pass(0, 1, 5, 2)
         write_pass(1, 1, 5, 3)
         write_pass(0, 2, 5, 4)
         write_pass(1, 2, 5, 5)
+        retain_old(1)
         write_pass(0, 0, 6, 0)
         write_pass(0, 0, 7, 0)
         write_out(0, 0, False)
@@ -352,133 +350,133 @@ def tile_memory_write_read_s4_kernel(
         write_out(1, 0, False)
         write_pass(0, 1, 6, 0)
         write_pass(0, 1, 7, 0)
-        split_query(0, True)
+        write_out(0, 1, False)
         write_pass(1, 1, 6, 0)
         write_pass(1, 1, 7, 0)
-        split_query(1, False)
-        write_out(1, 1, True)
+        split_query(0, False)
         write_pass(0, 2, 6, 0)
         write_pass(0, 2, 7, 0)
-        write_out(0, 1, True)
+        write_out(1, 1, True)
         write_pass(1, 2, 6, 0)
         write_pass(1, 2, 7, 0)
+        split_query(1, True)
         write_out(0, 2, False)
-        turn_query(0, 6)
-        split_query(2, True)
-        turn_write(0, 0, 7)
-        query_out(0, False)
-        turn_write(1, 0, 0)
+        turn_write(0, 0, 6)
+        turn_write(1, 0, 7)
         add_old(0, 0)
-        turn_query(1, 1)
         write_out(1, 2, False)
-        turn_write(0, 1, 3)
+        turn_write(0, 1, 0)
+        turn_query(0, 1)
         add_old(1, 0)
-        query_out(1, False)
-        turn_query(2, 2)
-        turn_query(3, 4)
-        add_old(0, 1)
+        split_query(2, False)
+        turn_query(1, 2)
+        query_out(0, True)
+        turn_query(2, 3)
+        turn_write(1, 1, 4)
         query_out(2, False)
-        turn_query(4, 6)
+        query_out(1, True)
+        turn_write(0, 2, 6)
+        turn_query(3, 5)
         split_query(3, True)
-        turn_query(5, 7)
+        turn_query(4, 7)
         query_out(3, False)
-        turn_write(1, 1, 5)
-        quantize_memory(0, 0)
-        turn_write(0, 2, 0)
-        query_out(4, False)
-        add_old(1, 1)
         turn_write(1, 2, 1)
-        turn_query(6, 3)
-        query_out(5, False)
-        add_old(0, 2)
-        turn_query(7, 2)
-        add_old(1, 2)
         quantize_query(0)
+        query_out(4, False)
+        turn_query(5, 3)
         quantize_query(1)
+        turn_query(6, 2)
+        query_out(5, False)
+        turn_query(7, 5)
+        add_old(0, 1)
         query_out(6, False)
-        write_group(0, 3, 4)
         quantize_query(2)
-        write_out(0, 3, False)
-        query_out(7, True)
-        split_query(5, False)
+        query_out(7, False)
+        add_old(1, 1)
+        split_query(4, False)
+        quantize_memory(0, 0)
         quantize_memory(1, 0)
+        write_group(0, 3, 7)
+        add_old(0, 2)
+        split_query(5, False)
         quantize_query(3)
+        write_out(0, 3, True)
         split_query(6, False)
-        write_group(1, 3, 6)
-        split_query(4, True)
-        turn_write(0, 3, 5)
-        add_old(0, 3)
+        add_old(1, 2)
+        write_group(1, 3, 3)
         write_out(1, 3, False)
-        read_half(3, 0, 7)
-        gate_half(3, 0)
-        store_half(3, 0)
-        split_query(7, False)
-        read_half(2, 0, 0)
-        gate_half(2, 0)
-        store_half(2, 0)
-        read_half(0, 0, 1)
-        turn_write(1, 3, 3)
-        quantize_memory(0, 1)
-        turn_query(8, 4)
-        add_old(1, 3)
-        turn_query(9, 2)
-        query_out(8, False)
+        read_half(0, 0, 0)
         gate_half(0, 0)
         store_half(0, 0)
-        read_half(1, 0, 5)
+        read_half(2, 0, 2)
+        split_query(7, False)
+        gate_half(2, 0)
+        store_half(2, 0)
+        turn_write(0, 3, 5)
+        turn_write(1, 3, 4)
+        add_old(0, 3)
+        turn_query(8, 6)
+        turn_query(9, 7)
+        query_out(8, False)
+        add_old(1, 3)
+        turn_query(10, 1)
         query_out(9, False)
+        turn_query(11, 3)
+        quantize_memory(0, 1)
         quantize_memory(1, 1)
-        turn_query(10, 6)
-        gate_half(1, 0)
-        store_half(1, 0)
-        turn_query(11, 7)
+        turn_query(12, 0)
         query_out(10, False)
         quantize_query(4)
-        read_half(2, 1, 0)
+        read_half(1, 0, 2)
         query_out(11, False)
+        gate_half(1, 0)
+        store_half(1, 0)
+        read(6, 5)
+        query_out(12, False)
+        gate_out(6, False)
+        store(6)
+        read_half(2, 1, 6)
         gate_half(2, 1)
         store_half(2, 1)
-        read_half(1, 1, 3)
-        quantize_query(5)
         read_half(0, 1, 4)
-        read_half(4, 0, 1)
         gate_half(0, 1)
         store_half(0, 1)
-        read_half(4, 1, 2)
+        read(7, 7)
+        gate_out(7, False)
+        store(7)
+        read(8, 1)
+        gate_out(8, False)
+        store(8)
+        read_half(1, 1, 3)
+        quantize_query(5)
+        read(9, 2)
+        turn_query(13, 0)
         gate_half(1, 1)
         store_half(1, 1)
-        turn_query(12, 5)
-        gate_half(4, 1)
-        store_half(4, 1)
-        turn_query(13, 6)
-        query_out(12, False)
-        gate_half(4, 0)
-        store_half(4, 0)
-        read(10, 7)
+        turn_query(14, 5)
         query_out(13, False)
-        gate_out(10, False)
-        store(10)
-        read_half(3, 1, 0)
-        turn_query(14, 4)
-        gate_half(3, 1)
-        store_half(3, 1)
-        turn_query(15, 3)
+        gate_out(9, False)
+        store(9)
+        turn_query(15, 6)
         query_out(14, False)
         quantize_query(6)
-        read(11, 2)
+        read(10, 4)
         query_out(15, False)
+        gate_out(10, False)
+        store(10)
+        read(11, 7)
         gate_out(11, False)
         store(11)
+        read(12, 1)
         quantize_query(7)
-        read(12, 5)
+        read(13, 3)
         gate_out(12, False)
         store(12)
-        read(13, 1)
         gate_out(13, False)
         store(13)
-        read(14, 6)
+        read(14, 0)
         gate_out(14, False)
         store(14)
-        read(15, 7)
+        read(15, 2)
         gate_out(15, False)
         store(15)

@@ -15,20 +15,25 @@ FP8X4 = mybir.dt.float8_e4m3fn_x4
 FP4X4 = mybir.dt.float4_e2m1fn_x4
 MULT = mybir.AluOpType.mult
 ADD = mybir.AluOpType.add
-COPY = mybir.ActivationFunctionType.Copy
 
 P = 128
 PACK = 4
 K_PASS = P * PACK
+QUADRANT = 32
+BANKS = 8
 T_PASSES = T // K_PASS
-D_PASSES = D // K_PASS
-E_TILES = E // P
+HALVES = D // K_PASS
 R_TILES = R // P
 CHUNK = 4
-HALF = E // 2
-WARM_PASSES = 36
-SINGLE = [0,2,3,4,5,6,7]
-SCALE_RUNS = [(0, 3), (3, 8)]
+SIDE = E // 2
+RUN = 4
+WARM_PASSES = 22
+FIRST_TURNS = 10
+COPIED_TILES = 8
+PAIR_STORES = (3, 4)
+SPLIT_BUFS = 12
+GROUPED_BUFS = 4
+RESULT_BUFS = 5
 
 
 def tile_memory_write_read_s4_kernel(
@@ -36,8 +41,7 @@ def tile_memory_write_read_s4_kernel(
 ):
     nc = tc.nc
     with ExitStack() as ctx:
-        keep = ctx.enter_context(tc.tile_pool(name="keep", bufs=1))
-        ring = ctx.enter_context(tc.tile_pool(name="ring", bufs=4))
+        sbuf = ctx.enter_context(tc.tile_pool(name="sbuf", bufs=1))
         psum = ctx.enter_context(tc.psum_pool(name="psum", bufs=1))
         ctx.enter_context(tc.manual_schedule())
 
@@ -45,438 +49,339 @@ def tile_memory_write_read_s4_kernel(
             return psum.tile(shape, F32, name=f"bank{b}", tag=f"bank{b}")
 
         def kept(name, shape, dtype):
-            return keep.tile(shape, dtype, name=name, tag=name, align_bytes=64)
+            return sbuf.tile(shape, dtype, name=name, tag=name, align_bytes=64)
 
-        ident = kept("ident", [P, P], F32)
-        make_identity(nc, ident[:])
+        def rotating(tag, shape, dtype, bufs):
+            return sbuf.tile(shape, dtype, name=tag, tag=tag, bufs=bufs, align_bytes=64)
 
-        def scale_plane(name, passes, width):
-            plane = kept(name, [P, passes, width], U8)
-            nc.vector.memset(plane[:].bitcast(I32), 0)
-            return plane
-
-        v_planes, k_planes, v_scale, k_scale = {}, {}, {}, {}
-        warm = kept("warm", [P, K_PASS], BF16)
-        warm_codes = kept("warm_codes", [P, P], U32)
-        warm_scale = kept("warm_scale", [P, P], U8)
-        for g0, g1 in SCALE_RUNS:
-            v_planes[g0] = scale_plane(f"v_scale{g0}", g1 - g0, E)
-            if g0 == 0:
-                nc.vector.memset(warm[:], 1.0)
-            else:
-                nc.vector.quantize_mx(out=warm_codes[:].bitcast(FP8X4), scales=warm_scale[:], in_=warm[:])
-            k_planes[g0] = scale_plane(f"k_scale{g0}", g1 - g0, D)
-            for g in range(g0, g1):
-                v_scale[g] = v_planes[g0][:, g - g0, :]
-                k_scale[g] = k_planes[g0][:, g - g0, :]
-
-        warm_out = bank(7, [P, P])
-        for n in range(WARM_PASSES):
-            nc.tensor.matmul_mx(
-                out=warm_out[:],
-                lhsT=warm_codes[:].bitcast(FP8X4),
-                lhsT_scale=warm_scale[:],
-                rhs=warm_codes[:].bitcast(FP8X4),
-                rhs_scale=warm_scale[:],
-                start=True,
-                stop=True,
-            )
-
-        def load_scale_run(n):
-            g0, g1 = SCALE_RUNS[n]
-            load_scales(v_planes[g0], values_scales[g0:g1])
-            load_scales(k_planes[g0], keys_scales[g0:g1])
-
-        def load_scales(plane, rows):
-            by_row = rows.rearrange("g (q r) n -> r q g n", r=4)
-            for r in range(4):
-                nc.sync.dma_start(out=plane[r:P:32, :, :].bitcast(I32), in_=by_row[r].bitcast(I32))
-
-        v_words, k_words = {}, {}
-
-        def load_words(name, into, words, g0, g1):
-            w = kept(f"{name}{g0}", [P, g1 - g0, words.shape[2]], U8)
-            nc.sync.dma_start(out=w[:].bitcast(I32), in_=words[g0:g1].rearrange("g p n -> p g n").bitcast(I32))
-            for g in range(g0, g1):
-                into[name, g] = w[:, g - g0, :]
-
-        def load_first_words(g0, g1):
-            load_words("v", v_words, values_words, g0, g1)
-            load_words("k", k_words, keys_words, g0, g1)
-
-        retain_sb = kept("retain_sb", [P, D_PASSES, PACK], BF16)
-        old_sb = [kept(f"old_sb{h}", [P, PACK, E], BF16) for h in range(D_PASSES)]
+        k_planes = [kept(f"k_planes{n}", [P, RUN, D], U8) for n in range(T_PASSES // RUN)]
+        v_planes = [kept(f"v_planes{n}", [P, RUN, E], U8) for n in range(T_PASSES // RUN)]
+        k_words = [kept(f"k_words{g}", [P, 2 * D], U8) for g in range(T_PASSES)]
+        v_words = [kept(f"v_words{g}", [P, 2 * E], U8) for g in range(T_PASSES)]
+        k_sorted = {(g, h): kept(f"k_sorted{g}{h}", [P, PACK, 2 * P], U8) for g in range(T_PASSES) for h in range(HALVES)}
+        retain_rows = kept("retain_rows", [P, HALVES, P], BF16)
+        retain_sorted = kept("retain_sorted", [P, HALVES, PACK, QUADRANT], BF16)
+        retain_sb = kept("retain_sb", [P, HALVES, PACK, QUADRANT], BF16)
+        old_sb = [kept(f"old_sb{h}", [P, PACK, E], BF16) for h in range(HALVES)]
+        memory_slots = [kept(f"memory_slots{h}", [P, PACK, E], BF16) for h in range(HALVES)]
+        memory = [kept(f"memory{h}", [P, E, PACK], BF16) for h in range(HALVES)]
+        m_codes = [kept(f"m_codes{h}", [P, E], U32) for h in range(HALVES)]
+        m_scales = [kept(f"m_scales{h}", [P, E], U8) for h in range(HALVES)]
         query_sb = [kept(f"query_sb{c}", [P, 2, D], BF16) for c in range(R_TILES // 2)]
-        gate_sb = [kept(f"gate_sb{c}", [P, CHUNK, E], BF16) for c in range(R_TILES // CHUNK)]
-        old_rows = old.rearrange("(h p t) e -> h p t e", p=P, t=PACK)
-        query_rows = query.rearrange("(c p j) d -> c p j d", p=P, j=CHUNK)
-        gate_rows = gate.rearrange("(c p j) e -> c p j e", p=P, j=CHUNK)
-        out_rows = out.rearrange("(c p j) e -> c p j e", p=P, j=CHUNK)
+        q_codes = [kept(f"q_codes{c}", [P, 2, HALVES, P], U32) for c in range(R_TILES // 2)]
+        q_scales = [kept(f"q_scales{c}", [P, 2, HALVES, P], U8) for c in range(R_TILES // 2)]
+        gate_sb = [kept(f"gate_sb{n}", [P, CHUNK, E], BF16) for n in range(R_TILES // CHUNK)]
+        ident = kept("ident", [P, P], F32)
+        ones = kept("ones", [P, K_PASS], BF16)
+        ones_codes = kept("ones_codes", [P, P], U32)
+        ones_scales = kept("ones_scales", [P, P], U8)
+        k_scales, write, q_words, q_turned, grouped, read_sums, result = {}, {}, {}, {}, {}, {}, {}
 
-        def load_old(h):
-            nc.sync.dma_start(out=old_sb[h][:], in_=old_rows[h])
+        query_rows = query.rearrange("(n p j) d -> n p j d", p=P, j=CHUNK)
+        gate_rows = gate.rearrange("(n p j) e -> n p j e", p=P, j=CHUNK)
+        out_rows = out.rearrange("(n p j) e -> n p j e", p=P, j=CHUNK)
+
+        def zero_planes(n):
+            nc.vector.memset(k_planes[n][:].bitcast(I32), 0)
+            nc.vector.memset(v_planes[n][:].bitcast(I32), 0)
+
+        def warm_up():
+            dummy = bank(BANKS - 1, [P, P])
+            for n in range(WARM_PASSES):
+                nc.tensor.matmul_mx(
+                    out=dummy[:],
+                    lhsT=ones_codes[:].bitcast(FP8X4),
+                    lhsT_scale=ones_scales[:],
+                    rhs=ones_codes[:].bitcast(FP8X4),
+                    rhs_scale=ones_scales[:],
+                    start=True,
+                    stop=True,
+                )
+
+        def load_words(g):
+            nc.sync.dma_start(out=k_words[g][:].bitcast(I32), in_=keys_words[g].bitcast(I32))
+            nc.sync.dma_start(out=v_words[g][:].bitcast(I32), in_=values_words[g].bitcast(I32))
+
+        def load_scales(n):
+            for planes, scales in ((k_planes[n], keys_scales), (v_planes[n], values_scales)):
+                by_row = scales[RUN * n : RUN * (n + 1)].rearrange("g (q r) n -> r q g n", r=4)
+                for r in range(4):
+                    nc.sync.dma_start(out=planes[r:P:QUADRANT, :, :].bitcast(I32), in_=by_row[r].bitcast(I32))
+
+        def load_retain():
+            rows = retain.rearrange("(h q c) -> q h c", h=HALVES, c=P)
+            nc.sync.dma_start(out=retain_rows[0:P:QUADRANT, :, :], in_=rows)
+
+        def load_old_first_half():
+            rows = old[0:K_PASS, :].rearrange("(a t i) e -> i a t e", t=PACK, i=PACK)
+            for i in range(PACK):
+                nc.sync.dma_start(out=old_sb[0][i:P:PACK, :, :], in_=rows[i])
+
+        def load_old_second_half():
+            nc.sync.dma_start(out=old_sb[1][:], in_=old[K_PASS:D, :].rearrange("(p t) e -> p t e", t=PACK))
 
         def load_query(c):
             nc.sync.dma_start(out=query_sb[c][:], in_=query_rows[c // 2][:, 2 * (c % 2) : 2 * (c % 2) + 2, :])
 
-        def load_gate(c):
-            nc.sync.dma_start(out=gate_sb[c][:], in_=gate_rows[c])
+        def load_gate(n):
+            nc.sync.dma_start(out=gate_sb[n][:], in_=gate_rows[n])
 
-        def load_retain():
-            nc.sync.dma_start(out=retain_sb[:], in_=retain.rearrange("(h p t) -> p h t", p=P, t=PACK))
-
-        retained = [kept(f"retained{h}", [P, E, PACK], F32) for h in range(D_PASSES)]
-        memory = [kept(f"memory{h}", [P, E, PACK], BF16) for h in range(D_PASSES)]
-        m_codes = [kept(f"m_codes{h}", [P, E], U32) for h in range(D_PASSES)]
-        m_scale = [kept(f"m_scale{h}", [P, E], U8) for h in range(D_PASSES)]
-        q_codes = [kept(f"q_codes{i}", [P, 2 * D_PASSES * P], U32) for i in range(R_TILES // 2)]
-        q_scale = [kept(f"q_scale{i}", [P, 2 * D_PASSES * P], U8) for i in range(R_TILES // 2)]
-        write_t, turned, split, q_turned, grouped, result, acc, sums = {}, {}, {}, {}, {}, {}, {}, {}
-
-        def retain_old(h):
-            nc.vector.tensor_tensor(
-                out=retained[h][:],
-                in0=old_sb[h][:].rearrange("p t e -> p e t"),
-                in1=retain_sb[:, h, :].unsqueeze(1).to_broadcast([P, E, PACK]),
-                op=MULT,
+        def sort_words_by_runs(g):
+            nc.vector.tensor_copy(
+                out=k_sorted[g, 0][:].bitcast(I32).rearrange("k t (a w) -> k t a w", w=2),
+                in_=k_words[g][:, 0:D].bitcast(I32).rearrange("k (a t w) -> k t a w", t=PACK, w=2),
             )
 
-        def write_pass(h, j, g, b):
+        def sort_words_by_columns(g):
+            nc.vector.tensor_copy(
+                out=k_sorted[g, 1][:].rearrange("k t (p b) -> k t p b", b=2),
+                in_=k_words[g][:, D : 2 * D].rearrange("k (p t b) -> k t p b", t=PACK, b=2),
+            )
+
+        def sort_key_scales(g0, g1):
+            rows = k_planes[g0 // RUN][:, g0 % RUN : g0 % RUN + g1 - g0, :]
+            by_slot = [kept(f"k_scales{g0}{h}", [P, g1 - g0, PACK, P], U8) for h in range(HALVES)]
+            nc.vector.tensor_copy(
+                out=by_slot[0][:].bitcast(I32),
+                in_=rows[:, :, 0:K_PASS].bitcast(I32).rearrange("k g (a t) -> k g t a", t=PACK),
+            )
+            nc.vector.tensor_copy(out=by_slot[1][:], in_=rows[:, :, K_PASS:D].rearrange("k g (p t) -> k g t p", t=PACK))
+            for g in range(g0, g1):
+                for h in range(HALVES):
+                    k_scales[g, h] = by_slot[h][:, g - g0, :, :]
+
+        def sort_retain():
+            nc.vector.tensor_copy(
+                out=retain_sorted[:, 0, :, :].rearrange("q t (a i) -> q t a i", i=PACK),
+                in_=retain_rows[:, 0, :].rearrange("q (a t i) -> q t a i", t=PACK, i=PACK),
+            )
+            nc.vector.tensor_copy(
+                out=retain_sorted[:, 1, :, :], in_=retain_rows[:, 1, :].rearrange("q (c t) -> q t c", t=PACK)
+            )
+
+        def turn_retain():
+            nc.vector.transpose(
+                out=retain_sb[:].rearrange("p h t c -> p (h t c)"),
+                in_=retain_sorted[:].rearrange("q h t c -> q (h t c)"),
+            )
+
+        def write_pass(h, t, g):
             if g == 0:
-                acc[h, j] = bank(b, [P, K_PASS])
+                write[h, t] = bank(PACK * h + t, [P, E])
             nc.tensor.matmul_mx(
-                out=acc[h, j][:],
-                lhsT=v_words["v", g][:, 2 * P * j : 2 * P * (j + 1)].bitcast(FP4X4),
-                lhsT_scale=v_scale[g][:, P * j : P * (j + 1)],
-                rhs=k_words["k", g][:, 2 * K_PASS * h : 2 * K_PASS * (h + 1)].bitcast(FP4X4),
-                rhs_scale=k_scale[g][:, K_PASS * h : K_PASS * (h + 1)],
+                out=write[h, t][:],
+                lhsT=k_sorted[g, h][:, t, :].bitcast(FP4X4),
+                lhsT_scale=k_scales[g, h][:, t, :],
+                rhs=v_words[g][:].bitcast(FP4X4),
+                rhs_scale=v_planes[g // RUN][:, g % RUN, :],
                 start=(g == 0),
                 stop=(g == T_PASSES - 1),
             )
 
-        def write_group(h, j, b):
-            for g in range(T_PASSES):
-                write_pass(h, j, g, b)
-
-        def write_out(h, j, on_vector=False):
-            w = ring.tile([P, PACK, P], F32, name=f"write_t{h}{j}", tag="write_t", bufs=6)
-            copy = nc.vector.tensor_copy if on_vector else nc.scalar.copy
-            copy(out=w[:], in_=acc[h, j][:].rearrange("e (p t) -> e t p", t=PACK))
-            write_t[h, j] = w
-
-        def turn_write(h, j, b):
-            turned[h, j] = bank(b, [P, PACK, P])
-            for t in range(PACK):
-                nc.tensor.transpose(turned[h, j][:, t, :], write_t[h, j][:, t, :], ident[:])
-
-        def add_old(h, j):
-            cols = slice(P * j, P * (j + 1))
-            nc.vector.tensor_tensor(
-                out=memory[h][:, cols, :],
-                in0=turned[h, j][:].rearrange("p t e -> p e t"),
-                in1=retained[h][:, cols, :],
-                op=ADD,
+        def add_old(h, t):
+            nc.vector.scalar_tensor_tensor(
+                out=memory_slots[h][:, t, :],
+                in0=old_sb[h][:, t, :],
+                scalar=retain_sb[:, h, t, 0:1],
+                in1=write[h, t][:],
+                op0=MULT,
+                op1=ADD,
             )
+
+        def interleave_memory(h, side):
+            cols = slice(SIDE * side, SIDE * (side + 1))
+            nc.vector.tensor_copy(out=memory[h][:, cols, :], in_=memory_slots[h][:, :, cols].rearrange("p t e -> p e t"))
 
         def quantize_memory(h, side):
-            cols = slice(HALF * side, HALF * (side + 1))
+            cols = slice(SIDE * side, SIDE * (side + 1))
             nc.vector.quantize_mx(
                 out=m_codes[h][:, cols].bitcast(FP8X4),
-                scales=m_scale[h][:, cols],
-                in_=memory[h][:, cols, :].rearrange("p e t -> p (e t)"),
+                scales=m_scales[h][:, cols],
+                in_=memory[h][:, cols, :].rearrange("r e t -> r (e t)"),
             )
 
-        def split_query(c, on_vector):
-            s = keep.tile([P, 2 * D_PASSES, 2, P], F32, name=f"split{c}", tag="split", bufs=6, align_bytes=64)
-            words = query_sb[c][:].rearrange("r j d -> r (j d)").bitcast(F32)
-            copy = nc.vector.tensor_copy if on_vector else nc.scalar.copy
-            copy(out=s[:], in_=words.rearrange("r (n p u) -> r n u p", p=P, u=2))
-            split[c] = s
+        def split_query(i):
+            row = query_sb[i // 2][:, i % 2, :]
+            pairs = rotating("pairs", [P, 2, K_PASS // 16, PACK, 2], BF16, SPLIT_BUFS)
+            nc.scalar.copy(out=pairs[:], in_=row[:, 0:K_PASS].rearrange("r (a u o i) -> r u a i o", u=2, o=2, i=PACK))
+            q_words[i, 0] = pairs[:].rearrange("r u a i o -> r u (a i o)").bitcast(F32)
+            q_words[i, 1] = row[:, K_PASS:D].bitcast(F32).rearrange("r (p u) -> r u p", u=2)
+            if i < COPIED_TILES:
+                words = rotating("words", [P, 2, P], F32, COPIED_TILES)
+                nc.scalar.copy(out=words[:], in_=q_words[i, 1])
+                q_words[i, 1] = words[:]
 
         def turn_query(i, b):
-            q_turned[i] = bank(b, [P, D_PASSES, 2, P])
-            for g in range(D_PASSES):
+            q_turned[i] = bank(b, [P, HALVES, 2, P])
+            for h in range(HALVES):
                 for u in range(2):
-                    if i // 2 in split:
-                        src = split[i // 2][:, D_PASSES * (i % 2) + g, u, :]
-                    else:
-                        src = query_sb[i // 2][:, i % 2, :].bitcast(F32)[:, 2 * P * g + u : 2 * P * (g + 1) : 2]
-                    nc.tensor.transpose(q_turned[i][:, g, u, :], src, ident[:])
+                    nc.tensor.transpose(q_turned[i][:, h, u, :], q_words[i, h][:, u, :], ident[:])
 
-        def query_out(i, on_vector):
-            if i // 2 not in grouped:
-                grouped[i // 2] = ring.tile([P, 2, D], BF16, name=f"grouped{i}", tag="grouped", bufs=4, align_bytes=64)
-            copy = nc.vector.tensor_copy if on_vector else nc.scalar.copy
-            copy(
-                out=grouped[i // 2][:, i % 2, :].bitcast(F32).rearrange("p (g r u) -> p g r u", g=D_PASSES, u=2),
-                in_=q_turned[i][:].rearrange("p g u r -> p g r u"),
+        def query_out(i):
+            if i % 2 == 0:
+                grouped[i // 2] = rotating("grouped", [P, 2, D], BF16, GROUPED_BUFS)
+            nc.scalar.copy(
+                out=grouped[i // 2][:, i % 2, :].bitcast(F32).rearrange("p (h r u) -> p h r u", h=HALVES, u=2),
+                in_=q_turned[i][:].rearrange("p h u r -> p h r u"),
             )
 
         def quantize_query(c):
             nc.vector.quantize_mx(
-                out=q_codes[c][:].bitcast(FP8X4), scales=q_scale[c][:], in_=grouped[c][:].rearrange("p j d -> p (j d)")
+                out=q_codes[c][:].rearrange("p j h r -> p (j h r)").bitcast(FP8X4),
+                scales=q_scales[c][:].rearrange("p j h r -> p (j h r)"),
+                in_=grouped[c][:].rearrange("p j d -> p (j d)"),
             )
 
         def read(i, b):
-            acc[i] = bank(b, [P, E])
-            for g in range(D_PASSES):
-                n = D_PASSES * (i % 2) + g
-                rows = slice(P * n, P * (n + 1))
+            read_sums[i] = bank(b, [P, E])
+            for h in range(HALVES):
                 nc.tensor.matmul_mx(
-                    out=acc[i][:],
-                    lhsT=q_codes[i // 2][:, rows].bitcast(FP8X4),
-                    lhsT_scale=q_scale[i // 2][:, rows],
-                    rhs=m_codes[g][:].bitcast(FP8X4),
-                    rhs_scale=m_scale[g][:],
-                    start=(g == 0),
-                    stop=(g == D_PASSES - 1),
+                    out=read_sums[i][:],
+                    lhsT=q_codes[i // 2][:, i % 2, h, :].bitcast(FP8X4),
+                    lhsT_scale=q_scales[i // 2][:, i % 2, h, :],
+                    rhs=m_codes[h][:].bitcast(FP8X4),
+                    rhs_scale=m_scales[h][:],
+                    start=(h == 0),
+                    stop=(h == HALVES - 1),
                 )
 
-        def read_out(i):
-            sums[i] = ring.tile([P, E], F32, name="sums", tag="sums", bufs=2)
-            nc.scalar.copy(out=sums[i][:], in_=acc[i][:])
-
-        def gate_out(i, on_gpsimd):
-            c, j = divmod(i, CHUNK)
-            if i // 2 not in result:
-                result[i // 2] = ring.tile([P, 2, E], F32, name=f"result{i}", tag="result", bufs=3)
-            if on_gpsimd:
-                nc.gpsimd.tensor_tensor(out=result[i // 2][:, i % 2, :], in0=sums[i][:], in1=gate_sb[c][:, j, :], op=MULT)
-            else:
-                nc.vector.tensor_tensor(out=result[i // 2][:, i % 2, :], in0=acc[i][:], in1=gate_sb[c][:, j, :], op=MULT)
-
-        def store(i):
-            c, j = divmod(i, CHUNK)
-            if i // 2 in SINGLE:
-                nc.sync.dma_start(out=out_rows[c][:, j, :], in_=result[i // 2][:, i % 2, :])
+        def gate_and_store(i):
+            n, j = divmod(i, CHUNK)
+            if i % 2 == 0:
+                result[i // 2] = rotating("result", [P, 2, E], F32, RESULT_BUFS)
+            pair = result[i // 2]
+            nc.vector.tensor_tensor(out=pair[:, i % 2, :], in0=read_sums[i][:], in1=gate_sb[n][:, j, :], op=MULT)
+            if i // 2 not in PAIR_STORES:
+                nc.sync.dma_start(out=out_rows[n][:, j, :], in_=pair[:, i % 2, :])
             elif i % 2 == 1:
-                nc.sync.dma_start(out=out_rows[c][:, j - 1 : j + 1, :], in_=result[i // 2][:])
+                nc.sync.dma_start(out=out_rows[n][:, j - 1 : j + 1, :], in_=pair[:])
 
+        zero_planes(0)
+        nc.vector.memset(ones[:], 1.0)
+        nc.vector.memset(retain_rows[:], 0.0)
+        nc.vector.quantize_mx(out=ones_codes[:].bitcast(FP8X4), scales=ones_scales[:], in_=ones[:])
+        zero_planes(1)
+        warm_up()
 
-        def read_half(c, side, b):
-            cols = slice(HALF * side, HALF * (side + 1))
-            acc[c, side, "read"] = bank(b, [P, 2, HALF])
-            for j in range(2):
-                for g in range(D_PASSES):
-                    n = D_PASSES * j + g
-                    rows = slice(P * n, P * (n + 1))
-                    nc.tensor.matmul_mx(
-                        out=acc[c, side, "read"][:, j, :],
-                        lhsT=q_codes[c][:, rows].bitcast(FP8X4),
-                        lhsT_scale=q_scale[c][:, rows],
-                        rhs=m_codes[g][:, cols].bitcast(FP8X4),
-                        rhs_scale=m_scale[g][:, cols],
-                        start=(g == 0),
-                        stop=(g == D_PASSES - 1),
-                    )
-
-        def gate_half(c, side):
-            cols = slice(HALF * side, HALF * (side + 1))
-            rows = slice(2 * (c % 2), 2 * (c % 2) + 2)
-            r = ring.tile([P, 2, HALF], F32, name=f"result{c}{side}", tag="half", bufs=6)
-            nc.vector.tensor_tensor(out=r[:], in0=acc[c, side, "read"][:], in1=gate_sb[c // 2][:, rows, cols], op=MULT)
-            result[c, side, "half"] = r
-
-        def store_half(c, side):
-            cols = slice(HALF * side, HALF * (side + 1))
-            rows = slice(2 * (c % 2), 2 * (c % 2) + 2)
-            nc.sync.dma_start(out=out_rows[c // 2][:, rows, cols], in_=result[c, side, "half"][:])
-
-        load_first_words(0, 2)
-        load_scale_run(0)
-        load_scale_run(1)
-        load_first_words(2, 3)
+        load_words(0)
+        load_scales(0)
+        for g in range(1, RUN):
+            load_words(g)
         load_retain()
-        load_first_words(3, 4)
-        load_first_words(4, 6)
-        load_old(0)
-        load_first_words(6, 8)
-        load_old(1)
-        load_gate(0)
+        load_scales(1)
         load_query(0)
+        for g in range(RUN, T_PASSES):
+            load_words(g)
         load_query(1)
+        load_old_first_half()
         load_query(2)
         load_query(3)
-        load_query(4)
+        load_old_second_half()
+        for c in (4, 5, 6):
+            load_query(c)
+        load_gate(0)
         load_gate(1)
-        load_query(5)
-        load_gate(2)
-        load_query(6)
-        load_gate(3)
         load_query(7)
-        write_pass(0, 0, 0, 0)
-        write_pass(1, 0, 0, 1)
-        write_pass(0, 1, 0, 2)
-        write_pass(1, 1, 0, 3)
-        write_pass(0, 2, 0, 4)
-        write_pass(1, 2, 0, 5)
-        write_pass(0, 0, 1, 0)
-        write_pass(1, 0, 1, 1)
-        write_pass(0, 1, 1, 2)
-        write_pass(1, 1, 1, 3)
-        write_pass(0, 2, 1, 4)
-        write_pass(1, 2, 1, 5)
-        write_pass(0, 0, 2, 0)
-        write_pass(1, 0, 2, 1)
-        write_pass(0, 1, 2, 2)
-        write_pass(1, 1, 2, 3)
-        write_pass(0, 2, 2, 4)
-        write_pass(1, 2, 2, 5)
-        write_pass(0, 0, 3, 0)
-        write_pass(1, 0, 3, 1)
-        write_pass(0, 1, 3, 2)
-        write_pass(1, 1, 3, 3)
-        write_pass(0, 2, 3, 4)
-        write_pass(1, 2, 3, 5)
-        retain_old(0)
-        write_pass(0, 0, 4, 0)
-        write_pass(1, 0, 4, 1)
-        write_pass(0, 1, 4, 2)
-        write_pass(1, 1, 4, 3)
-        write_pass(0, 2, 4, 4)
-        write_pass(1, 2, 4, 5)
-        write_pass(0, 0, 5, 0)
-        write_pass(1, 0, 5, 1)
-        write_pass(0, 1, 5, 2)
-        write_pass(1, 1, 5, 3)
-        write_pass(0, 2, 5, 4)
-        write_pass(1, 2, 5, 5)
-        retain_old(1)
-        write_pass(0, 0, 6, 0)
-        write_pass(0, 0, 7, 0)
-        write_out(0, 0, False)
-        write_pass(1, 0, 6, 0)
-        write_pass(1, 0, 7, 0)
-        write_out(1, 0, False)
-        write_pass(0, 1, 6, 0)
-        write_pass(0, 1, 7, 0)
-        write_out(0, 1, False)
-        write_pass(1, 1, 6, 0)
-        write_pass(1, 1, 7, 0)
-        split_query(0, False)
-        write_pass(0, 2, 6, 0)
-        write_pass(0, 2, 7, 0)
-        write_out(1, 1, True)
-        write_pass(1, 2, 6, 0)
-        write_pass(1, 2, 7, 0)
-        split_query(1, True)
-        write_out(0, 2, False)
-        turn_write(0, 0, 6)
-        turn_write(1, 0, 7)
-        add_old(0, 0)
-        write_out(1, 2, False)
-        turn_write(0, 1, 0)
-        turn_query(0, 1)
-        add_old(1, 0)
-        split_query(2, False)
-        turn_query(1, 2)
-        query_out(0, True)
-        turn_query(2, 3)
-        turn_write(1, 1, 4)
-        query_out(2, False)
-        query_out(1, True)
-        turn_write(0, 2, 6)
-        turn_query(3, 5)
-        split_query(3, True)
-        turn_query(4, 7)
-        query_out(3, False)
-        turn_write(1, 2, 1)
+        load_gate(2)
+        load_gate(3)
+
+        for i in range(FIRST_TURNS):
+            split_query(i)
+
+        for g in range(RUN):
+            sort_words_by_runs(g)
+            sort_words_by_columns(g)
+            if g == 0:
+                sort_key_scales(0, 1)
+                sort_key_scales(1, RUN)
+            for h in range(HALVES):
+                for t in range(PACK):
+                    write_pass(h, t, g)
+        nc.vector.memset(ident[:], 0.0)
+        make_identity(nc, ident[:], nomemset=True)
+        sort_key_scales(RUN, T_PASSES)
+
+        for g in (4, 5):
+            sort_words_by_runs(g)
+            for t in range(PACK):
+                write_pass(0, t, g)
+        sort_words_by_columns(4)
+        sort_retain()
+        sort_words_by_runs(6)
+        turn_retain()
+        sort_words_by_runs(7)
+        for g in (5, 6, 7):
+            sort_words_by_columns(g)
+        for t in range(PACK):
+            write_pass(0, t, 6)
+            write_pass(0, t, 7)
+            add_old(0, t)
+        interleave_memory(0, 0)
+        interleave_memory(0, 1)
+
+        for t in range(PACK):
+            for g in range(RUN, T_PASSES):
+                write_pass(1, t, g)
+            add_old(1, t)
+            if t % 2 == 1:
+                quantize_memory(0, t // 2)
+        interleave_memory(1, 0)
+        interleave_memory(1, 1)
+
+        def turns(first, banks):
+            for n, b in enumerate(banks):
+                turn_query(first + n, b)
+
+        def reads(first, banks):
+            for n, b in enumerate(banks):
+                read(first + n, b)
+
+        def gates(i0, i1):
+            for i in range(i0, i1):
+                gate_and_store(i)
+
+        def split_pair(c):
+            split_query(2 * c)
+            split_query(2 * c + 1)
+
+        def pair_out(c):
+            query_out(2 * c)
+            query_out(2 * c + 1)
+
+        turns(0, range(BANKS))
+        pair_out(0)
+        turns(8, (0, 1))
         quantize_query(0)
-        query_out(4, False)
-        turn_query(5, 3)
-        quantize_query(1)
-        turn_query(6, 2)
-        query_out(5, False)
-        turn_query(7, 5)
-        add_old(0, 1)
-        query_out(6, False)
-        quantize_query(2)
-        query_out(7, False)
-        add_old(1, 1)
-        split_query(4, False)
-        quantize_memory(0, 0)
         quantize_memory(1, 0)
-        write_group(0, 3, 7)
-        add_old(0, 2)
-        split_query(5, False)
-        quantize_query(3)
-        write_out(0, 3, True)
-        split_query(6, False)
-        add_old(1, 2)
-        write_group(1, 3, 3)
-        write_out(1, 3, False)
-        read_half(0, 0, 0)
-        gate_half(0, 0)
-        store_half(0, 0)
-        read_half(2, 0, 2)
-        split_query(7, False)
-        gate_half(2, 0)
-        store_half(2, 0)
-        turn_write(0, 3, 5)
-        turn_write(1, 3, 4)
-        add_old(0, 3)
-        turn_query(8, 6)
-        turn_query(9, 7)
-        query_out(8, False)
-        add_old(1, 3)
-        turn_query(10, 1)
-        query_out(9, False)
-        turn_query(11, 3)
-        quantize_memory(0, 1)
         quantize_memory(1, 1)
-        turn_query(12, 0)
-        query_out(10, False)
+        for c in (1, 2):
+            pair_out(c)
+            quantize_query(c)
+        pair_out(3)
+        reads(0, range(2, BANKS))
+        gates(0, 2)
+        quantize_query(3)
+
+        split_pair(5)
+        pair_out(4)
+        turns(10, (2, 3))
+        gates(2, 4)
         quantize_query(4)
-        read_half(1, 0, 2)
-        query_out(11, False)
-        gate_half(1, 0)
-        store_half(1, 0)
-        read(6, 5)
-        query_out(12, False)
-        gate_out(6, False)
-        store(6)
-        read_half(2, 1, 6)
-        gate_half(2, 1)
-        store_half(2, 1)
-        read_half(0, 1, 4)
-        gate_half(0, 1)
-        store_half(0, 1)
-        read(7, 7)
-        gate_out(7, False)
-        store(7)
-        read(8, 1)
-        gate_out(8, False)
-        store(8)
-        read_half(1, 1, 3)
+        reads(6, (0, 1, 4, 5))
+        gates(4, 7)
+
+        split_pair(6)
+        pair_out(5)
+        split_pair(7)
         quantize_query(5)
-        read(9, 2)
-        turn_query(13, 0)
-        gate_half(1, 1)
-        store_half(1, 1)
-        turn_query(14, 5)
-        query_out(13, False)
-        gate_out(9, False)
-        store(9)
-        turn_query(15, 6)
-        query_out(14, False)
+        turns(12, (6, 7, 2, 3))
+        gates(7, 10)
+        reads(10, (0, 1))
+        pair_out(6)
         quantize_query(6)
-        read(10, 4)
-        query_out(15, False)
-        gate_out(10, False)
-        store(10)
-        read(11, 7)
-        gate_out(11, False)
-        store(11)
-        read(12, 1)
+        gates(10, 12)
+        reads(12, (4, 5))
+        pair_out(7)
         quantize_query(7)
-        read(13, 3)
-        gate_out(12, False)
-        store(12)
-        gate_out(13, False)
-        store(13)
-        read(14, 0)
-        gate_out(14, False)
-        store(14)
-        read(15, 2)
-        gate_out(15, False)
-        store(15)
+        reads(14, (6, 7))
+        gates(12, 16)

@@ -27,7 +27,6 @@ R_TILES = R // P
 CHUNK = 4
 SIDE = E // 2
 RUN = 4
-WARM_PASSES = 22
 FIRST_TURNS = 10
 COPIED_TILES = 8
 PAIR_STORES = (3, 4)
@@ -72,9 +71,6 @@ def tile_memory_write_read_s4_kernel(
         q_scales = [kept(f"q_scales{c}", [P, 2, HALVES, P], U8) for c in range(R_TILES // 2)]
         gate_sb = [kept(f"gate_sb{n}", [P, CHUNK, E], BF16) for n in range(R_TILES // CHUNK)]
         ident = kept("ident", [P, P], F32)
-        ones = kept("ones", [P, K_PASS], BF16)
-        ones_codes = kept("ones_codes", [P, P], U32)
-        ones_scales = kept("ones_scales", [P, P], U8)
         k_scales, write, q_words, q_turned, grouped, read_sums, result = {}, {}, {}, {}, {}, {}, {}
 
         query_rows = query.rearrange("(n p j) d -> n p j d", p=P, j=CHUNK)
@@ -84,19 +80,6 @@ def tile_memory_write_read_s4_kernel(
         def zero_planes(n):
             nc.vector.memset(k_planes[n][:].bitcast(I32), 0)
             nc.vector.memset(v_planes[n][:].bitcast(I32), 0)
-
-        def warm_up():
-            dummy = bank(BANKS - 1, [P, P])
-            for n in range(WARM_PASSES):
-                nc.tensor.matmul_mx(
-                    out=dummy[:],
-                    lhsT=ones_codes[:].bitcast(FP8X4),
-                    lhsT_scale=ones_scales[:],
-                    rhs=ones_codes[:].bitcast(FP8X4),
-                    rhs_scale=ones_scales[:],
-                    start=True,
-                    stop=True,
-                )
 
         def load_words(g):
             nc.sync.dma_start(out=k_words[g][:].bitcast(I32), in_=keys_words[g].bitcast(I32))
@@ -257,11 +240,8 @@ def tile_memory_write_read_s4_kernel(
                 nc.sync.dma_start(out=out_rows[n][:, j - 1 : j + 1, :], in_=pair[:])
 
         zero_planes(0)
-        nc.vector.memset(ones[:], 1.0)
         nc.vector.memset(retain_rows[:], 0.0)
-        nc.vector.quantize_mx(out=ones_codes[:].bitcast(FP8X4), scales=ones_scales[:], in_=ones[:])
         zero_planes(1)
-        warm_up()
 
         load_words(0)
         load_scales(0)

@@ -10,6 +10,7 @@ F32 = mybir.dt.float32
 BF16 = mybir.dt.bfloat16
 I32 = mybir.dt.int32
 U32 = mybir.dt.uint32
+U16 = mybir.dt.uint16
 U8 = mybir.dt.uint8
 FP8X4 = mybir.dt.float8_e4m3fn_x4
 FP4X4 = mybir.dt.float4_e2m1fn_x4
@@ -117,8 +118,8 @@ def tile_memory_write_read_s4_kernel(
 
         def sort_words_by_columns(g):
             nc.vector.tensor_copy(
-                out=k_sorted[g, 1][:].rearrange("k t (p b) -> k t p b", b=2),
-                in_=k_words[g][:, D : 2 * D].rearrange("k (p t b) -> k t p b", t=PACK, b=2),
+                out=k_sorted[g, 1][:].bitcast(U16),
+                in_=k_words[g][:, D : 2 * D].bitcast(U16).rearrange("k (p t) -> k t p", t=PACK),
             )
 
         def sort_key_scales(g0, g1):

@@ -28,6 +28,8 @@ R_TILES = R // P
 CHUNK = 4
 SIDE = E // 2
 RUN = 4
+SCALE_RUNS = ((0, 4), (4, 8))
+WARM_PASSES = 3
 FIRST_TURNS = 10
 COPIED_TILES = 8
 PAIR_STORES = (3, 4)
@@ -54,10 +56,10 @@ def tile_memory_write_read_s4_kernel(
         def rotating(tag, shape, dtype, bufs):
             return sbuf.tile(shape, dtype, name=tag, tag=tag, bufs=bufs, align_bytes=64)
 
-        k_planes = [kept(f"k_planes{n}", [P, RUN, D], U8) for n in range(T_PASSES // RUN)]
-        v_planes = [kept(f"v_planes{n}", [P, RUN, E], U8) for n in range(T_PASSES // RUN)]
-        k_words = [kept(f"k_words{g}", [P, 2 * D], U8) for g in range(T_PASSES)]
-        v_words = [kept(f"v_words{g}", [P, 2 * E], U8) for g in range(T_PASSES)]
+        k_planes = [kept(f"k_planes{g0}", [P, g1 - g0, D], U8) for g0, g1 in SCALE_RUNS]
+        v_planes = [kept(f"v_planes{g0}", [P, g1 - g0, E], U8) for g0, g1 in SCALE_RUNS]
+        place = {g: (n, g - g0) for n, (g0, g1) in enumerate(SCALE_RUNS) for g in range(g0, g1)}
+        k_words, v_words = {}, {}
         k_sorted = {(g, h): kept(f"k_sorted{g}{h}", [P, PACK, 2 * P], U8) for g in range(T_PASSES) for h in range(HALVES)}
         retain_rows = kept("retain_rows", [P, HALVES, P], BF16)
         retain_sorted = kept("retain_sorted", [P, HALVES, PACK, QUADRANT], BF16)
@@ -79,18 +81,37 @@ def tile_memory_write_read_s4_kernel(
         out_rows = out.rearrange("(n p j) e -> n p j e", p=P, j=CHUNK)
 
         def zero_planes(n):
-            nc.vector.memset(k_planes[n][:].bitcast(I32), 0)
             nc.vector.memset(v_planes[n][:].bitcast(I32), 0)
+            nc.vector.memset(k_planes[n][:].bitcast(I32), 0)
 
-        def load_words(g):
-            nc.sync.dma_start(out=k_words[g][:].bitcast(I32), in_=keys_words[g].bitcast(I32))
-            nc.sync.dma_start(out=v_words[g][:].bitcast(I32), in_=values_words[g].bitcast(I32))
+        def load_words(g0, g1):
+            for tiles, name, words in ((k_words, "k_words", keys_words), (v_words, "v_words", values_words)):
+                rows = kept(f"{name}{g0}", [P, g1 - g0, words.shape[2]], U8)
+                nc.sync.dma_start(out=rows[:].bitcast(I32), in_=words[g0:g1].rearrange("g p n -> p g n").bitcast(I32))
+                for g in range(g0, g1):
+                    tiles[g] = rows[:, g - g0, :]
+
+        def warm_up():
+            unread = bank(BANKS - 1, [P, E])
+            for n in range(WARM_PASSES):
+                nc.tensor.matmul_mx(
+                    out=unread[:],
+                    lhsT=k_sorted[0, 0][:, n, :].bitcast(FP4X4),
+                    lhsT_scale=k_planes[1][:, 0, 0:P],
+                    rhs=v_words[0].bitcast(FP4X4),
+                    rhs_scale=v_planes[1][:, 0, :],
+                    start=True,
+                    stop=True,
+                )
+
+        def load_scale_rows(planes, scales, n, rows):
+            by_row = scales[SCALE_RUNS[n][0] : SCALE_RUNS[n][1]].rearrange("g (q r) n -> r q g n", r=4)
+            for r in rows:
+                nc.sync.dma_start(out=planes[n][r:P:QUADRANT, :, :].bitcast(I32), in_=by_row[r].bitcast(I32))
 
         def load_scales(n):
-            for planes, scales in ((k_planes[n], keys_scales), (v_planes[n], values_scales)):
-                by_row = scales[RUN * n : RUN * (n + 1)].rearrange("g (q r) n -> r q g n", r=4)
-                for r in range(4):
-                    nc.sync.dma_start(out=planes[r:P:QUADRANT, :, :].bitcast(I32), in_=by_row[r].bitcast(I32))
+            load_scale_rows(k_planes, keys_scales, n, range(4))
+            load_scale_rows(v_planes, values_scales, n, range(4))
 
         def load_retain():
             rows = retain.rearrange("(h q c) -> q h c", h=HALVES, c=P)
@@ -123,7 +144,7 @@ def tile_memory_write_read_s4_kernel(
             )
 
         def sort_key_scales(g0, g1):
-            rows = k_planes[g0 // RUN][:, g0 % RUN : g0 % RUN + g1 - g0, :]
+            rows = k_planes[place[g0][0]][:, place[g0][1] : place[g0][1] + g1 - g0, :]
             by_slot = [kept(f"k_scales{g0}{h}", [P, g1 - g0, PACK, P], U8) for h in range(HALVES)]
             nc.vector.tensor_copy(
                 out=by_slot[0][:].bitcast(I32),
@@ -156,8 +177,8 @@ def tile_memory_write_read_s4_kernel(
                 out=write[h, t][:],
                 lhsT=k_sorted[g, h][:, t, :].bitcast(FP4X4),
                 lhsT_scale=k_scales[g, h][:, t, :],
-                rhs=v_words[g][:].bitcast(FP4X4),
-                rhs_scale=v_planes[g // RUN][:, g % RUN, :],
+                rhs=v_words[g].bitcast(FP4X4),
+                rhs_scale=v_planes[place[g][0]][:, place[g][1], :],
                 start=(g == 0),
                 stop=(g == T_PASSES - 1),
             )
@@ -244,33 +265,35 @@ def tile_memory_write_read_s4_kernel(
         nc.vector.memset(retain_rows[:], 0.0)
         zero_planes(1)
 
-        load_words(0)
-        load_scales(0)
-        for g in range(1, RUN):
-            load_words(g)
-        load_retain()
-        load_scales(1)
+        load_words(0, 1)
+        load_scale_rows(v_planes, values_scales, 0, range(1))
+        load_scale_rows(k_planes, keys_scales, 0, range(4))
+        load_scale_rows(v_planes, values_scales, 0, range(1, 4))
+        load_words(1, 2)
+        load_words(2, 4)
         load_query(0)
-        for g in range(RUN, T_PASSES):
-            load_words(g)
-        load_query(1)
+        sort_words_by_runs(0)
+        warm_up()
+        load_retain()
+        load_scale_rows(k_planes, keys_scales, 1, range(4))
+        load_words(4, 6)
+        load_scale_rows(v_planes, values_scales, 1, range(4))
+        load_words(6, 8)
         load_old_first_half()
+        load_query(1)
         load_query(2)
-        load_query(3)
         load_old_second_half()
-        for c in (4, 5, 6):
+        for c in (3, 4, 5, 6, 7):
             load_query(c)
-        load_gate(0)
-        load_gate(1)
-        load_query(7)
-        load_gate(2)
-        load_gate(3)
+        for n in range(4):
+            load_gate(n)
 
         for i in range(FIRST_TURNS):
             split_query(i)
 
         for g in range(RUN):
-            sort_words_by_runs(g)
+            if g > 0:
+                sort_words_by_runs(g)
             sort_words_by_columns(g)
             if g == 0:
                 sort_key_scales(0, 1)
@@ -304,8 +327,8 @@ def tile_memory_write_read_s4_kernel(
             for g in range(RUN, T_PASSES):
                 write_pass(1, t, g)
             add_old(1, t)
-            if t % 2 == 1:
-                quantize_memory(0, t // 2)
+            if t in (1, 2):
+                quantize_memory(0, t - 1)
         interleave_memory(1, 0)
         interleave_memory(1, 1)
 

@@ -21,19 +21,18 @@ P = 128
 PACK = 4
 K_PASS = P * PACK
 QUADRANT = 32
-BANKS = 8
 T_PASSES = T // K_PASS
 HALVES = D // K_PASS
 R_TILES = R // P
 CHUNK = 4
 SIDE = E // 2
-RUN = 4
+WHOLE = slice(0, E)
+SIDES = (slice(0, SIDE), slice(SIDE, E))
+WORD_LOADS = ((0, 1), (1, 2), (2, 4), (4, 6), (6, 8))
 SCALE_RUNS = ((0, 4), (4, 8))
-WARM_PASSES = 3
-FIRST_TURNS = 10
-COPIED_TILES = 8
 PAIR_STORES = (3, 4)
-SPLIT_BUFS = 12
+WARM_PASSES = 3
+SPLIT_BUFS = 6
 GROUPED_BUFS = 4
 RESULT_BUFS = 5
 
@@ -56,11 +55,8 @@ def tile_memory_write_read_s4_kernel(
         def rotating(tag, shape, dtype, bufs):
             return sbuf.tile(shape, dtype, name=tag, tag=tag, bufs=bufs, align_bytes=64)
 
-        k_planes = [kept(f"k_planes{g0}", [P, g1 - g0, D], U8) for g0, g1 in SCALE_RUNS]
-        v_planes = [kept(f"v_planes{g0}", [P, g1 - g0, E], U8) for g0, g1 in SCALE_RUNS]
-        place = {g: (n, g - g0) for n, (g0, g1) in enumerate(SCALE_RUNS) for g in range(g0, g1)}
-        k_words, v_words = {}, {}
-        k_sorted = {(g, h): kept(f"k_sorted{g}{h}", [P, PACK, 2 * P], U8) for g in range(T_PASSES) for h in range(HALVES)}
+        k_planes = {run: kept(f"k_planes{run[0]}", [P, run[1] - run[0], D], U8) for run in SCALE_RUNS}
+        v_planes = {run: kept(f"v_planes{run[0]}", [P, run[1] - run[0], E], U8) for run in SCALE_RUNS}
         retain_rows = kept("retain_rows", [P, HALVES, P], BF16)
         retain_sorted = kept("retain_sorted", [P, HALVES, PACK, QUADRANT], BF16)
         retain_sb = kept("retain_sb", [P, HALVES, PACK, QUADRANT], BF16)
@@ -74,56 +70,45 @@ def tile_memory_write_read_s4_kernel(
         q_scales = [kept(f"q_scales{c}", [P, 2, HALVES, P], U8) for c in range(R_TILES // 2)]
         gate_sb = [kept(f"gate_sb{n}", [P, CHUNK, E], BF16) for n in range(R_TILES // CHUNK)]
         ident = kept("ident", [P, P], F32)
-        k_scales, write, q_words, q_turned, grouped, read_sums, result = {}, {}, {}, {}, {}, {}, {}
+        k_words, v_words, k_sorted, k_scales = {}, {}, {}, {}
+        v_scales = {g: v_planes[run][:, g - run[0], :] for run in SCALE_RUNS for g in range(*run)}
+        write, q_words, q_turned, grouped, read_sums, result = {}, {}, {}, {}, {}, {}
 
         query_rows = query.rearrange("(n p j) d -> n p j d", p=P, j=CHUNK)
         gate_rows = gate.rearrange("(n p j) e -> n p j e", p=P, j=CHUNK)
         out_rows = out.rearrange("(n p j) e -> n p j e", p=P, j=CHUNK)
 
-        def zero_planes(n):
-            nc.vector.memset(v_planes[n][:].bitcast(I32), 0)
-            nc.vector.memset(k_planes[n][:].bitcast(I32), 0)
+        def zero_planes(run):
+            nc.vector.memset(v_planes[run][:].bitcast(I32), 0)
+            nc.vector.memset(k_planes[run][:].bitcast(I32), 0)
 
-        def load_words(g0, g1):
-            for tiles, name, words in ((k_words, "k_words", keys_words), (v_words, "v_words", values_words)):
-                rows = kept(f"{name}{g0}", [P, g1 - g0, words.shape[2]], U8)
-                nc.sync.dma_start(out=rows[:].bitcast(I32), in_=words[g0:g1].rearrange("g p n -> p g n").bitcast(I32))
-                for g in range(g0, g1):
-                    tiles[g] = rows[:, g - g0, :]
+        def load_values(span):
+            g0, g1 = span
+            words = kept(f"v_words{g0}", [P, g1 - g0, 2 * E], U8)
+            nc.sync.dma_start(out=words[:].bitcast(I32), in_=values_words[g0:g1].rearrange("g p n -> p g n").bitcast(I32))
+            for g in range(g0, g1):
+                v_words[g] = words[:, g - g0, :]
 
-        def warm_up():
-            unread = bank(BANKS - 1, [P, E])
-            for n in range(WARM_PASSES):
-                nc.tensor.matmul_mx(
-                    out=unread[:],
-                    lhsT=k_sorted[0, 0][:, n, :].bitcast(FP4X4),
-                    lhsT_scale=k_planes[1][:, 0, 0:P],
-                    rhs=v_words[0].bitcast(FP4X4),
-                    rhs_scale=v_planes[1][:, 0, :],
-                    start=True,
-                    stop=True,
-                )
+        def load_keys(span):
+            g0, g1 = span
+            words = kept(f"k_words{g0}", [P, g1 - g0, 2 * D], U8)
+            nc.sync.dma_start(out=words[:].bitcast(I32), in_=keys_words[g0:g1].rearrange("g p n -> p g n").bitcast(I32))
+            for g in range(g0, g1):
+                for h0, h1 in ((0, 1), (1, 2), (0, 2)):
+                    k_words[g, h0, h1] = words[:, g - g0, D * h0 : D * h1]
 
-        def load_scale_rows(planes, scales, n, rows):
-            by_row = scales[SCALE_RUNS[n][0] : SCALE_RUNS[n][1]].rearrange("g (q r) n -> r q g n", r=4)
+        def load_scale_rows(planes, scales, run, rows):
+            by_row = scales[run[0] : run[1]].rearrange("g (q r) n -> r q g n", r=4)
             for r in rows:
-                nc.sync.dma_start(out=planes[n][r:P:QUADRANT, :, :].bitcast(I32), in_=by_row[r].bitcast(I32))
-
-        def load_scales(n):
-            load_scale_rows(k_planes, keys_scales, n, range(4))
-            load_scale_rows(v_planes, values_scales, n, range(4))
+                nc.sync.dma_start(out=planes[run][r:P:QUADRANT, :, :].bitcast(I32), in_=by_row[r].bitcast(I32))
 
         def load_retain():
             rows = retain.rearrange("(h q c) -> q h c", h=HALVES, c=P)
             nc.sync.dma_start(out=retain_rows[0:P:QUADRANT, :, :], in_=rows)
 
-        def load_old_first_half():
-            rows = old[0:K_PASS, :].rearrange("(a t i) e -> i a t e", t=PACK, i=PACK)
-            for i in range(PACK):
-                nc.sync.dma_start(out=old_sb[0][i:P:PACK, :, :], in_=rows[i])
-
-        def load_old_second_half():
-            nc.sync.dma_start(out=old_sb[1][:], in_=old[K_PASS:D, :].rearrange("(p t) e -> p t e", t=PACK))
+        def load_old(h):
+            rows = old[K_PASS * h : K_PASS * (h + 1), :].rearrange("(p t) e -> p t e", t=PACK)
+            nc.sync.dma_start(out=old_sb[h][:], in_=rows)
 
         def load_query(c):
             nc.sync.dma_start(out=query_sb[c][:], in_=query_rows[c // 2][:, 2 * (c % 2) : 2 * (c % 2) + 2, :])
@@ -131,38 +116,25 @@ def tile_memory_write_read_s4_kernel(
         def load_gate(n):
             nc.sync.dma_start(out=gate_sb[n][:], in_=gate_rows[n])
 
-        def sort_words_by_runs(g):
+        def sort_words(g, halves):
+            by_slot = kept(f"k_sorted{g}{halves.start}", [P, len(halves), PACK, 2 * P], U8)
             nc.vector.tensor_copy(
-                out=k_sorted[g, 0][:].bitcast(I32).rearrange("k t (a w) -> k t a w", w=2),
-                in_=k_words[g][:, 0:D].bitcast(I32).rearrange("k (a t w) -> k t a w", t=PACK, w=2),
+                out=by_slot[:].bitcast(U16),
+                in_=k_words[g, halves.start, halves.stop].bitcast(U16).rearrange("k (h p t) -> k h t p", p=P, t=PACK),
             )
+            for h in halves:
+                k_sorted[g, h] = by_slot[:, h - halves.start, :, :]
 
-        def sort_words_by_columns(g):
-            nc.vector.tensor_copy(
-                out=k_sorted[g, 1][:].bitcast(U16),
-                in_=k_words[g][:, D : 2 * D].bitcast(U16).rearrange("k (p t) -> k t p", t=PACK),
-            )
-
-        def sort_key_scales(g0, g1):
-            rows = k_planes[place[g0][0]][:, place[g0][1] : place[g0][1] + g1 - g0, :]
-            by_slot = [kept(f"k_scales{g0}{h}", [P, g1 - g0, PACK, P], U8) for h in range(HALVES)]
-            nc.vector.tensor_copy(
-                out=by_slot[0][:].bitcast(I32),
-                in_=rows[:, :, 0:K_PASS].bitcast(I32).rearrange("k g (a t) -> k g t a", t=PACK),
-            )
-            nc.vector.tensor_copy(out=by_slot[1][:], in_=rows[:, :, K_PASS:D].rearrange("k g (p t) -> k g t p", t=PACK))
-            for g in range(g0, g1):
-                for h in range(HALVES):
-                    k_scales[g, h] = by_slot[h][:, g - g0, :, :]
+        def sort_scales(g, halves):
+            run = [run for run in SCALE_RUNS if run[0] <= g < run[1]][0]
+            row = k_planes[run][:, g - run[0], K_PASS * halves.start : K_PASS * halves.stop]
+            by_slot = kept(f"k_scales{g}{halves.start}", [P, len(halves), PACK, P], U8)
+            nc.vector.tensor_copy(out=by_slot[:], in_=row.rearrange("k (h p t) -> k h t p", p=P, t=PACK))
+            for h in halves:
+                k_scales[g, h] = by_slot[:, h - halves.start, :, :]
 
         def sort_retain():
-            nc.vector.tensor_copy(
-                out=retain_sorted[:, 0, :, :].rearrange("q t (a i) -> q t a i", i=PACK),
-                in_=retain_rows[:, 0, :].rearrange("q (a t i) -> q t a i", t=PACK, i=PACK),
-            )
-            nc.vector.tensor_copy(
-                out=retain_sorted[:, 1, :, :], in_=retain_rows[:, 1, :].rearrange("q (c t) -> q t c", t=PACK)
-            )
+            nc.vector.tensor_copy(out=retain_sorted[:], in_=retain_rows[:].rearrange("q h (c t) -> q h t c", t=PACK))
 
         def turn_retain():
             nc.vector.transpose(
@@ -170,65 +142,86 @@ def tile_memory_write_read_s4_kernel(
                 in_=retain_sorted[:].rearrange("q h t c -> q (h t c)"),
             )
 
-        def write_pass(h, t, g):
-            if g == 0:
-                write[h, t] = bank(PACK * h + t, [P, E])
+        def write_pass(h, t, cols, g, start, stop):
             nc.tensor.matmul_mx(
-                out=write[h, t][:],
+                out=write[h, t, cols.start],
                 lhsT=k_sorted[g, h][:, t, :].bitcast(FP4X4),
                 lhsT_scale=k_scales[g, h][:, t, :],
-                rhs=v_words[g].bitcast(FP4X4),
-                rhs_scale=v_planes[place[g][0]][:, place[g][1], :],
-                start=(g == 0),
-                stop=(g == T_PASSES - 1),
+                rhs=v_words[g][:, 2 * cols.start : 2 * cols.stop].bitcast(FP4X4),
+                rhs_scale=v_scales[g][:, cols],
+                start=start,
+                stop=stop,
             )
 
-        def add_old(h, t):
+        def write_passes(h, t, cols, passes, b):
+            for g in passes:
+                if g == 0:
+                    write[h, t, cols.start] = bank(b, [P, cols.stop - cols.start])[:]
+                write_pass(h, t, cols, g, g == 0, g == T_PASSES - 1)
+
+        def warm_up():
+            unread = bank(7, [P, E])
+            for n in range(WARM_PASSES):
+                nc.tensor.matmul_mx(
+                    out=unread[:],
+                    lhsT=k_sorted[0, 0][:, n, :].bitcast(FP4X4),
+                    lhsT_scale=k_planes[SCALE_RUNS[1]][:, 0, 0:P],
+                    rhs=v_words[0].bitcast(FP4X4),
+                    rhs_scale=v_planes[SCALE_RUNS[1]][:, 0, :],
+                    start=True,
+                    stop=True,
+                )
+
+        def add_old(h, t, cols):
             nc.vector.scalar_tensor_tensor(
-                out=memory_slots[h][:, t, :],
-                in0=old_sb[h][:, t, :],
+                out=memory_slots[h][:, t, cols],
+                in0=old_sb[h][:, t, cols],
                 scalar=retain_sb[:, h, t, 0:1],
-                in1=write[h, t][:],
+                in1=write[h, t, cols.start],
                 op0=MULT,
                 op1=ADD,
             )
 
-        def interleave_memory(h, side):
-            cols = slice(SIDE * side, SIDE * (side + 1))
-            nc.vector.tensor_copy(out=memory[h][:, cols, :], in_=memory_slots[h][:, :, cols].rearrange("p t e -> p e t"))
+        def interleave_memory(h, cols, copy):
+            copy(
+                out=memory[h][:, cols, :].rearrange("p (c i) t -> p c t i", i=4),
+                in_=memory_slots[h][:, :, cols].rearrange("p t (c i) -> p c t i", i=4),
+            )
 
-        def quantize_memory(h, side):
-            cols = slice(SIDE * side, SIDE * (side + 1))
+        def quantize_memory(h, cols):
             nc.vector.quantize_mx(
                 out=m_codes[h][:, cols].bitcast(FP8X4),
                 scales=m_scales[h][:, cols],
                 in_=memory[h][:, cols, :].rearrange("r e t -> r (e t)"),
             )
 
-        def split_query(i):
-            row = query_sb[i // 2][:, i % 2, :]
-            pairs = rotating("pairs", [P, 2, K_PASS // 16, PACK, 2], BF16, SPLIT_BUFS)
-            nc.scalar.copy(out=pairs[:], in_=row[:, 0:K_PASS].rearrange("r (a u o i) -> r u a i o", u=2, o=2, i=PACK))
-            q_words[i, 0] = pairs[:].rearrange("r u a i o -> r u (a i o)").bitcast(F32)
-            q_words[i, 1] = row[:, K_PASS:D].bitcast(F32).rearrange("r (p u) -> r u p", u=2)
-            if i < COPIED_TILES:
-                words = rotating("words", [P, 2, P], F32, COPIED_TILES)
-                nc.scalar.copy(out=words[:], in_=q_words[i, 1])
-                q_words[i, 1] = words[:]
-
-        def turn_query(i, b):
-            q_turned[i] = bank(b, [P, HALVES, 2, P])
-            for h in range(HALVES):
-                for u in range(2):
-                    nc.tensor.transpose(q_turned[i][:, h, u, :], q_words[i, h][:, u, :], ident[:])
-
-        def query_out(i):
-            if i % 2 == 0:
-                grouped[i // 2] = rotating("grouped", [P, 2, D], BF16, GROUPED_BUFS)
+        def split_pair(c):
+            words = rotating("q_words", [P, 2, 2, HALVES, P], F32, SPLIT_BUFS)
             nc.scalar.copy(
-                out=grouped[i // 2][:, i % 2, :].bitcast(F32).rearrange("p (h r u) -> p h r u", h=HALVES, u=2),
-                in_=q_turned[i][:].rearrange("p h u r -> p h r u"),
+                out=words[:].rearrange("r u j h (b x) -> r (j h b) u x", x=4),
+                in_=query_sb[c][:].rearrange("r j d -> r (j d)").bitcast(F32).rearrange("r (b x u) -> r b u x", x=4, u=2),
             )
+            for j in range(2):
+                q_words[2 * c + j] = words[:, :, j, :, :]
+
+        def leave_pair(c):
+            for j in range(2):
+                q_words[2 * c + j] = query_sb[c][:, j, :].bitcast(F32).rearrange("r (h p u) -> r u h p", h=HALVES, u=2)
+
+        def turns(first, banks):
+            for i, b in enumerate(banks, first):
+                q_turned[i] = bank(b, [P, HALVES, 2, P])
+                for h in range(HALVES):
+                    for u in range(2):
+                        nc.tensor.transpose(q_turned[i][:, h, u, :], q_words[i][:, u, h, :], ident[:])
+
+        def pair_out(c):
+            grouped[c] = rotating("grouped", [P, 2, D], BF16, GROUPED_BUFS)
+            for j in range(2):
+                nc.scalar.copy(
+                    out=grouped[c][:, j, :].bitcast(F32).rearrange("p (h r u) -> p h r u", h=HALVES, u=2),
+                    in_=q_turned[2 * c + j][:].rearrange("p h u r -> p h r u"),
+                )
 
         def quantize_query(c):
             nc.vector.quantize_mx(
@@ -237,155 +230,151 @@ def tile_memory_write_read_s4_kernel(
                 in_=grouped[c][:].rearrange("p j d -> p (j d)"),
             )
 
-        def read(i, b):
-            read_sums[i] = bank(b, [P, E])
+        def read(i, cols, sums):
             for h in range(HALVES):
                 nc.tensor.matmul_mx(
-                    out=read_sums[i][:],
+                    out=sums,
                     lhsT=q_codes[i // 2][:, i % 2, h, :].bitcast(FP8X4),
                     lhsT_scale=q_scales[i // 2][:, i % 2, h, :],
-                    rhs=m_codes[h][:].bitcast(FP8X4),
-                    rhs_scale=m_scales[h][:],
+                    rhs=m_codes[h][:, cols].bitcast(FP8X4),
+                    rhs_scale=m_scales[h][:, cols],
                     start=(h == 0),
                     stop=(h == HALVES - 1),
                 )
 
-        def gate_and_store(i):
-            n, j = divmod(i, CHUNK)
-            if i % 2 == 0:
-                result[i // 2] = rotating("result", [P, 2, E], F32, RESULT_BUFS)
-            pair = result[i // 2]
-            nc.vector.tensor_tensor(out=pair[:, i % 2, :], in0=read_sums[i][:], in1=gate_sb[n][:, j, :], op=MULT)
-            if i // 2 not in PAIR_STORES:
-                nc.sync.dma_start(out=out_rows[n][:, j, :], in_=pair[:, i % 2, :])
-            elif i % 2 == 1:
-                nc.sync.dma_start(out=out_rows[n][:, j - 1 : j + 1, :], in_=pair[:])
+        def reads(first, banks):
+            for i, b in enumerate(banks, first):
+                read_sums[i] = bank(b, [P, E])
+                read(i, WHOLE, read_sums[i][:])
 
-        zero_planes(0)
+        def store(i0, i1):
+            n, j = divmod(i0, CHUNK)
+            nc.sync.dma_start(out=out_rows[n][:, j : j + i1 - i0, :], in_=result[i0 // 2][:, i0 % 2 : i0 % 2 + i1 - i0, :])
+
+        def gates(i0, i1):
+            for i in range(i0, i1):
+                n, j = divmod(i, CHUNK)
+                if i % 2 == 0:
+                    result[i // 2] = rotating("result", [P, 2, E], F32, RESULT_BUFS)
+                nc.vector.tensor_tensor(out=result[i // 2][:, i % 2, :], in0=read_sums[i][:], in1=gate_sb[n][:, j, :], op=MULT)
+                if i // 2 not in PAIR_STORES:
+                    store(i, i + 1)
+                elif i % 2 == 1:
+                    store(i - 1, i + 1)
+
+        first_run, second_run = SCALE_RUNS
+        both_halves, all_passes = range(HALVES), range(T_PASSES)
+
+        zero_planes(first_run)
         nc.vector.memset(retain_rows[:], 0.0)
-        zero_planes(1)
+        zero_planes(second_run)
+        make_identity(nc, ident[:])
 
-        load_words(0, 1)
-        load_scale_rows(v_planes, values_scales, 0, range(1))
-        load_scale_rows(k_planes, keys_scales, 0, range(4))
-        load_scale_rows(v_planes, values_scales, 0, range(1, 4))
-        load_words(1, 2)
-        load_words(2, 4)
-        load_query(0)
-        sort_words_by_runs(0)
+        def load_words(n):
+            load_keys(WORD_LOADS[n])
+            load_values(WORD_LOADS[n])
+
+        load_words(0)
+        load_scale_rows(v_planes, values_scales, first_run, range(1))
+        load_scale_rows(k_planes, keys_scales, first_run, range(4))
+        load_scale_rows(v_planes, values_scales, first_run, range(1, 4))
+        load_words(1)
+        load_words(2)
+        sort_words(0, range(0, 1))
         warm_up()
         load_retain()
-        load_scale_rows(k_planes, keys_scales, 1, range(4))
-        load_words(4, 6)
-        load_scale_rows(v_planes, values_scales, 1, range(4))
-        load_words(6, 8)
-        load_old_first_half()
+        load_scale_rows(k_planes, keys_scales, second_run, range(4))
+        load_query(0)
+        load_words(3)
+        load_scale_rows(v_planes, values_scales, second_run, range(4))
+        load_words(4)
+        load_old(0)
         load_query(1)
         load_query(2)
-        load_old_second_half()
+        load_old(1)
         for c in (3, 4, 5, 6, 7):
             load_query(c)
         for n in range(4):
             load_gate(n)
 
-        for i in range(FIRST_TURNS):
-            split_query(i)
-
-        for g in range(RUN):
-            if g > 0:
-                sort_words_by_runs(g)
-            sort_words_by_columns(g)
-            if g == 0:
-                sort_key_scales(0, 1)
-                sort_key_scales(1, RUN)
-            for h in range(HALVES):
+        first_passes, last_passes = range(T_PASSES // 2), range(T_PASSES // 2, T_PASSES)
+        first_half, second_half = range(0, 1), range(1, 2)
+        sort_words(0, second_half)
+        for half in (first_half, second_half):
+            sort_scales(0, half)
+        for g in first_passes[1:]:
+            sort_scales(g, both_halves)
+            sort_words(g, both_halves)
+        for g in first_passes:
+            for h in both_halves:
                 for t in range(PACK):
-                    write_pass(h, t, g)
-        nc.vector.memset(ident[:], 0.0)
-        make_identity(nc, ident[:], nomemset=True)
-        sort_key_scales(RUN, T_PASSES)
+                    write_passes(h, t, WHOLE, (g,), PACK * h + t)
+        for c in range(5):
+            split_pair(c)
 
-        for g in (4, 5):
-            sort_words_by_runs(g)
-            for t in range(PACK):
-                write_pass(0, t, g)
-        sort_words_by_columns(4)
         sort_retain()
-        sort_words_by_runs(6)
+        for g in last_passes:
+            sort_scales(g, first_half)
         turn_retain()
-        sort_words_by_runs(7)
-        for g in (5, 6, 7):
-            sort_words_by_columns(g)
+        for g in (4, 5):
+            sort_words(g, first_half)
+        for g in last_passes:
+            sort_scales(g, second_half)
+        for g in (6, 7):
+            sort_words(g, first_half)
+        for g in last_passes:
+            sort_words(g, second_half)
+        for g in (4, 5):
+            for t in range(PACK):
+                write_passes(0, t, WHOLE, (g,), t)
         for t in range(PACK):
-            write_pass(0, t, 6)
-            write_pass(0, t, 7)
-            add_old(0, t)
-        interleave_memory(0, 0)
-        interleave_memory(0, 1)
+            write_passes(0, t, WHOLE, (6, 7), t)
+            add_old(0, t, WHOLE)
+        interleave_memory(0, SIDES[0], nc.vector.tensor_copy)
+        interleave_memory(0, SIDES[1], nc.vector.tensor_copy)
 
         for t in range(PACK):
-            for g in range(RUN, T_PASSES):
-                write_pass(1, t, g)
-            add_old(1, t)
+            write_passes(1, t, WHOLE, last_passes, PACK + t)
+            add_old(1, t, WHOLE)
             if t in (1, 2):
-                quantize_memory(0, t - 1)
-        interleave_memory(1, 0)
-        interleave_memory(1, 1)
+                quantize_memory(0, SIDES[t - 1])
+        interleave_memory(1, SIDES[0], nc.vector.tensor_copy)
+        interleave_memory(1, SIDES[1], nc.vector.tensor_copy)
 
-        def turns(first, banks):
-            for n, b in enumerate(banks):
-                turn_query(first + n, b)
-
-        def reads(first, banks):
-            for n, b in enumerate(banks):
-                read(first + n, b)
-
-        def gates(i0, i1):
-            for i in range(i0, i1):
-                gate_and_store(i)
-
-        def split_pair(c):
-            split_query(2 * c)
-            split_query(2 * c + 1)
-
-        def pair_out(c):
-            query_out(2 * c)
-            query_out(2 * c + 1)
-
-        turns(0, range(BANKS))
+        turns(0, range(8))
         pair_out(0)
         turns(8, (0, 1))
         quantize_query(0)
-        quantize_memory(1, 0)
-        quantize_memory(1, 1)
+        quantize_memory(1, SIDES[0])
+        quantize_memory(1, SIDES[1])
         for c in (1, 2):
             pair_out(c)
             quantize_query(c)
         pair_out(3)
-        reads(0, range(2, BANKS))
+        reads(0, range(2, 8))
         gates(0, 2)
         quantize_query(3)
 
-        split_pair(5)
         pair_out(4)
-        turns(10, (2, 3))
+        split_pair(5)
+        split_pair(6)
+        leave_pair(7)
+        reads(6, (0, 1))
         gates(2, 4)
         quantize_query(4)
-        reads(6, (0, 1, 4, 5))
-        gates(4, 7)
-
-        split_pair(6)
+        turns(10, (2, 3))
         pair_out(5)
-        split_pair(7)
+        reads(8, (4, 5))
+        gates(4, 8)
         quantize_query(5)
-        turns(12, (6, 7, 2, 3))
-        gates(7, 10)
-        reads(10, (0, 1))
+        turns(12, (6, 7, 0, 1))
         pair_out(6)
-        quantize_query(6)
-        gates(10, 12)
-        reads(12, (4, 5))
         pair_out(7)
+        gates(8, 10)
+        reads(10, (2, 3))
+        quantize_query(6)
+        reads(12, (4, 5))
+        gates(10, 12)
         quantize_query(7)
         reads(14, (6, 7))
         gates(12, 16)

@@ -30,11 +30,10 @@ WHOLE = slice(0, E)
 SIDES = (slice(0, SIDE), slice(SIDE, E))
 WORD_LOADS = ((0, 1), (1, 2), (2, 4), (4, 6), (6, 8))
 SCALE_RUNS = ((0, 4), (4, 8))
-PAIR_STORES = (3, 4)
 WARM_PASSES = 3
-SPLIT_BUFS = 6
+SPLIT_BUFS = 8
 GROUPED_BUFS = 4
-RESULT_BUFS = 5
+RESULT_BUFS = {1: 6, 2: 2}
 
 
 def tile_memory_write_read_s4_kernel(
@@ -72,7 +71,7 @@ def tile_memory_write_read_s4_kernel(
         ident = kept("ident", [P, P], F32)
         k_words, v_words, k_sorted, k_scales = {}, {}, {}, {}
         v_scales = {g: v_planes[run][:, g - run[0], :] for run in SCALE_RUNS for g in range(*run)}
-        write, q_words, q_turned, grouped, read_sums, result = {}, {}, {}, {}, {}, {}
+        write, q_words, q_turned, grouped, read_sums, staged = {}, {}, {}, {}, {}, {}
 
         query_rows = query.rearrange("(n p j) d -> n p j d", p=P, j=CHUNK)
         gate_rows = gate.rearrange("(n p j) e -> n p j e", p=P, j=CHUNK)
@@ -94,8 +93,7 @@ def tile_memory_write_read_s4_kernel(
             words = kept(f"k_words{g0}", [P, g1 - g0, 2 * D], U8)
             nc.sync.dma_start(out=words[:].bitcast(I32), in_=keys_words[g0:g1].rearrange("g p n -> p g n").bitcast(I32))
             for g in range(g0, g1):
-                for h0, h1 in ((0, 1), (1, 2), (0, 2)):
-                    k_words[g, h0, h1] = words[:, g - g0, D * h0 : D * h1]
+                k_words[g] = (words, g0)
 
         def load_scale_rows(planes, scales, run, rows):
             by_row = scales[run[0] : run[1]].rearrange("g (q r) n -> r q g n", r=4)
@@ -116,22 +114,26 @@ def tile_memory_write_read_s4_kernel(
         def load_gate(n):
             nc.sync.dma_start(out=gate_sb[n][:], in_=gate_rows[n])
 
-        def sort_words(g, halves):
-            by_slot = kept(f"k_sorted{g}{halves.start}", [P, len(halves), PACK, 2 * P], U8)
+        def sort_words(passes, halves):
+            by_slot = kept(f"k_sorted{passes.start}{halves.start}", [P, len(passes), len(halves), PACK, 2 * P], U8)
+            words, first = k_words[passes.start]
+            rows = words[:, passes.start - first : passes.stop - first, D * halves.start : D * halves.stop]
             nc.vector.tensor_copy(
                 out=by_slot[:].bitcast(U16),
-                in_=k_words[g, halves.start, halves.stop].bitcast(U16).rearrange("k (h p t) -> k h t p", p=P, t=PACK),
+                in_=rows.bitcast(U16).rearrange("k g (h p t) -> k g h t p", p=P, t=PACK),
             )
-            for h in halves:
-                k_sorted[g, h] = by_slot[:, h - halves.start, :, :]
+            for g in passes:
+                for h in halves:
+                    k_sorted[g, h] = by_slot[:, g - passes.start, h - halves.start, :, :]
 
-        def sort_scales(g, halves):
-            run = [run for run in SCALE_RUNS if run[0] <= g < run[1]][0]
-            row = k_planes[run][:, g - run[0], K_PASS * halves.start : K_PASS * halves.stop]
-            by_slot = kept(f"k_scales{g}{halves.start}", [P, len(halves), PACK, P], U8)
-            nc.vector.tensor_copy(out=by_slot[:], in_=row.rearrange("k (h p t) -> k h t p", p=P, t=PACK))
-            for h in halves:
-                k_scales[g, h] = by_slot[:, h - halves.start, :, :]
+        def sort_scales(passes, halves):
+            run = [run for run in SCALE_RUNS if run[0] <= passes.start < run[1]][0]
+            rows = k_planes[run][:, passes.start - run[0] : passes.stop - run[0], K_PASS * halves.start : K_PASS * halves.stop]
+            by_slot = kept(f"k_scales{passes.start}{halves.start}", [P, len(passes), len(halves), PACK, P], U8)
+            nc.vector.tensor_copy(out=by_slot[:], in_=rows.rearrange("k g (h p t) -> k g h t p", p=P, t=PACK))
+            for g in passes:
+                for h in halves:
+                    k_scales[g, h] = by_slot[:, g - passes.start, h - halves.start, :, :]
 
         def sort_retain():
             nc.vector.tensor_copy(out=retain_sorted[:], in_=retain_rows[:].rearrange("q h (c t) -> q h t c", t=PACK))
@@ -177,7 +179,7 @@ def tile_memory_write_read_s4_kernel(
                 out=memory_slots[h][:, t, cols],
                 in0=old_sb[h][:, t, cols],
                 scalar=retain_sb[:, h, t, 0:1],
-                in1=write[h, t, cols.start],
+                in1=write[h, t, 0][:, cols],
                 op0=MULT,
                 op1=ADD,
             )
@@ -204,8 +206,17 @@ def tile_memory_write_read_s4_kernel(
             for j in range(2):
                 q_words[2 * c + j] = words[:, :, j, :, :]
 
-        def leave_pair(c):
-            for j in range(2):
+        def split_tile(i):
+            c, j = divmod(i, 2)
+            words = rotating("q_words", [P, 2, HALVES, P], F32, SPLIT_BUFS)
+            nc.scalar.copy(
+                out=words[:].rearrange("r u h (b x) -> r (h b) u x", x=4),
+                in_=query_sb[c][:, j, :].bitcast(F32).rearrange("r (b x u) -> r b u x", x=4, u=2),
+            )
+            q_words[i] = words[:]
+
+        def leave_pair(c, tiles=range(2)):
+            for j in tiles:
                 q_words[2 * c + j] = query_sb[c][:, j, :].bitcast(F32).rearrange("r (h p u) -> r u h p", h=HALVES, u=2)
 
         def turns(first, banks):
@@ -216,7 +227,7 @@ def tile_memory_write_read_s4_kernel(
                         nc.tensor.transpose(q_turned[i][:, h, u, :], q_words[i][:, u, h, :], ident[:])
 
         def pair_out(c):
-            grouped[c] = rotating("grouped", [P, 2, D], BF16, GROUPED_BUFS)
+            grouped[c] = kept(f"grouped{c % GROUPED_BUFS}", [P, 2, D], BF16)
             for j in range(2):
                 nc.scalar.copy(
                     out=grouped[c][:, j, :].bitcast(F32).rearrange("p (h r u) -> p h r u", h=HALVES, u=2),
@@ -247,20 +258,30 @@ def tile_memory_write_read_s4_kernel(
                 read_sums[i] = bank(b, [P, E])
                 read(i, WHOLE, read_sums[i][:])
 
-        def store(i0, i1):
+        def store(i0, i1, rows):
             n, j = divmod(i0, CHUNK)
-            nc.sync.dma_start(out=out_rows[n][:, j : j + i1 - i0, :], in_=result[i0 // 2][:, i0 % 2 : i0 % 2 + i1 - i0, :])
+            nc.sync.dma_start(out=out_rows[n][:, j : j + i1 - i0, :], in_=rows)
 
-        def gates(i0, i1):
-            for i in range(i0, i1):
-                n, j = divmod(i, CHUNK)
-                if i % 2 == 0:
-                    result[i // 2] = rotating("result", [P, 2, E], F32, RESULT_BUFS)
-                nc.vector.tensor_tensor(out=result[i // 2][:, i % 2, :], in0=read_sums[i][:], in1=gate_sb[n][:, j, :], op=MULT)
-                if i // 2 not in PAIR_STORES:
-                    store(i, i + 1)
-                elif i % 2 == 1:
-                    store(i - 1, i + 1)
+        def gate_rows_of(i):
+            n, j = divmod(i, CHUNK)
+            return gate_sb[n][:, j, :]
+
+        def gates(*tiles):
+            for unit in tiles:
+                unit = unit if isinstance(unit, tuple) else (unit,)
+                result = rotating(f"result{len(unit)}", [P, len(unit), E], F32, RESULT_BUFS[len(unit)])
+                for j, i in enumerate(unit):
+                    nc.vector.tensor_tensor(out=result[:, j, :], in0=read_sums[i][:], in1=gate_rows_of(i), op=MULT)
+                store(unit[0], unit[-1] + 1, result[:])
+
+        def sums_out(i):
+            staged[i] = rotating("staged", [P, E], F32, 1)
+            nc.scalar.copy(out=staged[i][:], in_=read_sums[i][:])
+
+        def side_gate(i, c):
+            result = kept(f"grouped{c % GROUPED_BUFS}", [P, 1, E], F32)
+            nc.gpsimd.tensor_tensor(out=result[:, 0, :], in0=staged[i][:], in1=gate_rows_of(i), op=MULT)
+            store(i, i + 1, result[:])
 
         first_run, second_run = SCALE_RUNS
         both_halves, all_passes = range(HALVES), range(T_PASSES)
@@ -274,56 +295,63 @@ def tile_memory_write_read_s4_kernel(
             load_keys(WORD_LOADS[n])
             load_values(WORD_LOADS[n])
 
-        load_words(0)
-        load_scale_rows(v_planes, values_scales, first_run, range(1))
-        load_scale_rows(k_planes, keys_scales, first_run, range(4))
+        load_keys((0, 1))
+        load_values((0, 1))
+        load_scale_rows(v_planes, values_scales, first_run, range(0, 1))
+        load_scale_rows(k_planes, keys_scales, first_run, range(0, 4))
         load_scale_rows(v_planes, values_scales, first_run, range(1, 4))
-        load_words(1)
-        load_words(2)
-        sort_words(0, range(0, 1))
+        load_keys((1, 2))
+        load_values((1, 2))
+        load_keys((2, 4))
+        load_values((2, 4))
+        sort_words(range(0, 1), range(0, 1))
         warm_up()
         load_retain()
-        load_scale_rows(k_planes, keys_scales, second_run, range(4))
+        load_scale_rows(k_planes, keys_scales, second_run, range(0, 4))
         load_query(0)
-        load_words(3)
-        load_scale_rows(v_planes, values_scales, second_run, range(4))
-        load_words(4)
+        load_keys((4, 6))
+        load_values((4, 6))
+        load_scale_rows(v_planes, values_scales, second_run, range(0, 4))
+        load_keys((6, 8))
+        load_values((6, 8))
         load_old(0)
         load_query(1)
         load_query(2)
         load_old(1)
-        for c in (3, 4, 5, 6, 7):
-            load_query(c)
-        for n in range(4):
-            load_gate(n)
+        load_query(3)
+        load_query(4)
+        load_query(5)
+        load_query(6)
+        load_query(7)
+        load_gate(0)
+        load_gate(1)
+        load_gate(2)
+        load_gate(3)
 
         first_passes, last_passes = range(T_PASSES // 2), range(T_PASSES // 2, T_PASSES)
         first_half, second_half = range(0, 1), range(1, 2)
-        sort_words(0, second_half)
+        sort_words(range(0, 1), second_half)
         for half in (first_half, second_half):
-            sort_scales(0, half)
+            sort_scales(range(0, 1), half)
         for g in first_passes[1:]:
-            sort_scales(g, both_halves)
-            sort_words(g, both_halves)
+            sort_scales(range(g, g + 1), both_halves)
+            sort_words(range(g, g + 1), both_halves)
         for g in first_passes:
             for h in both_halves:
                 for t in range(PACK):
                     write_passes(h, t, WHOLE, (g,), PACK * h + t)
-        for c in range(5):
+        for c in range(4):
             split_pair(c)
 
         sort_retain()
-        for g in last_passes:
-            sort_scales(g, first_half)
+        sort_scales(range(4, 8), first_half)
         turn_retain()
-        for g in (4, 5):
-            sort_words(g, first_half)
-        for g in last_passes:
-            sort_scales(g, second_half)
-        for g in (6, 7):
-            sort_words(g, first_half)
-        for g in last_passes:
-            sort_words(g, second_half)
+        sort_words(range(4, 6), first_half)
+        sort_scales(range(4, 8), second_half)
+        sort_words(range(6, 7), first_half)
+        sort_words(range(7, 8), first_half)
+        sort_words(range(4, 6), second_half)
+        sort_words(range(6, 8), second_half)
         for g in (4, 5):
             for t in range(PACK):
                 write_passes(0, t, WHOLE, (g,), t)
@@ -335,46 +363,50 @@ def tile_memory_write_read_s4_kernel(
 
         for t in range(PACK):
             write_passes(1, t, WHOLE, last_passes, PACK + t)
-            add_old(1, t, WHOLE)
+            for cols in SIDES if t == PACK - 1 else (WHOLE,):
+                add_old(1, t, cols)
             if t in (1, 2):
                 quantize_memory(0, SIDES[t - 1])
-        interleave_memory(1, SIDES[0], nc.vector.tensor_copy)
-        interleave_memory(1, SIDES[1], nc.vector.tensor_copy)
+        for side in SIDES:
+            interleave_memory(1, side, nc.vector.tensor_copy)
 
+        split_tile(8)
+        leave_pair(4, range(1, 2))
         turns(0, range(8))
         pair_out(0)
         turns(8, (0, 1))
         quantize_query(0)
-        quantize_memory(1, SIDES[0])
-        quantize_memory(1, SIDES[1])
+        for side in SIDES:
+            quantize_memory(1, side)
         for c in (1, 2):
             pair_out(c)
             quantize_query(c)
         pair_out(3)
         reads(0, range(2, 8))
-        gates(0, 2)
+        gates(0, 1)
         quantize_query(3)
-
         pair_out(4)
         split_pair(5)
         split_pair(6)
-        leave_pair(7)
+        leave_pair(7, range(1, 2))
         reads(6, (0, 1))
-        gates(2, 4)
+        gates(2, 3)
         quantize_query(4)
         turns(10, (2, 3))
         pair_out(5)
+        split_tile(14)
         reads(8, (4, 5))
-        gates(4, 8)
+        gates(4, 5)
+        gates((6, 7))
         quantize_query(5)
         turns(12, (6, 7, 0, 1))
         pair_out(6)
         pair_out(7)
-        gates(8, 10)
+        gates((8, 9))
         reads(10, (2, 3))
         quantize_query(6)
         reads(12, (4, 5))
-        gates(10, 12)
+        gates(10, 11)
         quantize_query(7)
         reads(14, (6, 7))
-        gates(12, 16)
+        gates(12, 13, 14, 15)

@@ -30,8 +30,9 @@ WHOLE = slice(0, E)
 SIDES = (slice(0, SIDE), slice(SIDE, E))
 WORD_LOADS = ((0, 1), (1, 2), (2, 4), (4, 6), (6, 8))
 SCALE_RUNS = ((0, 4), (4, 8))
+ALIGN = 256
 WARM_PASSES = 3
-SPLIT_BUFS = 8
+SPLIT_BUFS = 6
 GROUPED_BUFS = 4
 RESULT_BUFS = {1: 6, 2: 2}
 
@@ -49,10 +50,10 @@ def tile_memory_write_read_s4_kernel(
             return psum.tile(shape, F32, name=f"bank{b}", tag=f"bank{b}")
 
         def kept(name, shape, dtype):
-            return sbuf.tile(shape, dtype, name=name, tag=name, align_bytes=64)
+            return sbuf.tile(shape, dtype, name=name, tag=name, align_bytes=ALIGN)
 
         def rotating(tag, shape, dtype, bufs):
-            return sbuf.tile(shape, dtype, name=tag, tag=tag, bufs=bufs, align_bytes=64)
+            return sbuf.tile(shape, dtype, name=tag, tag=tag, bufs=bufs, align_bytes=ALIGN)
 
         k_planes = {run: kept(f"k_planes{run[0]}", [P, run[1] - run[0], D], U8) for run in SCALE_RUNS}
         v_planes = {run: kept(f"v_planes{run[0]}", [P, run[1] - run[0], E], U8) for run in SCALE_RUNS}

@@ -31,6 +31,7 @@ SIDES = (slice(0, SIDE), slice(SIDE, E))
 WORD_LOADS = ((0, 1), (1, 2), (2, 4), (4, 6), (6, 8))
 SCALE_RUNS = ((0, 4), (4, 8))
 ALIGN = 256
+LINE = 16
 WARM_PASSES = 3
 SPLIT_BUFS = 6
 GROUPED_BUFS = 4
@@ -120,8 +121,8 @@ def tile_memory_write_read_s4_kernel(
             words, first = k_words[passes.start]
             rows = words[:, passes.start - first : passes.stop - first, D * halves.start : D * halves.stop]
             nc.vector.tensor_copy(
-                out=by_slot[:].bitcast(U16),
-                in_=rows.bitcast(U16).rearrange("k g (h p t) -> k g h t p", p=P, t=PACK),
+                out=by_slot[:].bitcast(U16).rearrange("k g h t (b i) -> k (g h) b t i", i=LINE // 2),
+                in_=rows.bitcast(U16).rearrange("k g (h b i t) -> k (g h) b t i", h=len(halves), i=LINE // 2, t=PACK),
             )
             for g in passes:
                 for h in halves:
@@ -131,7 +132,10 @@ def tile_memory_write_read_s4_kernel(
             run = [run for run in SCALE_RUNS if run[0] <= passes.start < run[1]][0]
             rows = k_planes[run][:, passes.start - run[0] : passes.stop - run[0], K_PASS * halves.start : K_PASS * halves.stop]
             by_slot = kept(f"k_scales{passes.start}{halves.start}", [P, len(passes), len(halves), PACK, P], U8)
-            nc.vector.tensor_copy(out=by_slot[:], in_=rows.rearrange("k g (h p t) -> k g h t p", p=P, t=PACK))
+            nc.vector.tensor_copy(
+                out=by_slot[:].rearrange("k g h t (b i) -> k (g h) b t i", i=LINE),
+                in_=rows.rearrange("k g (h b i t) -> k (g h) b t i", h=len(halves), i=LINE, t=PACK),
+            )
             for g in passes:
                 for h in halves:
                     k_scales[g, h] = by_slot[:, g - passes.start, h - halves.start, :, :]

@@ -28,11 +28,10 @@ CHUNK = 4
 SIDE = E // 2
 WHOLE = slice(0, E)
 SIDES = (slice(0, SIDE), slice(SIDE, E))
-WORD_LOADS = ((0, 1), (1, 2), (2, 4), (4, 6), (6, 8))
 SCALE_RUNS = ((0, 4), (4, 8))
 ALIGN = 256
 LINE = 16
-WARM_PASSES = 3
+WARM_PASSES = 6
 SPLIT_BUFS = 6
 GROUPED_BUFS = 4
 RESULT_BUFS = {1: 6, 2: 2}
@@ -73,15 +72,11 @@ def tile_memory_write_read_s4_kernel(
         ident = kept("ident", [P, P], F32)
         k_words, v_words, k_sorted, k_scales = {}, {}, {}, {}
         v_scales = {g: v_planes[run][:, g - run[0], :] for run in SCALE_RUNS for g in range(*run)}
-        write, q_words, q_turned, grouped, read_sums, staged = {}, {}, {}, {}, {}, {}
+        write, q_words, q_turned, grouped, read_sums = {}, {}, {}, {}, {}
 
         query_rows = query.rearrange("(n p j) d -> n p j d", p=P, j=CHUNK)
         gate_rows = gate.rearrange("(n p j) e -> n p j e", p=P, j=CHUNK)
         out_rows = out.rearrange("(n p j) e -> n p j e", p=P, j=CHUNK)
-
-        def zero_planes(run):
-            nc.vector.memset(v_planes[run][:].bitcast(I32), 0)
-            nc.vector.memset(k_planes[run][:].bitcast(I32), 0)
 
         def load_values(span):
             g0, g1 = span
@@ -141,7 +136,7 @@ def tile_memory_write_read_s4_kernel(
                     k_scales[g, h] = by_slot[:, g - passes.start, h - halves.start, :, :]
 
         def sort_retain():
-            nc.vector.tensor_copy(out=retain_sorted[:], in_=retain_rows[:].rearrange("q h (c t) -> q h t c", t=PACK))
+            nc.scalar.copy(out=retain_sorted[:], in_=retain_rows[:].rearrange("q h (c t) -> q h t c", t=PACK))
 
         def turn_retain():
             nc.vector.transpose(
@@ -168,13 +163,14 @@ def tile_memory_write_read_s4_kernel(
 
         def warm_up():
             unread = bank(7, [P, E])
+            zeros = v_planes[SCALE_RUNS[1]]
             for n in range(WARM_PASSES):
                 nc.tensor.matmul_mx(
                     out=unread[:],
-                    lhsT=k_sorted[0, 0][:, n, :].bitcast(FP4X4),
-                    lhsT_scale=k_planes[SCALE_RUNS[1]][:, 0, 0:P],
-                    rhs=v_words[0].bitcast(FP4X4),
-                    rhs_scale=v_planes[SCALE_RUNS[1]][:, 0, :],
+                    lhsT=zeros[:, 3, 0 : 2 * P].bitcast(FP4X4),
+                    lhsT_scale=zeros[:, 3, 2 * P : 3 * P],
+                    rhs=zeros[:, 0:2, :].rearrange("k g n -> k (g n)").bitcast(FP4X4),
+                    rhs_scale=zeros[:, 2, :],
                     start=True,
                     stop=True,
                 )
@@ -279,26 +275,16 @@ def tile_memory_write_read_s4_kernel(
                     nc.vector.tensor_tensor(out=result[:, j, :], in0=read_sums[i][:], in1=gate_rows_of(i), op=MULT)
                 store(unit[0], unit[-1] + 1, result[:])
 
-        def sums_out(i):
-            staged[i] = rotating("staged", [P, E], F32, 1)
-            nc.scalar.copy(out=staged[i][:], in_=read_sums[i][:])
-
-        def side_gate(i, c):
-            result = kept(f"grouped{c % GROUPED_BUFS}", [P, 1, E], F32)
-            nc.gpsimd.tensor_tensor(out=result[:, 0, :], in0=staged[i][:], in1=gate_rows_of(i), op=MULT)
-            store(i, i + 1, result[:])
-
         first_run, second_run = SCALE_RUNS
-        both_halves, all_passes = range(HALVES), range(T_PASSES)
+        both_halves = range(HALVES)
 
-        zero_planes(first_run)
+        nc.vector.memset(v_planes[first_run][:].bitcast(I32), 0)
+        nc.vector.memset(k_planes[first_run][:].bitcast(I32), 0)
+        nc.vector.memset(k_planes[second_run][:].bitcast(I32), 0)
+        nc.vector.memset(v_planes[second_run][:].bitcast(I32), 0)
         nc.vector.memset(retain_rows[:], 0.0)
-        zero_planes(second_run)
-        make_identity(nc, ident[:])
-
-        def load_words(n):
-            load_keys(WORD_LOADS[n])
-            load_values(WORD_LOADS[n])
+        nc.vector.memset(ident[:], 0.0)
+        make_identity(nc, ident[:], nomemset=True)
 
         load_keys((0, 1))
         load_values((0, 1))
@@ -345,10 +331,10 @@ def tile_memory_write_read_s4_kernel(
             for h in both_halves:
                 for t in range(PACK):
                     write_passes(h, t, WHOLE, (g,), PACK * h + t)
+        sort_retain()
         for c in range(4):
             split_pair(c)
 
-        sort_retain()
         sort_scales(range(4, 8), first_half)
         turn_retain()
         sort_words(range(4, 6), first_half)

@@ -24,17 +24,18 @@ QUADRANT = 32
 T_PASSES = T // K_PASS
 HALVES = D // K_PASS
 R_TILES = R // P
-CHUNK = 4
+CHUNK = 8
 SIDE = E // 2
 WHOLE = slice(0, E)
 SIDES = (slice(0, SIDE), slice(SIDE, E))
-SCALE_RUNS = ((0, 4), (4, 8))
+KEY_RUNS = ((0, 3), (3, 8))
+VALUE_RUNS = ((0, 3), (3, 8))
 ALIGN = 256
 LINE = 16
-WARM_PASSES = 6
-SPLIT_BUFS = 6
+WARM_PASSES = 5
+SPLIT_BUFS = 5
 GROUPED_BUFS = 4
-RESULT_BUFS = {1: 6, 2: 2}
+RESULT_BUFS = {1: 4, 2: 4}
 
 
 def tile_memory_write_read_s4_kernel(
@@ -55,8 +56,8 @@ def tile_memory_write_read_s4_kernel(
         def rotating(tag, shape, dtype, bufs):
             return sbuf.tile(shape, dtype, name=tag, tag=tag, bufs=bufs, align_bytes=ALIGN)
 
-        k_planes = {run: kept(f"k_planes{run[0]}", [P, run[1] - run[0], D], U8) for run in SCALE_RUNS}
-        v_planes = {run: kept(f"v_planes{run[0]}", [P, run[1] - run[0], E], U8) for run in SCALE_RUNS}
+        k_planes = {run: kept(f"k_planes{run[0]}", [P, run[1] - run[0], D], U8) for run in KEY_RUNS}
+        v_planes = {run: kept(f"v_planes{run[0]}", [P, run[1] - run[0], E], U8) for run in VALUE_RUNS}
         retain_rows = kept("retain_rows", [P, HALVES, P], BF16)
         retain_sorted = kept("retain_sorted", [P, HALVES, PACK, QUADRANT], BF16)
         retain_sb = kept("retain_sb", [P, HALVES, PACK, QUADRANT], BF16)
@@ -65,13 +66,12 @@ def tile_memory_write_read_s4_kernel(
         memory = [kept(f"memory{h}", [P, E, PACK], BF16) for h in range(HALVES)]
         m_codes = [kept(f"m_codes{h}", [P, E], U32) for h in range(HALVES)]
         m_scales = [kept(f"m_scales{h}", [P, E], U8) for h in range(HALVES)]
-        query_sb = [kept(f"query_sb{c}", [P, 2, D], BF16) for c in range(R_TILES // 2)]
         q_codes = [kept(f"q_codes{c}", [P, 2, HALVES, P], U32) for c in range(R_TILES // 2)]
         q_scales = [kept(f"q_scales{c}", [P, 2, HALVES, P], U8) for c in range(R_TILES // 2)]
-        gate_sb = [kept(f"gate_sb{n}", [P, CHUNK, E], BF16) for n in range(R_TILES // CHUNK)]
         ident = kept("ident", [P, P], F32)
         k_words, v_words, k_sorted, k_scales = {}, {}, {}, {}
-        v_scales = {g: v_planes[run][:, g - run[0], :] for run in SCALE_RUNS for g in range(*run)}
+        v_scales = {g: v_planes[run][:, g - run[0], :] for run in VALUE_RUNS for g in range(*run)}
+        query_sb, gate_sb = {}, {}
         write, q_words, q_turned, grouped, read_sums = {}, {}, {}, {}, {}
 
         query_rows = query.rearrange("(n p j) d -> n p j d", p=P, j=CHUNK)
@@ -85,12 +85,14 @@ def tile_memory_write_read_s4_kernel(
             for g in range(g0, g1):
                 v_words[g] = words[:, g - g0, :]
 
-        def load_keys(span):
+        def load_keys(span, halves=range(HALVES)):
             g0, g1 = span
-            words = kept(f"k_words{g0}", [P, g1 - g0, 2 * D], U8)
-            nc.sync.dma_start(out=words[:].bitcast(I32), in_=keys_words[g0:g1].rearrange("g p n -> p g n").bitcast(I32))
+            words = kept(f"k_words{g0}{halves.start}", [P, g1 - g0, D * len(halves)], U8)
+            rows = keys_words[g0:g1, :, D * halves.start : D * halves.stop].rearrange("g p n -> p g n")
+            nc.sync.dma_start(out=words[:].bitcast(I32), in_=rows.bitcast(I32))
             for g in range(g0, g1):
-                k_words[g] = (words, g0)
+                for h in halves:
+                    k_words[g, h] = (words, g0, halves.start)
 
         def load_scale_rows(planes, scales, run, rows):
             by_row = scales[run[0] : run[1]].rearrange("g (q r) n -> r q g n", r=4)
@@ -105,16 +107,24 @@ def tile_memory_write_read_s4_kernel(
             rows = old[K_PASS * h : K_PASS * (h + 1), :].rearrange("(p t) e -> p t e", t=PACK)
             nc.sync.dma_start(out=old_sb[h][:], in_=rows)
 
-        def load_query(c):
-            nc.sync.dma_start(out=query_sb[c][:], in_=query_rows[c // 2][:, 2 * (c % 2) : 2 * (c % 2) + 2, :])
+        def load_query(c0, c1):
+            n, j = divmod(2 * c0, CHUNK)
+            rows = kept(f"query_sb{c0}", [P, 2 * (c1 - c0), D], BF16)
+            nc.sync.dma_start(out=rows[:], in_=query_rows[n][:, j : j + 2 * (c1 - c0), :])
+            for c in range(c0, c1):
+                query_sb[c] = rows[:, 2 * (c - c0) : 2 * (c - c0) + 2, :]
 
-        def load_gate(n):
-            nc.sync.dma_start(out=gate_sb[n][:], in_=gate_rows[n])
+        def load_gate(i0, i1):
+            n, j = divmod(i0, CHUNK)
+            rows = kept(f"gate_sb{i0}", [P, i1 - i0, E], BF16)
+            nc.sync.dma_start(out=rows[:], in_=gate_rows[n][:, j : j + i1 - i0, :])
+            for i in range(i0, i1):
+                gate_sb[i] = rows[:, i - i0, :]
 
         def sort_words(passes, halves):
             by_slot = kept(f"k_sorted{passes.start}{halves.start}", [P, len(passes), len(halves), PACK, 2 * P], U8)
-            words, first = k_words[passes.start]
-            rows = words[:, passes.start - first : passes.stop - first, D * halves.start : D * halves.stop]
+            words, g0, h0 = k_words[passes.start, halves.start]
+            rows = words[:, passes.start - g0 : passes.stop - g0, D * (halves.start - h0) : D * (halves.stop - h0)]
             nc.vector.tensor_copy(
                 out=by_slot[:].bitcast(U16).rearrange("k g h t (b i) -> k (g h) b t i", i=LINE // 2),
                 in_=rows.bitcast(U16).rearrange("k g (h b i t) -> k (g h) b t i", h=len(halves), i=LINE // 2, t=PACK),
@@ -124,7 +134,7 @@ def tile_memory_write_read_s4_kernel(
                     k_sorted[g, h] = by_slot[:, g - passes.start, h - halves.start, :, :]
 
         def sort_scales(passes, halves):
-            run = [run for run in SCALE_RUNS if run[0] <= passes.start < run[1]][0]
+            run = [run for run in KEY_RUNS if run[0] <= passes.start < run[1]][0]
             rows = k_planes[run][:, passes.start - run[0] : passes.stop - run[0], K_PASS * halves.start : K_PASS * halves.stop]
             by_slot = kept(f"k_scales{passes.start}{halves.start}", [P, len(passes), len(halves), PACK, P], U8)
             nc.vector.tensor_copy(
@@ -163,7 +173,7 @@ def tile_memory_write_read_s4_kernel(
 
         def warm_up():
             unread = bank(7, [P, E])
-            zeros = v_planes[SCALE_RUNS[1]]
+            zeros = v_planes[VALUE_RUNS[-1]]
             for n in range(WARM_PASSES):
                 nc.tensor.matmul_mx(
                     out=unread[:],
@@ -202,7 +212,7 @@ def tile_memory_write_read_s4_kernel(
             words = rotating("q_words", [P, 2, 2, HALVES, P], F32, SPLIT_BUFS)
             nc.scalar.copy(
                 out=words[:].rearrange("r u j h (b x) -> r (j h b) u x", x=4),
-                in_=query_sb[c][:].rearrange("r j d -> r (j d)").bitcast(F32).rearrange("r (b x u) -> r b u x", x=4, u=2),
+                in_=query_sb[c].rearrange("r j d -> r (j d)").bitcast(F32).rearrange("r (b x u) -> r b u x", x=4, u=2),
             )
             for j in range(2):
                 q_words[2 * c + j] = words[:, :, j, :, :]
@@ -263,70 +273,66 @@ def tile_memory_write_read_s4_kernel(
             n, j = divmod(i0, CHUNK)
             nc.sync.dma_start(out=out_rows[n][:, j : j + i1 - i0, :], in_=rows)
 
-        def gate_rows_of(i):
-            n, j = divmod(i, CHUNK)
-            return gate_sb[n][:, j, :]
-
         def gates(*tiles):
             for unit in tiles:
                 unit = unit if isinstance(unit, tuple) else (unit,)
                 result = rotating(f"result{len(unit)}", [P, len(unit), E], F32, RESULT_BUFS[len(unit)])
                 for j, i in enumerate(unit):
-                    nc.vector.tensor_tensor(out=result[:, j, :], in0=read_sums[i][:], in1=gate_rows_of(i), op=MULT)
+                    nc.vector.tensor_tensor(out=result[:, j, :], in0=read_sums[i][:], in1=gate_sb[i], op=MULT)
                 store(unit[0], unit[-1] + 1, result[:])
 
-        first_run, second_run = SCALE_RUNS
         both_halves = range(HALVES)
-
-        nc.vector.memset(v_planes[first_run][:].bitcast(I32), 0)
-        nc.vector.memset(k_planes[first_run][:].bitcast(I32), 0)
-        nc.vector.memset(k_planes[second_run][:].bitcast(I32), 0)
-        nc.vector.memset(v_planes[second_run][:].bitcast(I32), 0)
+        nc.vector.memset(v_planes[VALUE_RUNS[0]][:].bitcast(I32), 0)
+        nc.vector.memset(k_planes[KEY_RUNS[0]][:].bitcast(I32), 0)
+        nc.vector.memset(v_planes[VALUE_RUNS[1]][:].bitcast(I32), 0)
+        nc.vector.memset(k_planes[KEY_RUNS[1]][:].bitcast(I32), 0)
         nc.vector.memset(retain_rows[:], 0.0)
         nc.vector.memset(ident[:], 0.0)
         make_identity(nc, ident[:], nomemset=True)
-
-        load_keys((0, 1))
         load_values((0, 1))
-        load_scale_rows(v_planes, values_scales, first_run, range(0, 1))
-        load_scale_rows(k_planes, keys_scales, first_run, range(0, 4))
-        load_scale_rows(v_planes, values_scales, first_run, range(1, 4))
+        load_keys((0, 1), range(0, 1))
+        load_scale_rows(v_planes, values_scales, VALUE_RUNS[0], range(0, 1))
+        load_scale_rows(k_planes, keys_scales, KEY_RUNS[0], range(0, 4))
+        load_scale_rows(v_planes, values_scales, VALUE_RUNS[0], range(1, 4))
+        load_keys((0, 1), range(1, 2))
         load_keys((1, 2))
         load_values((1, 2))
         load_keys((2, 4))
         load_values((2, 4))
         sort_words(range(0, 1), range(0, 1))
         warm_up()
-        load_retain()
-        load_scale_rows(k_planes, keys_scales, second_run, range(0, 4))
-        load_query(0)
+        load_scale_rows(k_planes, keys_scales, KEY_RUNS[1], range(0, 4))
+        load_scale_rows(v_planes, values_scales, VALUE_RUNS[1], range(0, 4))
         load_keys((4, 6))
         load_values((4, 6))
-        load_scale_rows(v_planes, values_scales, second_run, range(0, 4))
+        load_retain()
         load_keys((6, 8))
         load_values((6, 8))
         load_old(0)
-        load_query(1)
-        load_query(2)
+        load_query(0, 1)
+        load_query(1, 2)
+        load_query(2, 3)
         load_old(1)
-        load_query(3)
-        load_query(4)
-        load_query(5)
-        load_query(6)
-        load_query(7)
-        load_gate(0)
-        load_gate(1)
-        load_gate(2)
-        load_gate(3)
+        load_query(3, 4)
+        load_query(4, 5)
+        load_query(5, 6)
+        load_query(6, 7)
+        load_gate(0, 4)
+        load_query(7, 8)
+        load_gate(4, 8)
+        load_gate(8, 16)
 
         first_passes, last_passes = range(T_PASSES // 2), range(T_PASSES // 2, T_PASSES)
         first_half, second_half = range(0, 1), range(1, 2)
+        sort_scales(range(0, 1), first_half)
+        sort_scales(range(0, 1), second_half)
         sort_words(range(0, 1), second_half)
-        for half in (first_half, second_half):
-            sort_scales(range(0, 1), half)
-        for g in first_passes[1:]:
-            sort_scales(range(g, g + 1), both_halves)
-            sort_words(range(g, g + 1), both_halves)
+        sort_scales(range(1, 2), both_halves)
+        sort_words(range(1, 2), both_halves)
+        sort_scales(range(2, 3), both_halves)
+        sort_words(range(2, 3), both_halves)
+        sort_words(range(3, 4), both_halves)
+        sort_scales(range(3, 4), both_halves)
         for g in first_passes:
             for h in both_halves:
                 for t in range(PACK):
@@ -336,11 +342,10 @@ def tile_memory_write_read_s4_kernel(
             split_pair(c)
 
         sort_scales(range(4, 8), first_half)
-        turn_retain()
         sort_words(range(4, 6), first_half)
         sort_scales(range(4, 8), second_half)
-        sort_words(range(6, 7), first_half)
-        sort_words(range(7, 8), first_half)
+        sort_words(range(6, 8), first_half)
+        turn_retain()
         sort_words(range(4, 6), second_half)
         sort_words(range(6, 8), second_half)
         for g in (4, 5):
@@ -354,15 +359,14 @@ def tile_memory_write_read_s4_kernel(
 
         for t in range(PACK):
             write_passes(1, t, WHOLE, last_passes, PACK + t)
+            if t < len(SIDES):
+                quantize_memory(0, SIDES[t])
             for cols in SIDES if t == PACK - 1 else (WHOLE,):
                 add_old(1, t, cols)
-            if t in (1, 2):
-                quantize_memory(0, SIDES[t - 1])
         for side in SIDES:
             interleave_memory(1, side, nc.vector.tensor_copy)
 
-        split_tile(8)
-        leave_pair(4, range(1, 2))
+        leave_pair(4)
         turns(0, range(8))
         pair_out(0)
         turns(8, (0, 1))
@@ -374,20 +378,20 @@ def tile_memory_write_read_s4_kernel(
             quantize_query(c)
         pair_out(3)
         reads(0, range(2, 8))
-        gates(0, 1)
+        gates((0, 1))
         quantize_query(3)
         pair_out(4)
         split_pair(5)
         split_pair(6)
-        leave_pair(7, range(1, 2))
         reads(6, (0, 1))
-        gates(2, 3)
+        gates((2, 3))
         quantize_query(4)
         turns(10, (2, 3))
         pair_out(5)
         split_tile(14)
+        leave_pair(7, range(1, 2))
         reads(8, (4, 5))
-        gates(4, 5)
+        gates((4, 5))
         gates((6, 7))
         quantize_query(5)
         turns(12, (6, 7, 0, 1))
@@ -397,7 +401,7 @@ def tile_memory_write_read_s4_kernel(
         reads(10, (2, 3))
         quantize_query(6)
         reads(12, (4, 5))
-        gates(10, 11)
+        gates((10, 11))
         quantize_query(7)
         reads(14, (6, 7))
         gates(12, 13, 14, 15)

@@ -33,9 +33,8 @@ VALUE_RUNS = ((0, 3), (3, 8))
 ALIGN = 256
 LINE = 16
 WARM_PASSES = 5
-SPLIT_BUFS = 5
+SPLIT_BUFS = 8
 GROUPED_BUFS = 4
-RESULT_BUFS = {1: 4, 2: 4}
 
 
 def tile_memory_write_read_s4_kernel(
@@ -71,8 +70,8 @@ def tile_memory_write_read_s4_kernel(
         ident = kept("ident", [P, P], F32)
         k_words, v_words, k_sorted, k_scales = {}, {}, {}, {}
         v_scales = {g: v_planes[run][:, g - run[0], :] for run in VALUE_RUNS for g in range(*run)}
-        query_sb, gate_sb = {}, {}
-        write, q_words, q_turned, grouped, read_sums = {}, {}, {}, {}, {}
+        query_sb, query_tile, gate_sb = {}, {}, {}
+        write, q_words, q_turned, grouped, read_sums, result = {}, {}, {}, {}, {}, {}
 
         query_rows = query.rearrange("(n p j) d -> n p j d", p=P, j=CHUNK)
         gate_rows = gate.rearrange("(n p j) e -> n p j e", p=P, j=CHUNK)
@@ -103,9 +102,9 @@ def tile_memory_write_read_s4_kernel(
             rows = retain.rearrange("(h q c) -> q h c", h=HALVES, c=P)
             nc.sync.dma_start(out=retain_rows[0:P:QUADRANT, :, :], in_=rows)
 
-        def load_old(h):
+        def load_old(h, slots=slice(0, PACK)):
             rows = old[K_PASS * h : K_PASS * (h + 1), :].rearrange("(p t) e -> p t e", t=PACK)
-            nc.sync.dma_start(out=old_sb[h][:], in_=rows)
+            nc.sync.dma_start(out=old_sb[h][:, slots, :], in_=rows[:, slots, :])
 
         def load_query(c0, c1):
             n, j = divmod(2 * c0, CHUNK)
@@ -113,6 +112,14 @@ def tile_memory_write_read_s4_kernel(
             nc.sync.dma_start(out=rows[:], in_=query_rows[n][:, j : j + 2 * (c1 - c0), :])
             for c in range(c0, c1):
                 query_sb[c] = rows[:, 2 * (c - c0) : 2 * (c - c0) + 2, :]
+                for j in range(2):
+                    query_tile[2 * c + j] = query_sb[c][:, j, :]
+
+        def load_query_tile(i):
+            n, j = divmod(i, CHUNK)
+            rows = kept(f"query_sb{i // 2}" + "b" * (i % 2), [P, D], BF16)
+            nc.sync.dma_start(out=rows[:], in_=query_rows[n][:, j, :])
+            query_tile[i] = rows[:]
 
         def load_gate(i0, i1):
             n, j = divmod(i0, CHUNK)
@@ -218,17 +225,16 @@ def tile_memory_write_read_s4_kernel(
                 q_words[2 * c + j] = words[:, :, j, :, :]
 
         def split_tile(i):
-            c, j = divmod(i, 2)
             words = rotating("q_words", [P, 2, HALVES, P], F32, SPLIT_BUFS)
             nc.scalar.copy(
                 out=words[:].rearrange("r u h (b x) -> r (h b) u x", x=4),
-                in_=query_sb[c][:, j, :].bitcast(F32).rearrange("r (b x u) -> r b u x", x=4, u=2),
+                in_=query_tile[i].bitcast(F32).rearrange("r (b x u) -> r b u x", x=4, u=2),
             )
             q_words[i] = words[:]
 
         def leave_pair(c, tiles=range(2)):
             for j in tiles:
-                q_words[2 * c + j] = query_sb[c][:, j, :].bitcast(F32).rearrange("r (h p u) -> r u h p", h=HALVES, u=2)
+                q_words[2 * c + j] = query_tile[2 * c + j].bitcast(F32).rearrange("r (h p u) -> r u h p", h=HALVES, u=2)
 
         def turns(first, banks):
             for i, b in enumerate(banks, first):
@@ -245,11 +251,11 @@ def tile_memory_write_read_s4_kernel(
                     in_=q_turned[2 * c + j][:].rearrange("p h u r -> p h r u"),
                 )
 
-        def quantize_query(c):
+        def quantize_query(c, tiles=slice(0, 2)):
             nc.vector.quantize_mx(
-                out=q_codes[c][:].rearrange("p j h r -> p (j h r)").bitcast(FP8X4),
-                scales=q_scales[c][:].rearrange("p j h r -> p (j h r)"),
-                in_=grouped[c][:].rearrange("p j d -> p (j d)"),
+                out=q_codes[c][:, tiles].rearrange("p j h r -> p (j h r)").bitcast(FP8X4),
+                scales=q_scales[c][:, tiles].rearrange("p j h r -> p (j h r)"),
+                in_=grouped[c][:, tiles].rearrange("p j d -> p (j d)"),
             )
 
         def read(i, cols, sums):
@@ -276,10 +282,12 @@ def tile_memory_write_read_s4_kernel(
         def gates(*tiles):
             for unit in tiles:
                 unit = unit if isinstance(unit, tuple) else (unit,)
-                result = rotating(f"result{len(unit)}", [P, len(unit), E], F32, RESULT_BUFS[len(unit)])
-                for j, i in enumerate(unit):
-                    nc.vector.tensor_tensor(out=result[:, j, :], in0=read_sums[i][:], in1=gate_sb[i], op=MULT)
-                store(unit[0], unit[-1] + 1, result[:])
+                for i in unit:
+                    c, j = divmod(i, 2)
+                    if j == 0:
+                        result[c] = kept(f"query_sb{c}", [P, 2, E], F32)
+                    nc.vector.tensor_tensor(out=result[c][:, j, :], in0=read_sums[i][:], in1=gate_sb[i], op=MULT)
+                store(unit[0], unit[-1] + 1, result[unit[0] // 2][:, unit[0] % 2 : unit[-1] % 2 + 1, :])
 
         both_halves = range(HALVES)
         nc.vector.memset(v_planes[VALUE_RUNS[0]][:].bitcast(I32), 0)
@@ -287,11 +295,9 @@ def tile_memory_write_read_s4_kernel(
         nc.vector.memset(v_planes[VALUE_RUNS[1]][:].bitcast(I32), 0)
         nc.vector.memset(k_planes[KEY_RUNS[1]][:].bitcast(I32), 0)
         nc.vector.memset(retain_rows[:], 0.0)
-        nc.vector.memset(ident[:], 0.0)
-        make_identity(nc, ident[:], nomemset=True)
         load_values((0, 1))
-        load_keys((0, 1), range(0, 1))
         load_scale_rows(v_planes, values_scales, VALUE_RUNS[0], range(0, 1))
+        load_keys((0, 1), range(0, 1))
         load_scale_rows(k_planes, keys_scales, KEY_RUNS[0], range(0, 4))
         load_scale_rows(v_planes, values_scales, VALUE_RUNS[0], range(1, 4))
         load_keys((0, 1), range(1, 2))
@@ -312,9 +318,11 @@ def tile_memory_write_read_s4_kernel(
         load_query(0, 1)
         load_query(1, 2)
         load_query(2, 3)
-        load_old(1)
+        load_old(1, slice(0, 2))
         load_query(3, 4)
-        load_query(4, 5)
+        load_old(1, slice(2, 4))
+        load_query_tile(8)
+        load_query_tile(9)
         load_query(5, 6)
         load_query(6, 7)
         load_gate(0, 4)
@@ -326,8 +334,8 @@ def tile_memory_write_read_s4_kernel(
         first_half, second_half = range(0, 1), range(1, 2)
         sort_scales(range(0, 1), first_half)
         sort_scales(range(0, 1), second_half)
-        sort_words(range(0, 1), second_half)
         sort_scales(range(1, 2), both_halves)
+        sort_words(range(0, 1), second_half)
         sort_words(range(1, 2), both_halves)
         sort_scales(range(2, 3), both_halves)
         sort_words(range(2, 3), both_halves)
@@ -348,6 +356,8 @@ def tile_memory_write_read_s4_kernel(
         turn_retain()
         sort_words(range(4, 6), second_half)
         sort_words(range(6, 8), second_half)
+        nc.vector.memset(ident[:], 0.0)
+        make_identity(nc, ident[:], nomemset=True)
         for g in (4, 5):
             for t in range(PACK):
                 write_passes(0, t, WHOLE, (g,), t)
@@ -366,16 +376,19 @@ def tile_memory_write_read_s4_kernel(
         for side in SIDES:
             interleave_memory(1, side, nc.vector.tensor_copy)
 
-        leave_pair(4)
+        split_tile(8)
+        leave_pair(4, range(1, 2))
         turns(0, range(8))
         pair_out(0)
         turns(8, (0, 1))
         quantize_query(0)
         for side in SIDES:
             quantize_memory(1, side)
-        for c in (1, 2):
-            pair_out(c)
-            quantize_query(c)
+        pair_out(1)
+        quantize_query(1)
+        pair_out(2)
+        quantize_query(2, slice(0, 1))
+        quantize_query(2, slice(1, 2))
         pair_out(3)
         reads(0, range(2, 8))
         gates((0, 1))
@@ -385,23 +398,23 @@ def tile_memory_write_read_s4_kernel(
         split_pair(6)
         reads(6, (0, 1))
         gates((2, 3))
+        gates((4, 5))
         quantize_query(4)
-        turns(10, (2, 3))
+        turns(10, (2, 3, 4, 5))
         pair_out(5)
         split_tile(14)
+        pair_out(6)
         leave_pair(7, range(1, 2))
-        reads(8, (4, 5))
-        gates((4, 5))
+        reads(8, (6, 7))
         gates((6, 7))
         quantize_query(5)
-        turns(12, (6, 7, 0, 1))
-        pair_out(6)
+        turns(14, (0, 1))
         pair_out(7)
         gates((8, 9))
-        reads(10, (2, 3))
         quantize_query(6)
-        reads(12, (4, 5))
-        gates((10, 11))
-        quantize_query(7)
+        reads(10, (2, 3, 4, 5))
+        quantize_query(7, slice(0, 1))
+        gates(10)
+        quantize_query(7, slice(1, 2))
         reads(14, (6, 7))
-        gates(12, 13, 14, 15)
+        gates(11, 12, 13, 14, 15)

@@ -24,7 +24,7 @@ QUADRANT = 32
 T_PASSES = T // K_PASS
 HALVES = D // K_PASS
 R_TILES = R // P
-CHUNK = 8
+CHUNK = 2
 SIDE = E // 2
 WHOLE = slice(0, E)
 SIDES = (slice(0, SIDE), slice(SIDE, E))
@@ -74,7 +74,7 @@ def tile_memory_write_read_s4_kernel(
         write, q_words, q_turned, grouped, read_sums, result = {}, {}, {}, {}, {}, {}
 
         query_rows = query.rearrange("(n p j) d -> n p j d", p=P, j=CHUNK)
-        gate_rows = gate.rearrange("(n p j) e -> n p j e", p=P, j=CHUNK)
+        gate_rows = gate.rearrange("(n p j) e -> p n (j e)", p=P, j=CHUNK)
         out_rows = out.rearrange("(n p j) e -> n p j e", p=P, j=CHUNK)
 
         def load_values(span):
@@ -122,9 +122,9 @@ def tile_memory_write_read_s4_kernel(
             query_tile[i] = rows[:]
 
         def load_gate(i0, i1):
-            n, j = divmod(i0, CHUNK)
             rows = kept(f"gate_sb{i0}", [P, i1 - i0, E], BF16)
-            nc.sync.dma_start(out=rows[:], in_=gate_rows[n][:, j : j + i1 - i0, :])
+            pairs = rows[:].rearrange("p (n j) e -> p n (j e)", j=CHUNK)
+            nc.sync.dma_start(out=pairs, in_=gate_rows[:, i0 // CHUNK : i1 // CHUNK, :])
             for i in range(i0, i1):
                 gate_sb[i] = rows[:, i - i0, :]
 

@@ -24,14 +24,14 @@ QUADRANT = 32
 T_PASSES = T // K_PASS
 HALVES = D // K_PASS
 R_TILES = R // P
-CHUNK = 2
 SIDE = E // 2
 WHOLE = slice(0, E)
 SIDES = (slice(0, SIDE), slice(SIDE, E))
-KEY_RUNS = ((0, 3), (3, 8))
-VALUE_RUNS = ((0, 3), (3, 8))
 ALIGN = 256
 LINE = 16
+SCALE_RUNS = ((0, 3), (3, 8))
+SWEEP = 4
+SPLIT_SLOTS = ()
 WARM_PASSES = 5
 SPLIT_BUFS = 8
 GROUPED_BUFS = 4
@@ -55,8 +55,8 @@ def tile_memory_write_read_s4_kernel(
         def rotating(tag, shape, dtype, bufs):
             return sbuf.tile(shape, dtype, name=tag, tag=tag, bufs=bufs, align_bytes=ALIGN)
 
-        k_planes = {run: kept(f"k_planes{run[0]}", [P, run[1] - run[0], D], U8) for run in KEY_RUNS}
-        v_planes = {run: kept(f"v_planes{run[0]}", [P, run[1] - run[0], E], U8) for run in VALUE_RUNS}
+        k_planes = {run: kept(f"k_planes{run[0]}", [P, run[1] - run[0], D], U8) for run in SCALE_RUNS}
+        v_planes = {run: kept(f"v_planes{run[0]}", [P, run[1] - run[0], E], U8) for run in SCALE_RUNS}
         retain_rows = kept("retain_rows", [P, HALVES, P], BF16)
         retain_sorted = kept("retain_sorted", [P, HALVES, PACK, QUADRANT], BF16)
         retain_sb = kept("retain_sb", [P, HALVES, PACK, QUADRANT], BF16)
@@ -69,23 +69,27 @@ def tile_memory_write_read_s4_kernel(
         q_scales = [kept(f"q_scales{c}", [P, 2, HALVES, P], U8) for c in range(R_TILES // 2)]
         ident = kept("ident", [P, P], F32)
         k_words, v_words, k_sorted, k_scales = {}, {}, {}, {}
-        v_scales = {g: v_planes[run][:, g - run[0], :] for run in VALUE_RUNS for g in range(*run)}
-        query_sb, query_tile, gate_sb = {}, {}, {}
+        v_scales = {g: v_planes[run][:, g - run[0], :] for run in SCALE_RUNS for g in range(*run)}
+        query_load, gate_sb, side_sums = {}, {}, {}
+        split = {(1, t, side.start) for t in SPLIT_SLOTS for side in SIDES}
         write, q_words, q_turned, grouped, read_sums, result = {}, {}, {}, {}, {}, {}
 
-        query_rows = query.rearrange("(n p j) d -> n p j d", p=P, j=CHUNK)
-        gate_rows = gate.rearrange("(n p j) e -> p n (j e)", p=P, j=CHUNK)
-        out_rows = out.rearrange("(n p j) e -> n p j e", p=P, j=CHUNK)
+        def tile_rows(tensor, i0, i1):
+            pairs = tensor.rearrange("(c p j) n -> p c j n", p=P, j=2)
+            if i1 - i0 == 1:
+                return pairs[:, i0 // 2, i0 % 2 : i0 % 2 + 1, :]
+            return pairs[:, i0 // 2 : i1 // 2].rearrange("p c j n -> p c (j n)")
 
-        def load_values(span):
-            g0, g1 = span
+        def by_pairs(rows):
+            return rows if rows.shape[1] == 1 else rows.rearrange("p (c j) n -> p c (j n)", j=2)
+
+        def load_values(g0, g1):
             words = kept(f"v_words{g0}", [P, g1 - g0, 2 * E], U8)
             nc.sync.dma_start(out=words[:].bitcast(I32), in_=values_words[g0:g1].rearrange("g p n -> p g n").bitcast(I32))
             for g in range(g0, g1):
                 v_words[g] = words[:, g - g0, :]
 
-        def load_keys(span, halves=range(HALVES)):
-            g0, g1 = span
+        def load_keys(g0, g1, halves=range(HALVES)):
             words = kept(f"k_words{g0}{halves.start}", [P, g1 - g0, D * len(halves)], U8)
             rows = keys_words[g0:g1, :, D * halves.start : D * halves.stop].rearrange("g p n -> p g n")
             nc.sync.dma_start(out=words[:].bitcast(I32), in_=rows.bitcast(I32))
@@ -93,10 +97,10 @@ def tile_memory_write_read_s4_kernel(
                 for h in halves:
                     k_words[g, h] = (words, g0, halves.start)
 
-        def load_scale_rows(planes, scales, run, rows):
+        def load_scale_rows(planes, scales, run, rows, queue=nc.sync):
             by_row = scales[run[0] : run[1]].rearrange("g (q r) n -> r q g n", r=4)
             for r in rows:
-                nc.sync.dma_start(out=planes[run][r:P:QUADRANT, :, :].bitcast(I32), in_=by_row[r].bitcast(I32))
+                queue.dma_start(out=planes[run][r:P:QUADRANT, :, :].bitcast(I32), in_=by_row[r].bitcast(I32))
 
         def load_retain():
             rows = retain.rearrange("(h q c) -> q h c", h=HALVES, c=P)
@@ -106,33 +110,23 @@ def tile_memory_write_read_s4_kernel(
             rows = old[K_PASS * h : K_PASS * (h + 1), :].rearrange("(p t) e -> p t e", t=PACK)
             nc.sync.dma_start(out=old_sb[h][:, slots, :], in_=rows[:, slots, :])
 
-        def load_query(c0, c1):
-            n, j = divmod(2 * c0, CHUNK)
-            rows = kept(f"query_sb{c0}", [P, 2 * (c1 - c0), D], BF16)
-            nc.sync.dma_start(out=rows[:], in_=query_rows[n][:, j : j + 2 * (c1 - c0), :])
-            for c in range(c0, c1):
-                query_sb[c] = rows[:, 2 * (c - c0) : 2 * (c - c0) + 2, :]
-                for j in range(2):
-                    query_tile[2 * c + j] = query_sb[c][:, j, :]
-
-        def load_query_tile(i):
-            n, j = divmod(i, CHUNK)
-            rows = kept(f"query_sb{i // 2}" + "b" * (i % 2), [P, D], BF16)
-            nc.sync.dma_start(out=rows[:], in_=query_rows[n][:, j, :])
-            query_tile[i] = rows[:]
+        def load_query(i0, i1):
+            rows = kept(f"query_sb{i0}", [P, i1 - i0, D], BF16)
+            nc.sync.dma_start(out=by_pairs(rows[:]), in_=tile_rows(query, i0, i1))
+            for i in range(i0, i1):
+                query_load[i] = (rows, i0)
 
         def load_gate(i0, i1):
             rows = kept(f"gate_sb{i0}", [P, i1 - i0, E], BF16)
-            pairs = rows[:].rearrange("p (n j) e -> p n (j e)", j=CHUNK)
-            nc.sync.dma_start(out=pairs, in_=gate_rows[:, i0 // CHUNK : i1 // CHUNK, :])
+            nc.sync.dma_start(out=by_pairs(rows[:]), in_=tile_rows(gate, i0, i1))
             for i in range(i0, i1):
                 gate_sb[i] = rows[:, i - i0, :]
 
-        def sort_words(passes, halves):
+        def sort_words(passes, halves, copy=nc.vector.tensor_copy):
             by_slot = kept(f"k_sorted{passes.start}{halves.start}", [P, len(passes), len(halves), PACK, 2 * P], U8)
             words, g0, h0 = k_words[passes.start, halves.start]
             rows = words[:, passes.start - g0 : passes.stop - g0, D * (halves.start - h0) : D * (halves.stop - h0)]
-            nc.vector.tensor_copy(
+            copy(
                 out=by_slot[:].bitcast(U16).rearrange("k g h t (b i) -> k (g h) b t i", i=LINE // 2),
                 in_=rows.bitcast(U16).rearrange("k g (h b i t) -> k (g h) b t i", h=len(halves), i=LINE // 2, t=PACK),
             )
@@ -141,7 +135,7 @@ def tile_memory_write_read_s4_kernel(
                     k_sorted[g, h] = by_slot[:, g - passes.start, h - halves.start, :, :]
 
         def sort_scales(passes, halves):
-            run = [run for run in KEY_RUNS if run[0] <= passes.start < run[1]][0]
+            run = [run for run in SCALE_RUNS if run[0] <= passes.start < run[1]][0]
             rows = k_planes[run][:, passes.start - run[0] : passes.stop - run[0], K_PASS * halves.start : K_PASS * halves.stop]
             by_slot = kept(f"k_scales{passes.start}{halves.start}", [P, len(passes), len(halves), PACK, P], U8)
             nc.vector.tensor_copy(
@@ -163,7 +157,7 @@ def tile_memory_write_read_s4_kernel(
 
         def write_pass(h, t, cols, g, start, stop):
             nc.tensor.matmul_mx(
-                out=write[h, t, cols.start],
+                out=write[h, t][:, cols],
                 lhsT=k_sorted[g, h][:, t, :].bitcast(FP4X4),
                 lhsT_scale=k_scales[g, h][:, t, :],
                 rhs=v_words[g][:, 2 * cols.start : 2 * cols.stop].bitcast(FP4X4),
@@ -172,22 +166,39 @@ def tile_memory_write_read_s4_kernel(
                 stop=stop,
             )
 
-        def write_passes(h, t, cols, passes, b):
+        def write_passes(h, t, passes):
             for g in passes:
                 if g == 0:
-                    write[h, t, cols.start] = bank(b, [P, cols.stop - cols.start])[:]
-                write_pass(h, t, cols, g, g == 0, g == T_PASSES - 1)
+                    write[h, t] = bank(PACK * h + t, [P, E])[:]
+                write_pass(h, t, WHOLE, g, g == 0, g == T_PASSES - 1)
+
+        def side_passes(side, passes):
+            if passes.start == 0:
+                sums = bank(6 + side.start // SIDE, [P, 2, SIDE])
+                for t in (2, 3):
+                    side_sums[t, side.start] = sums[:, t - 2, :]
+            for t in (2, 3):
+                for g in passes:
+                    nc.tensor.matmul_mx(
+                        out=side_sums[t, side.start],
+                        lhsT=k_sorted[g, 1][:, t, :].bitcast(FP4X4),
+                        lhsT_scale=k_scales[g, 1][:, t, :],
+                        rhs=v_words[g][:, 2 * side.start : 2 * side.stop].bitcast(FP4X4),
+                        rhs_scale=v_scales[g][:, side],
+                        start=(g, t) == (0, 2),
+                        stop=(g, t) == (T_PASSES - 1, 3),
+                    )
 
         def warm_up():
             unread = bank(7, [P, E])
-            zeros = v_planes[VALUE_RUNS[-1]]
+            zeros = k_planes[SCALE_RUNS[-1]][:].rearrange("k g n -> k (g n)")
             for n in range(WARM_PASSES):
                 nc.tensor.matmul_mx(
                     out=unread[:],
-                    lhsT=zeros[:, 3, 0 : 2 * P].bitcast(FP4X4),
-                    lhsT_scale=zeros[:, 3, 2 * P : 3 * P],
-                    rhs=zeros[:, 0:2, :].rearrange("k g n -> k (g n)").bitcast(FP4X4),
-                    rhs_scale=zeros[:, 2, :],
+                    lhsT=zeros[:, 3 * E : 3 * E + 2 * P].bitcast(FP4X4),
+                    lhsT_scale=zeros[:, 3 * E + 2 * P : 3 * E + 3 * P],
+                    rhs=zeros[:, 0 : 2 * E].bitcast(FP4X4),
+                    rhs_scale=zeros[:, 2 * E : 3 * E],
                     start=True,
                     stop=True,
                 )
@@ -197,13 +208,30 @@ def tile_memory_write_read_s4_kernel(
                 out=memory_slots[h][:, t, cols],
                 in0=old_sb[h][:, t, cols],
                 scalar=retain_sb[:, h, t, 0:1],
-                in1=write[h, t, 0][:, cols],
+                in1=side_sums[t, cols.start] if (h, t, cols.start) in split else write[h, t][:, cols],
                 op0=MULT,
                 op1=ADD,
             )
 
-        def interleave_memory(h, cols, copy):
-            copy(
+        def add_old_paired(h, t, cols):
+            nc.vector.scalar_tensor_tensor(
+                out=memory_slots[h][:].rearrange("p t c -> p (t c)").rearrange("p (u c e) -> p u c e", u=2, e=2)[:, t // 2, cols, t % 2],
+                in0=old_sb[h][:, t, cols],
+                scalar=retain_sb[:, h, t, 0:1],
+                in1=write[h, t][:, cols],
+                op0=MULT,
+                op1=ADD,
+            )
+
+        def interleave_words(h, cols):
+            words = memory_slots[h][:].rearrange("p t c -> p (t c)").bitcast(F32).rearrange("p (u c) -> p u c", u=2)
+            nc.vector.tensor_copy(
+                out=memory[h][:, cols, :].bitcast(F32).rearrange("p (c i) u -> p c u i", i=2),
+                in_=words[:, :, cols].rearrange("p u (c i) -> p c u i", i=2),
+            )
+
+        def interleave_memory(h, cols):
+            nc.vector.tensor_copy(
                 out=memory[h][:, cols, :].rearrange("p (c i) t -> p c t i", i=4),
                 in_=memory_slots[h][:, :, cols].rearrange("p t (c i) -> p c t i", i=4),
             )
@@ -215,26 +243,22 @@ def tile_memory_write_read_s4_kernel(
                 in_=memory[h][:, cols, :].rearrange("r e t -> r (e t)"),
             )
 
-        def split_pair(c):
-            words = rotating("q_words", [P, 2, 2, HALVES, P], F32, SPLIT_BUFS)
-            nc.scalar.copy(
+        def deal(i0, i1, copy=nc.scalar.copy):
+            rows, first = query_load[i0]
+            words = rotating("q_words", [P, 2, i1 - i0, HALVES, P], F32, SPLIT_BUFS)
+            copy(
                 out=words[:].rearrange("r u j h (b x) -> r (j h b) u x", x=4),
-                in_=query_sb[c].rearrange("r j d -> r (j d)").bitcast(F32).rearrange("r (b x u) -> r b u x", x=4, u=2),
+                in_=rows[:, i0 - first : i1 - first, :]
+                .rearrange("r j d -> r (j d)")
+                .bitcast(F32)
+                .rearrange("r (b x u) -> r b u x", x=4, u=2),
             )
-            for j in range(2):
-                q_words[2 * c + j] = words[:, :, j, :, :]
+            for i in range(i0, i1):
+                q_words[i] = words[:, :, i - i0, :, :]
 
-        def split_tile(i):
-            words = rotating("q_words", [P, 2, HALVES, P], F32, SPLIT_BUFS)
-            nc.scalar.copy(
-                out=words[:].rearrange("r u h (b x) -> r (h b) u x", x=4),
-                in_=query_tile[i].bitcast(F32).rearrange("r (b x u) -> r b u x", x=4, u=2),
-            )
-            q_words[i] = words[:]
-
-        def leave_pair(c, tiles=range(2)):
-            for j in tiles:
-                q_words[2 * c + j] = query_tile[2 * c + j].bitcast(F32).rearrange("r (h p u) -> r u h p", h=HALVES, u=2)
+        def leave(i):
+            rows, first = query_load[i]
+            q_words[i] = rows[:, i - first, :].bitcast(F32).rearrange("r (h p u) -> r u h p", h=HALVES, u=2)
 
         def turns(first, banks):
             for i, b in enumerate(banks, first):
@@ -243,95 +267,97 @@ def tile_memory_write_read_s4_kernel(
                     for u in range(2):
                         nc.tensor.transpose(q_turned[i][:, h, u, :], q_words[i][:, u, h, :], ident[:])
 
-        def pair_out(c):
-            grouped[c] = kept(f"grouped{c % GROUPED_BUFS}", [P, 2, D], BF16)
-            for j in range(2):
+        def turned_out(*tiles):
+            for i in tiles:
+                c, j = divmod(i, 2)
+                if j == 0:
+                    grouped[c] = kept(f"grouped{c % GROUPED_BUFS}", [P, 2, D], BF16)
                 nc.scalar.copy(
                     out=grouped[c][:, j, :].bitcast(F32).rearrange("p (h r u) -> p h r u", h=HALVES, u=2),
-                    in_=q_turned[2 * c + j][:].rearrange("p h u r -> p h r u"),
+                    in_=q_turned[i][:].rearrange("p h u r -> p h r u"),
                 )
 
-        def quantize_query(c, tiles=slice(0, 2)):
+        def quantize_query(i0, i1):
+            c, tiles = i0 // 2, slice(i0 % 2, i0 % 2 + i1 - i0)
             nc.vector.quantize_mx(
                 out=q_codes[c][:, tiles].rearrange("p j h r -> p (j h r)").bitcast(FP8X4),
                 scales=q_scales[c][:, tiles].rearrange("p j h r -> p (j h r)"),
                 in_=grouped[c][:, tiles].rearrange("p j d -> p (j d)"),
             )
 
-        def read(i, cols, sums):
-            for h in range(HALVES):
-                nc.tensor.matmul_mx(
-                    out=sums,
-                    lhsT=q_codes[i // 2][:, i % 2, h, :].bitcast(FP8X4),
-                    lhsT_scale=q_scales[i // 2][:, i % 2, h, :],
-                    rhs=m_codes[h][:, cols].bitcast(FP8X4),
-                    rhs_scale=m_scales[h][:, cols],
-                    start=(h == 0),
-                    stop=(h == HALVES - 1),
-                )
-
         def reads(first, banks):
             for i, b in enumerate(banks, first):
                 read_sums[i] = bank(b, [P, E])
-                read(i, WHOLE, read_sums[i][:])
+                for h in range(HALVES):
+                    nc.tensor.matmul_mx(
+                        out=read_sums[i][:],
+                        lhsT=q_codes[i // 2][:, i % 2, h, :].bitcast(FP8X4),
+                        lhsT_scale=q_scales[i // 2][:, i % 2, h, :],
+                        rhs=m_codes[h][:].bitcast(FP8X4),
+                        rhs_scale=m_scales[h][:],
+                        start=(h == 0),
+                        stop=(h == HALVES - 1),
+                    )
 
-        def store(i0, i1, rows):
-            n, j = divmod(i0, CHUNK)
-            nc.sync.dma_start(out=out_rows[n][:, j : j + i1 - i0, :], in_=rows)
+        def results(i0, i1):
+            rows = kept(f"query_sb{i0}", [P, i1 - i0, E], F32)
+            for i in range(i0, i1):
+                result[i] = (rows, i0)
 
-        def gates(*tiles):
-            for unit in tiles:
-                unit = unit if isinstance(unit, tuple) else (unit,)
-                for i in unit:
-                    c, j = divmod(i, 2)
-                    if j == 0:
-                        result[c] = kept(f"query_sb{c}", [P, 2, E], F32)
-                    nc.vector.tensor_tensor(out=result[c][:, j, :], in0=read_sums[i][:], in1=gate_sb[i], op=MULT)
-                store(unit[0], unit[-1] + 1, result[unit[0] // 2][:, unit[0] % 2 : unit[-1] % 2 + 1, :])
+        def gates(i0, i1):
+            for i in range(i0, i1):
+                rows, first = result[i]
+                nc.vector.tensor_tensor(out=rows[:, i - first, :], in0=read_sums[i][:], in1=gate_sb[i], op=MULT)
 
-        both_halves = range(HALVES)
-        nc.vector.memset(v_planes[VALUE_RUNS[0]][:].bitcast(I32), 0)
-        nc.vector.memset(k_planes[KEY_RUNS[0]][:].bitcast(I32), 0)
-        nc.vector.memset(v_planes[VALUE_RUNS[1]][:].bitcast(I32), 0)
-        nc.vector.memset(k_planes[KEY_RUNS[1]][:].bitcast(I32), 0)
+        def store(i0, i1):
+            rows, first = result[i0]
+            nc.sync.dma_start(out=tile_rows(out, i0, i1), in_=by_pairs(rows[:, i0 - first : i1 - first, :]))
+
+        def gate_and_store(i0, i1):
+            gates(i0, i1)
+            store(i0, i1)
+
+        both_halves, first_half, second_half = range(HALVES), range(0, 1), range(1, 2)
+        first_run, last_run = SCALE_RUNS
+        nc.vector.memset(k_planes[first_run][:].bitcast(I32), 0)
+        nc.vector.memset(k_planes[last_run][:, 0:2, :].bitcast(I32), 0)
+        nc.vector.memset(k_planes[last_run][:, 2:5, :].bitcast(I32), 0)
         nc.vector.memset(retain_rows[:], 0.0)
-        load_values((0, 1))
-        load_scale_rows(v_planes, values_scales, VALUE_RUNS[0], range(0, 1))
-        load_keys((0, 1), range(0, 1))
-        load_scale_rows(k_planes, keys_scales, KEY_RUNS[0], range(0, 4))
-        load_scale_rows(v_planes, values_scales, VALUE_RUNS[0], range(1, 4))
-        load_keys((0, 1), range(1, 2))
-        load_keys((1, 2))
-        load_values((1, 2))
-        load_keys((2, 4))
-        load_values((2, 4))
-        sort_words(range(0, 1), range(0, 1))
+        load_scale_rows(v_planes, values_scales, first_run, range(0, 2))
+        load_keys(0, 1, first_half)
+        load_scale_rows(k_planes, keys_scales, first_run, range(0, 4))
+        load_values(0, 1)
+        load_scale_rows(v_planes, values_scales, first_run, range(2, 4))
+        load_keys(0, 1, second_half)
+        load_keys(1, 2)
+        load_values(1, 2)
+        load_keys(2, 4)
+        load_values(2, 4)
+        sort_words(range(0, 1), first_half)
         warm_up()
-        load_scale_rows(k_planes, keys_scales, KEY_RUNS[1], range(0, 4))
-        load_scale_rows(v_planes, values_scales, VALUE_RUNS[1], range(0, 4))
-        load_keys((4, 6))
-        load_values((4, 6))
+        load_scale_rows(k_planes, keys_scales, last_run, range(0, 4))
+        load_scale_rows(v_planes, values_scales, last_run, range(0, 4))
+        load_keys(4, 6)
+        load_values(4, 6)
         load_retain()
-        load_keys((6, 8))
-        load_values((6, 8))
+        load_keys(6, 8)
+        load_values(6, 8)
         load_old(0)
-        load_query(0, 1)
-        load_query(1, 2)
-        load_query(2, 3)
+        load_query(0, 2)
+        load_query(2, 4)
+        load_query(4, 6)
         load_old(1, slice(0, 2))
-        load_query(3, 4)
+        load_query(6, 8)
         load_old(1, slice(2, 4))
-        load_query_tile(8)
-        load_query_tile(9)
-        load_query(5, 6)
-        load_query(6, 7)
+        load_query(8, 9)
+        load_query(9, 10)
+        load_query(10, 12)
+        load_query(12, 14)
         load_gate(0, 4)
-        load_query(7, 8)
+        load_query(14, 16)
         load_gate(4, 8)
         load_gate(8, 16)
 
-        first_passes, last_passes = range(T_PASSES // 2), range(T_PASSES // 2, T_PASSES)
-        first_half, second_half = range(0, 1), range(1, 2)
         sort_scales(range(0, 1), first_half)
         sort_scales(range(0, 1), second_half)
         sort_scales(range(1, 2), both_halves)
@@ -341,14 +367,13 @@ def tile_memory_write_read_s4_kernel(
         sort_words(range(2, 3), both_halves)
         sort_words(range(3, 4), both_halves)
         sort_scales(range(3, 4), both_halves)
-        for g in first_passes:
+        for g in range(SWEEP):
             for h in both_halves:
                 for t in range(PACK):
-                    write_passes(h, t, WHOLE, (g,), PACK * h + t)
+                    write_passes(h, t, (g,))
         sort_retain()
-        for c in range(4):
-            split_pair(c)
-
+        for i in range(0, 8, 2):
+            deal(i, i + 2)
         sort_scales(range(4, 8), first_half)
         sort_words(range(4, 6), first_half)
         sort_scales(range(4, 8), second_half)
@@ -360,61 +385,74 @@ def tile_memory_write_read_s4_kernel(
         make_identity(nc, ident[:], nomemset=True)
         for g in (4, 5):
             for t in range(PACK):
-                write_passes(0, t, WHOLE, (g,), t)
+                write_passes(0, t, (g,))
         for t in range(PACK):
-            write_passes(0, t, WHOLE, (6, 7), t)
+            write_passes(0, t, (6, 7))
             add_old(0, t, WHOLE)
-        interleave_memory(0, SIDES[0], nc.vector.tensor_copy)
-        interleave_memory(0, SIDES[1], nc.vector.tensor_copy)
-
+        for side in SIDES:
+            interleave_memory(0, side)
         for t in range(PACK):
-            write_passes(1, t, WHOLE, last_passes, PACK + t)
+            write_passes(1, t, range(SWEEP, T_PASSES))
             if t < len(SIDES):
                 quantize_memory(0, SIDES[t])
             for cols in SIDES if t == PACK - 1 else (WHOLE,):
                 add_old(1, t, cols)
         for side in SIDES:
-            interleave_memory(1, side, nc.vector.tensor_copy)
+            interleave_memory(1, side)
 
-        split_tile(8)
-        leave_pair(4, range(1, 2))
+        deal(8, 9)
+        leave(9)
         turns(0, range(8))
-        pair_out(0)
+        turned_out(0, 1)
         turns(8, (0, 1))
-        quantize_query(0)
+        quantize_query(0, 2)
         for side in SIDES:
             quantize_memory(1, side)
-        pair_out(1)
-        quantize_query(1)
-        pair_out(2)
-        quantize_query(2, slice(0, 1))
-        quantize_query(2, slice(1, 2))
-        pair_out(3)
+        turned_out(2, 3)
+        quantize_query(2, 4)
+        turned_out(4, 5)
+        quantize_query(4, 5)
+        quantize_query(5, 6)
+        turned_out(6, 7)
         reads(0, range(2, 8))
-        gates((0, 1))
-        quantize_query(3)
-        pair_out(4)
-        split_pair(5)
-        split_pair(6)
+        results(0, 2)
+        gate_and_store(0, 2)
+        quantize_query(6, 8)
+        turned_out(8, 9)
+        deal(10, 12)
+        deal(12, 13)
+        deal(13, 14)
         reads(6, (0, 1))
-        gates((2, 3))
-        gates((4, 5))
-        quantize_query(4)
+        results(2, 4)
+        gate_and_store(2, 4)
+        results(4, 6)
+        gate_and_store(4, 6)
+        quantize_query(8, 10)
         turns(10, (2, 3, 4, 5))
-        pair_out(5)
-        split_tile(14)
-        pair_out(6)
-        leave_pair(7, range(1, 2))
+        turned_out(10, 11)
+        deal(14, 15)
+        turned_out(12, 13)
+        leave(15)
         reads(8, (6, 7))
-        gates((6, 7))
-        quantize_query(5)
+        results(6, 8)
+        gate_and_store(6, 8)
+        quantize_query(10, 12)
         turns(14, (0, 1))
-        pair_out(7)
-        gates((8, 9))
-        quantize_query(6)
+        turned_out(14, 15)
+        results(8, 10)
+        gate_and_store(8, 10)
+        quantize_query(12, 14)
         reads(10, (2, 3, 4, 5))
-        quantize_query(7, slice(0, 1))
-        gates(10)
-        quantize_query(7, slice(1, 2))
-        reads(14, (6, 7))
-        gates(11, 12, 13, 14, 15)
+        quantize_query(14, 15)
+        results(10, 12)
+        gate_and_store(10, 11)
+        gate_and_store(11, 12)
+        reads(14, (6,))
+        results(12, 14)
+        gate_and_store(12, 13)
+        quantize_query(15, 16)
+        reads(15, (7,))
+        gate_and_store(13, 14)
+        results(14, 16)
+        gate_and_store(14, 15)
+        gate_and_store(15, 16)

@@ -349,8 +349,7 @@ def tile_memory_write_read_s4_kernel(
         load_old(1, slice(0, 2))
         load_query(6, 8)
         load_old(1, slice(2, 4))
-        load_query(8, 9)
-        load_query(9, 10)
+        load_query(8, 10)
         load_query(10, 12)
         load_query(12, 14)
         load_gate(0, 4)
@@ -400,7 +399,7 @@ def tile_memory_write_read_s4_kernel(
         for side in SIDES:
             interleave_memory(1, side)
 
-        deal(8, 9)
+        leave(8)
         leave(9)
         turns(0, range(8))
         turned_out(0, 1)

@@ -70,7 +70,7 @@ def tile_memory_write_read_s4_kernel(
         ident = kept("ident", [P, P], F32)
         k_words, v_words, k_sorted, k_scales = {}, {}, {}, {}
         v_scales = {g: v_planes[run][:, g - run[0], :] for run in SCALE_RUNS for g in range(*run)}
-        query_load, gate_sb, side_sums = {}, {}, {}
+        query_load, gate_sb, side_sums, q_halves = {}, {}, {}, {}
         split = {(1, t, side.start) for t in SPLIT_SLOTS for side in SIDES}
         write, q_words, q_turned, grouped, read_sums, result = {}, {}, {}, {}, {}, {}
 
@@ -256,6 +256,15 @@ def tile_memory_write_read_s4_kernel(
             for i in range(i0, i1):
                 q_words[i] = words[:, :, i - i0, :, :]
 
+        def deal_half(i, h):
+            rows, first = query_load[i]
+            words = kept(f"q_half{i}{h}", [P, 2, P], F32)
+            nc.scalar.copy(
+                out=words[:].rearrange("r u (b x) -> r b u x", x=4),
+                in_=rows[:, i - first, K_PASS * h : K_PASS * (h + 1)].bitcast(F32).rearrange("r (b x u) -> r b u x", x=4, u=2),
+            )
+            q_halves[i, h] = words[:]
+
         def leave(i):
             rows, first = query_load[i]
             q_words[i] = rows[:, i - first, :].bitcast(F32).rearrange("r (h p u) -> r u h p", h=HALVES, u=2)
@@ -265,7 +274,8 @@ def tile_memory_write_read_s4_kernel(
                 q_turned[i] = bank(b, [P, HALVES, 2, P])
                 for h in range(HALVES):
                     for u in range(2):
-                        nc.tensor.transpose(q_turned[i][:, h, u, :], q_words[i][:, u, h, :], ident[:])
+                        words = q_halves[i, h][:, u, :] if (i, h) in q_halves else q_words[i][:, u, h, :]
+                        nc.tensor.transpose(q_turned[i][:, h, u, :], words, ident[:])
 
         def turned_out(*tiles):
             for i in tiles:
@@ -420,7 +430,8 @@ def tile_memory_write_read_s4_kernel(
         turned_out(8, 9)
         deal(10, 12)
         deal(12, 13)
-        deal(13, 14)
+        deal_half(14, 0)
+        leave(13)
         reads(6, (0, 1))
         results(2, 4)
         gate_and_store(2, 4)
@@ -429,7 +440,7 @@ def tile_memory_write_read_s4_kernel(
         quantize_query(8, 10)
         turns(10, (2, 3, 4, 5))
         turned_out(10, 11)
-        deal(14, 15)
+        deal_half(14, 1)
         turned_out(12, 13)
         leave(15)
         reads(8, (6, 7))

from contextlib import ExitStack

import concourse.mybir as mybir
from concourse.masks import make_identity

R, T, D, E = 2048, 4096, 1024, 512
FLOPS = 2 * T * D * E + 2 * R * D * E

F32 = mybir.dt.float32
BF16 = mybir.dt.bfloat16
I32 = mybir.dt.int32
U32 = mybir.dt.uint32
U16 = mybir.dt.uint16
U8 = mybir.dt.uint8
FP8X4 = mybir.dt.float8_e4m3fn_x4
FP4X4 = mybir.dt.float4_e2m1fn_x4
MULT = mybir.AluOpType.mult
ADD = mybir.AluOpType.add

P = 128
PACK = 4
K_PASS = P * PACK
QUADRANT = 32
T_PASSES = T // K_PASS
HALVES = D // K_PASS
R_TILES = R // P
SIDE = E // 2
WHOLE = slice(0, E)
SIDES = (slice(0, SIDE), slice(SIDE, E))
ALIGN = 256
LINE = 16
SCALE_RUNS = ((0, 3), (3, 8))
SWEEP = 4
SPLIT_SLOTS = ()
WARM_PASSES = 5
SPLIT_BUFS = 8
GROUPED_BUFS = 4


def tile_memory_write_read_s4_kernel(
    tc, keys_words, keys_scales, values_words, values_scales, old, retain, query, gate, out
):
    nc = tc.nc
    with ExitStack() as ctx:
        sbuf = ctx.enter_context(tc.tile_pool(name="sbuf", bufs=1))
        psum = ctx.enter_context(tc.psum_pool(name="psum", bufs=1))
        ctx.enter_context(tc.manual_schedule())

        def bank(b, shape):
            return psum.tile(shape, F32, name=f"bank{b}", tag=f"bank{b}")

        def kept(name, shape, dtype):
            return sbuf.tile(shape, dtype, name=name, tag=name, align_bytes=ALIGN)

        def rotating(tag, shape, dtype, bufs):
            return sbuf.tile(shape, dtype, name=tag, tag=tag, bufs=bufs, align_bytes=ALIGN)

        k_planes = {run: kept(f"k_planes{run[0]}", [P, run[1] - run[0], D], U8) for run in SCALE_RUNS}
        v_planes = {run: kept(f"v_planes{run[0]}", [P, run[1] - run[0], E], U8) for run in SCALE_RUNS}
        retain_rows = kept("retain_rows", [P, HALVES, P], BF16)
        retain_sorted = kept("retain_sorted", [P, HALVES, PACK, QUADRANT], BF16)
        retain_sb = kept("retain_sb", [P, HALVES, PACK, QUADRANT], BF16)
        old_sb = [kept(f"old_sb{h}", [P, PACK, E], BF16) for h in range(HALVES)]
        memory_slots = [kept(f"memory_slots{h}", [P, PACK, E], BF16) for h in range(HALVES)]
        memory = [kept(f"memory{h}", [P, E, PACK], BF16) for h in range(HALVES)]
        m_codes = [kept(f"m_codes{h}", [P, E], U32) for h in range(HALVES)]
        m_scales = [kept(f"m_scales{h}", [P, E], U8) for h in range(HALVES)]
        q_codes = [kept(f"q_codes{c}", [P, 2, HALVES, P], U32) for c in range(R_TILES // 2)]
        q_scales = [kept(f"q_scales{c}", [P, 2, HALVES, P], U8) for c in range(R_TILES // 2)]
        ident = kept("ident", [P, P], F32)
        k_words, v_words, k_sorted, k_scales = {}, {}, {}, {}
        v_scales = {g: v_planes[run][:, g - run[0], :] for run in SCALE_RUNS for g in range(*run)}
        query_load, gate_sb, side_sums, q_halves = {}, {}, {}, {}
        split = {(1, t, side.start) for t in SPLIT_SLOTS for side in SIDES}
        write, q_words, q_turned, grouped, read_sums, result = {}, {}, {}, {}, {}, {}

        def tile_rows(tensor, i0, i1):
            pairs = tensor.rearrange("(c p j) n -> p c j n", p=P, j=2)
            if i1 - i0 == 1:
                return pairs[:, i0 // 2, i0 % 2 : i0 % 2 + 1, :]
            return pairs[:, i0 // 2 : i1 // 2].rearrange("p c j n -> p c (j n)")

        def by_pairs(rows):
            return rows if rows.shape[1] == 1 else rows.rearrange("p (c j) n -> p c (j n)", j=2)

        def load_values(g0, g1):
            words = kept(f"v_words{g0}", [P, g1 - g0, 2 * E], U8)
            nc.sync.dma_start(out=words[:].bitcast(I32), in_=values_words[g0:g1].rearrange("g p n -> p g n").bitcast(I32))
            for g in range(g0, g1):
                v_words[g] = words[:, g - g0, :]

        def load_keys(g0, g1, halves=range(HALVES)):
            words = kept(f"k_words{g0}{halves.start}", [P, g1 - g0, D * len(halves)], U8)
            rows = keys_words[g0:g1, :, D * halves.start : D * halves.stop].rearrange("g p n -> p g n")
            nc.sync.dma_start(out=words[:].bitcast(I32), in_=rows.bitcast(I32))
            for g in range(g0, g1):
                for h in halves:
                    k_words[g, h] = (words, g0, halves.start)

        def load_scale_rows(planes, scales, run, rows, queue=nc.sync):
            by_row = scales[run[0] : run[1]].rearrange("g (q r) n -> r q g n", r=4)
            for r in rows:
                queue.dma_start(out=planes[run][r:P:QUADRANT, :, :].bitcast(I32), in_=by_row[r].bitcast(I32))

        def load_retain():
            rows = retain.rearrange("(h q c) -> q h c", h=HALVES, c=P)
            nc.sync.dma_start(out=retain_rows[0:P:QUADRANT, :, :], in_=rows)

        def load_old(h, slots=slice(0, PACK)):
            rows = old[K_PASS * h : K_PASS * (h + 1), :].rearrange("(p t) e -> p t e", t=PACK)
            nc.sync.dma_start(out=old_sb[h][:, slots, :], in_=rows[:, slots, :])

        def load_query(i0, i1):
            rows = kept(f"query_sb{i0}", [P, i1 - i0, D], BF16)
            nc.sync.dma_start(out=by_pairs(rows[:]), in_=tile_rows(query, i0, i1))
            for i in range(i0, i1):
                query_load[i] = (rows, i0)

        def load_gate(i0, i1):
            rows = kept(f"gate_sb{i0}", [P, i1 - i0, E], BF16)
            nc.sync.dma_start(out=by_pairs(rows[:]), in_=tile_rows(gate, i0, i1))
            for i in range(i0, i1):
                gate_sb[i] = rows[:, i - i0, :]

        def sort_words(passes, halves, copy=nc.vector.tensor_copy):
            by_slot = kept(f"k_sorted{passes.start}{halves.start}", [P, len(passes), len(halves), PACK, 2 * P], U8)
            words, g0, h0 = k_words[passes.start, halves.start]
            rows = words[:, passes.start - g0 : passes.stop - g0, D * (halves.start - h0) : D * (halves.stop - h0)]
            copy(
                out=by_slot[:].bitcast(U16).rearrange("k g h t (b i) -> k (g h) b t i", i=LINE // 2),
                in_=rows.bitcast(U16).rearrange("k g (h b i t) -> k (g h) b t i", h=len(halves), i=LINE // 2, t=PACK),
            )
            for g in passes:
                for h in halves:
                    k_sorted[g, h] = by_slot[:, g - passes.start, h - halves.start, :, :]

        def sort_scales(passes, halves):
            run = [run for run in SCALE_RUNS if run[0] <= passes.start < run[1]][0]
            rows = k_planes[run][:, passes.start - run[0] : passes.stop - run[0], K_PASS * halves.start : K_PASS * halves.stop]
            by_slot = kept(f"k_scales{passes.start}{halves.start}", [P, len(passes), len(halves), PACK, P], U8)
            nc.vector.tensor_copy(
                out=by_slot[:].rearrange("k g h t (b i) -> k (g h) b t i", i=LINE),
                in_=rows.rearrange("k g (h b i t) -> k (g h) b t i", h=len(halves), i=LINE, t=PACK),
            )
            for g in passes:
                for h in halves:
                    k_scales[g, h] = by_slot[:, g - passes.start, h - halves.start, :, :]

        def sort_retain():
            nc.scalar.copy(out=retain_sorted[:], in_=retain_rows[:].rearrange("q h (c t) -> q h t c", t=PACK))

        def turn_retain():
            nc.vector.transpose(
                out=retain_sb[:].rearrange("p h t c -> p (h t c)"),
                in_=retain_sorted[:].rearrange("q h t c -> q (h t c)"),
            )

        def write_pass(h, t, cols, g, start, stop):
            nc.tensor.matmul_mx(
                out=write[h, t][:, cols],
                lhsT=k_sorted[g, h][:, t, :].bitcast(FP4X4),
                lhsT_scale=k_scales[g, h][:, t, :],
                rhs=v_words[g][:, 2 * cols.start : 2 * cols.stop].bitcast(FP4X4),
                rhs_scale=v_scales[g][:, cols],
                start=start,
                stop=stop,
            )

        def write_passes(h, t, passes):
            for g in passes:
                if g == 0:
                    write[h, t] = bank(PACK * h + t, [P, E])[:]
                write_pass(h, t, WHOLE, g, g == 0, g == T_PASSES - 1)

        def side_passes(side, passes):
            if passes.start == 0:
                sums = bank(6 + side.start // SIDE, [P, 2, SIDE])
                for t in (2, 3):
                    side_sums[t, side.start] = sums[:, t - 2, :]
            for t in (2, 3):
                for g in passes:
                    nc.tensor.matmul_mx(
                        out=side_sums[t, side.start],
                        lhsT=k_sorted[g, 1][:, t, :].bitcast(FP4X4),
                        lhsT_scale=k_scales[g, 1][:, t, :],
                        rhs=v_words[g][:, 2 * side.start : 2 * side.stop].bitcast(FP4X4),
                        rhs_scale=v_scales[g][:, side],
                        start=(g, t) == (0, 2),
                        stop=(g, t) == (T_PASSES - 1, 3),
                    )

        def warm_up():
            unread = bank(7, [P, E])
            zeros = k_planes[SCALE_RUNS[-1]][:].rearrange("k g n -> k (g n)")
            for n in range(WARM_PASSES):
                nc.tensor.matmul_mx(
                    out=unread[:],
                    lhsT=zeros[:, 3 * E : 3 * E + 2 * P].bitcast(FP4X4),
                    lhsT_scale=zeros[:, 3 * E + 2 * P : 3 * E + 3 * P],
                    rhs=zeros[:, 0 : 2 * E].bitcast(FP4X4),
                    rhs_scale=zeros[:, 2 * E : 3 * E],
                    start=True,
                    stop=True,
                )

        def add_old(h, t, cols):
            nc.vector.scalar_tensor_tensor(
                out=memory_slots[h][:, t, cols],
                in0=old_sb[h][:, t, cols],
                scalar=retain_sb[:, h, t, 0:1],
                in1=side_sums[t, cols.start] if (h, t, cols.start) in split else write[h, t][:, cols],
                op0=MULT,
                op1=ADD,
            )

        def add_old_paired(h, t, cols):
            nc.vector.scalar_tensor_tensor(
                out=memory_slots[h][:].rearrange("p t c -> p (t c)").rearrange("p (u c e) -> p u c e", u=2, e=2)[:, t // 2, cols, t % 2],
                in0=old_sb[h][:, t, cols],
                scalar=retain_sb[:, h, t, 0:1],
                in1=write[h, t][:, cols],
                op0=MULT,
                op1=ADD,
            )

        def interleave_words(h, cols):
            words = memory_slots[h][:].rearrange("p t c -> p (t c)").bitcast(F32).rearrange("p (u c) -> p u c", u=2)
            nc.vector.tensor_copy(
                out=memory[h][:, cols, :].bitcast(F32).rearrange("p (c i) u -> p c u i", i=2),
                in_=words[:, :, cols].rearrange("p u (c i) -> p c u i", i=2),
            )

        def interleave_memory(h, cols):
            nc.vector.tensor_copy(
                out=memory[h][:, cols, :].rearrange("p (c i) t -> p c t i", i=4),
                in_=memory_slots[h][:, :, cols].rearrange("p t (c i) -> p c t i", i=4),
            )

        def quantize_memory(h, cols):
            nc.vector.quantize_mx(
                out=m_codes[h][:, cols].bitcast(FP8X4),
                scales=m_scales[h][:, cols],
                in_=memory[h][:, cols, :].rearrange("r e t -> r (e t)"),
            )

        def deal(i0, i1, copy=nc.scalar.copy):
            rows, first = query_load[i0]
            words = rotating("q_words", [P, 2, i1 - i0, HALVES, P], F32, SPLIT_BUFS)
            copy(
                out=words[:].rearrange("r u j h (b x) -> r (j h b) u x", x=4),
                in_=rows[:, i0 - first : i1 - first, :]
                .rearrange("r j d -> r (j d)")
                .bitcast(F32)
                .rearrange("r (b x u) -> r b u x", x=4, u=2),
            )
            for i in range(i0, i1):
                q_words[i] = words[:, :, i - i0, :, :]

        def deal_half(i, h):
            rows, first = query_load[i]
            words = kept(f"q_half{i}{h}", [P, 2, P], F32)
            nc.scalar.copy(
                out=words[:].rearrange("r u (b x) -> r b u x", x=4),
                in_=rows[:, i - first, K_PASS * h : K_PASS * (h + 1)].bitcast(F32).rearrange("r (b x u) -> r b u x", x=4, u=2),
            )
            q_halves[i, h] = words[:]

        def leave(i):
            rows, first = query_load[i]
            q_words[i] = rows[:, i - first, :].bitcast(F32).rearrange("r (h p u) -> r u h p", h=HALVES, u=2)

        def turns(first, banks):
            for i, b in enumerate(banks, first):
                q_turned[i] = bank(b, [P, HALVES, 2, P])
                for h in range(HALVES):
                    for u in range(2):
                        words = q_halves[i, h][:, u, :] if (i, h) in q_halves else q_words[i][:, u, h, :]
                        nc.tensor.transpose(q_turned[i][:, h, u, :], words, ident[:])

        def turned_out(*tiles):
            for i in tiles:
                c, j = divmod(i, 2)
                if j == 0:
                    grouped[c] = kept(f"grouped{c % GROUPED_BUFS}", [P, 2, D], BF16)
                nc.scalar.copy(
                    out=grouped[c][:, j, :].bitcast(F32).rearrange("p (h r u) -> p h r u", h=HALVES, u=2),
                    in_=q_turned[i][:].rearrange("p h u r -> p h r u"),
                )

        def quantize_query(i0, i1):
            c, tiles = i0 // 2, slice(i0 % 2, i0 % 2 + i1 - i0)
            nc.vector.quantize_mx(
                out=q_codes[c][:, tiles].rearrange("p j h r -> p (j h r)").bitcast(FP8X4),
                scales=q_scales[c][:, tiles].rearrange("p j h r -> p (j h r)"),
                in_=grouped[c][:, tiles].rearrange("p j d -> p (j d)"),
            )

        def reads(first, banks):
            for i, b in enumerate(banks, first):
                read_sums[i] = bank(b, [P, E])
                for h in range(HALVES):
                    nc.tensor.matmul_mx(
                        out=read_sums[i][:],
                        lhsT=q_codes[i // 2][:, i % 2, h, :].bitcast(FP8X4),
                        lhsT_scale=q_scales[i // 2][:, i % 2, h, :],
                        rhs=m_codes[h][:].bitcast(FP8X4),
                        rhs_scale=m_scales[h][:],
                        start=(h == 0),
                        stop=(h == HALVES - 1),
                    )

        def results(i0, i1):
            rows = kept(f"query_sb{i0}", [P, i1 - i0, E], F32)
            for i in range(i0, i1):
                result[i] = (rows, i0)

        def gates(i0, i1):
            for i in range(i0, i1):
                rows, first = result[i]
                nc.vector.tensor_tensor(out=rows[:, i - first, :], in0=read_sums[i][:], in1=gate_sb[i], op=MULT)

        def store(i0, i1):
            rows, first = result[i0]
            nc.sync.dma_start(out=tile_rows(out, i0, i1), in_=by_pairs(rows[:, i0 - first : i1 - first, :]))

        def gate_and_store(i0, i1):
            gates(i0, i1)
            store(i0, i1)

        both_halves, first_half, second_half = range(HALVES), range(0, 1), range(1, 2)
        first_run, last_run = SCALE_RUNS
        nc.vector.memset(k_planes[first_run][:].bitcast(I32), 0)
        nc.vector.memset(k_planes[last_run][:, 0:2, :].bitcast(I32), 0)
        nc.vector.memset(k_planes[last_run][:, 2:5, :].bitcast(I32), 0)
        nc.vector.memset(retain_rows[:], 0.0)
        load_scale_rows(v_planes, values_scales, first_run, range(0, 2))
        load_keys(0, 1, first_half)
        load_scale_rows(k_planes, keys_scales, first_run, range(0, 4))
        load_values(0, 1)
        load_scale_rows(v_planes, values_scales, first_run, range(2, 4))
        load_keys(0, 1, second_half)
        load_keys(1, 2)
        load_values(1, 2)
        load_keys(2, 4)
        load_values(2, 4)
        sort_words(range(0, 1), first_half)
        warm_up()
        load_scale_rows(k_planes, keys_scales, last_run, range(0, 4))
        load_scale_rows(v_planes, values_scales, last_run, range(0, 4))
        load_keys(4, 6)
        load_values(4, 6)
        load_retain()
        load_keys(6, 8)
        load_values(6, 8)
        load_old(0)
        load_query(0, 2)
        load_query(2, 4)
        load_query(4, 6)
        load_old(1, slice(0, 2))
        load_query(6, 8)
        load_old(1, slice(2, 4))
        load_query(8, 10)
        load_query(10, 12)
        load_query(12, 14)
        load_gate(0, 4)
        load_query(14, 16)
        load_gate(4, 8)
        load_gate(8, 16)

        sort_scales(range(0, 1), first_half)
        sort_scales(range(0, 1), second_half)
        sort_scales(range(1, 2), both_halves)
        sort_words(range(0, 1), second_half)
        sort_words(range(1, 2), both_halves)
        sort_scales(range(2, 3), both_halves)
        sort_words(range(2, 3), both_halves)
        sort_words(range(3, 4), both_halves)
        sort_scales(range(3, 4), both_halves)
        for g in range(SWEEP):
            for h in both_halves:
                for t in range(PACK):
                    write_passes(h, t, (g,))
        sort_retain()
        for i in range(0, 8, 2):
            deal(i, i + 2)
        sort_scales(range(4, 8), first_half)
        sort_words(range(4, 6), first_half)
        sort_scales(range(4, 8), second_half)
        sort_words(range(6, 8), first_half)
        turn_retain()
        sort_words(range(4, 6), second_half)
        sort_words(range(6, 8), second_half)
        nc.vector.memset(ident[:], 0.0)
        make_identity(nc, ident[:], nomemset=True)
        for g in (4, 5):
            for t in range(PACK):
                write_passes(0, t, (g,))
        for t in range(PACK):
            write_passes(0, t, (6, 7))
            add_old(0, t, WHOLE)
        for side in SIDES:
            interleave_memory(0, side)
        for t in range(PACK):
            write_passes(1, t, range(SWEEP, T_PASSES))
            if t < len(SIDES):
                quantize_memory(0, SIDES[t])
            for cols in SIDES if t == PACK - 1 else (WHOLE,):
                add_old(1, t, cols)
        for side in SIDES:
            interleave_memory(1, side)

        leave(8)
        leave(9)
        turns(0, range(8))
        turned_out(0, 1)
        turns(8, (0, 1))
        quantize_query(0, 2)
        for side in SIDES:
            quantize_memory(1, side)
        turned_out(2, 3)
        quantize_query(2, 4)
        turned_out(4, 5)
        quantize_query(4, 5)
        quantize_query(5, 6)
        turned_out(6, 7)
        reads(0, range(2, 8))
        results(0, 2)
        gate_and_store(0, 2)
        quantize_query(6, 8)
        turned_out(8, 9)
        deal(10, 12)
        deal(12, 13)
        deal_half(14, 0)
        leave(13)
        reads(6, (0, 1))
        results(2, 4)
        gate_and_store(2, 4)
        results(4, 6)
        gate_and_store(4, 6)
        quantize_query(8, 10)
        turns(10, (2, 3, 4, 5))
        turned_out(10, 11)
        deal_half(14, 1)
        turned_out(12, 13)
        leave(15)
        reads(8, (6, 7))
        results(6, 8)
        gate_and_store(6, 8)
        quantize_query(10, 12)
        turns(14, (0, 1))
        turned_out(14, 15)
        results(8, 10)
        gate_and_store(8, 10)
        quantize_query(12, 14)
        reads(10, (2, 3, 4, 5))
        quantize_query(14, 15)
        results(10, 12)
        gate_and_store(10, 11)
        gate_and_store(11, 12)
        reads(14, (6,))
        results(12, 14)
        gate_and_store(12, 13)
        quantize_query(15, 16)
        reads(15, (7,))
        gate_and_store(13, 14)
        results(14, 16)
        gate_and_store(14, 15)
        gate_and_store(15, 16)
